import numpy as np, ml_dtypes
CORES = [16,18,20,22]
N = 4
BF = ml_dtypes.bfloat16
P, U, S, RO, TH, PH = 4096, 256, 256, 4, 85, 102
def places(rng):
    c = rng.integers(0, 256, (N, 8, 3, 16)); c[:, :, 1] >>= 3
    k = rng.integers(0, 3, (N, 8, P)); a = rng.choice(np.array([4, 16, 48, 128, 255]), (N, 8, 1, P))
    m = np.take_along_axis(c, k[..., None], 2).transpose(0, 1, 3, 2)
    return np.clip(m + np.floor((2 * rng.random((N, 8, 16, P)) - 1) * a).astype(np.int64), 0, 255)
def near(rng, X, n):
    k = rng.integers(0, P, (N, 8, 1, n)); a = rng.choice(np.array([0, 8, 40, 160]), (N, 8, 1, n))
    return np.clip(np.take_along_axis(X, k, 3) + np.floor((2 * rng.random((N, 8, 16, n)) - 1) * a).astype(np.int64), 0, 255)
def parts(rng):
    X = places(rng); nb = rng.integers(0, P, (N, 8, 16, P)); v = rng.integers(0, P, (N, 8, U))
    A = np.where(rng.random((N, 8, 16, U)) < 0.6, v[:, :, None, :], rng.integers(0, P, (N, 8, 16, U)))
    return X, nb, v, A, near(rng, X, U), rng.integers(0, U, (N, 8, S)), near(rng, X, S), rng.integers(0, 4096, (N, 8, 16))
def pack(X, nb, v, A, y, j, z, w):
    fl = lambda a: np.ascontiguousarray(a.reshape(N, 128, -1)).astype(np.float32).astype(BF)
    wh = lambda a, p: np.ascontiguousarray(a.reshape(N, p, -1)).astype(np.int32)
    return {"x": fl(X), "nb": wh(nb, 128), "v0": wh(v, 8), "a0": wh(A, 128), "y0": fl(y), "j0": wh(j, 8), "z0": fl(z), "w": wh(w, 128)}
def setup_inputs(rng):
    return pack(*parts(rng))
def setup_inputs_spread(rng):
    def skew(hi, e, *shape): return (hi * rng.random(shape) ** e).astype(np.int64)
    def size(n): return np.minimum(np.exp2(8 * rng.random((N, 8, 1, n))) * rng.random((N, 8, 16, n)) * 1.5, 255).astype(np.int64)
    return pack(size(P), skew(P, 3, N, 8, 16, P), skew(P, 4, N, 8, U), skew(P, 2, N, 8, 16, U), size(U), skew(U, 3, N, 8, S), size(S), np.exp2(12 * rng.random((N, 8, 16))).astype(np.int64) - 1)
def setup_inputs_ends(rng):
    def edge(hi, *shape): return np.where(rng.random(shape) < 0.7, hi * rng.integers(0, 2, shape), rng.integers(0, hi + 1, shape))
    def bits(n):
        q = rng.integers(0, 4, (N, 8, 1, n)); m = rng.integers(0, 2, (N, 8, 16, n))
        return 255 * np.where(q == 0, 0, np.where(q == 1, 1, m))
    big = np.array([P - 1, P - 2, 1, 2, 3]); X = bits(P); X[:, :, :, 0] = 0; X[:, :, :, big] = 255
    nb = edge(P - 1, N, 8, 16, P); nb[:, 1::2, :, P - 1] = rng.choice(big, (N, 4, 16))
    v, A, y, j, z = edge(P - 1, N, 8, U), edge(P - 1, N, 8, 16, U), bits(U), edge(U - 1, N, 8, S), bits(S)
    for u in (0, 1, 6, U - 1):
        v[:, 1::2, u] = P - 1; y[:, 1::2, :, u] = 0; A[:, 1::2, 15, u] = 0; A[:, 1::2, 14, u] = P - 1
    w = 4095 * rng.integers(0, 2, (N, 8, 16)); w[:, 1] = 4095; w[:, 7] = 4095; w[:, 2] = 0
    for s in (0, S - 1): z[:, 7, :, s] = 255
    for s in (1, S - 2): z[:, 7, :, s] = 0; z[:, 7, 5, s] = 1; j[:, 7, s] = U - 1
    return pack(X, nb, v, A, y, j, z, w)
def level(s):
    return (s >> 4) + (np.arange(16) < (s & 15))
def setup_inputs_corners(rng):
    X, nb, v, A, y, j, z, w = parts(rng); kind = rng.permutation(8); a = np.arange(P); st = P // U; us = rng.permutation(U)
    ut = np.array([4075, 4087, 4089, 0, 0, 4095]); at = np.array([4093, 4089, 4087, 7, 100, 301]) & (P - 1)
    h = (((at * ut) >> 5) + at) & (P - 1); hw = (h + np.array([1, 1, 1, 128 * 7, 128 * 100, -128 * 301])) & (P - 1)
    zt = np.full((16, 6), 250); zt[0] = np.where(ut > 0, 251, 250); zt[14] = np.where(ut > 0, (ut - 3072) >> 4, 0); zt[15] = ut & 15
    for r in range(N):
        for g in range(8):
            f = kind[g]; Xg, n = X[r, g], nb[r, g]
            if f in (0, 4, 5):
                c = rng.integers(0, 256, (16, 1)); Xg[:] = c; y[r, g] = c; n[:] = (a ^ 1) if f == 5 else ((a + 1) & (P - 1))
                v[r, g] = st * rng.permutation(U) + st - 1; A[r, g] = v[r, g]; w[r, g] = rng.choice(np.array([0, 4095, 1, 2048]), 16) if f != 4 else 4095
            if f == 1: n[:] = a; A[r, g] = v[r, g]; w[r, g] = 0
            if f == 2:
                o = rng.permutation(P)
                for l in range(16):
                    for d in range(3): Xg[:, o[3 * l + d]] = level(TH * (l + 1) + d - 1); Xg[:, o[48 + 3 * l + d]] = level(PH * (l + 1) + d - 1)
                Xg[:, o[96]] = 0; Xg[:, o[97]] = level(8 * PH)
                v[r, g] = o[128:128 + U]; odd = np.arange(U) & 1; n[:, v[r, g]] = np.where(odd == 1, o[97], o[96])[None, :]
                y[r, g] = np.where(odd == 1, Xg[:, o[97]][:, None], 0)
                d = np.where(rng.random((16, U)) < 0.6 * odd, 2, rng.integers(0, 3, (16, U))); A[r, g] = o[3 * np.arange(16)[:, None] + d + 48 * odd]
                z[r, g] = 0
            if f == 3:
                q = rng.integers(0, 4, (16, P)); n[:] = np.where(q == 0, 0, np.where(q == 1, P - 1, np.where(q == 2, a, n)))
                q = rng.integers(0, 3, U); v[r, g] = np.where(q == 0, 0, np.where(q == 1, P - 1, v[r, g]))
                q = rng.integers(0, 3, (16, U)); A[r, g] = np.where(q == 0, 0, np.where(q == 1, P - 1, v[r, g])); j[r, g] = (U - 1) * rng.integers(0, 2, S)
            if f == 6: w[r, g] = 4095 * rng.integers(0, 2, 16)
            if f == 7:
                sp = np.concatenate([at, h, hw]); o = rng.permutation(np.setdiff1d(a, sp)); isp = np.zeros(P, bool); isp[sp] = True; isp[o[:8]] = True
                n[:] = np.where(isp[n], rng.choice(o[8:], (16, P)), n)
                v[r, g] = np.where(isp[v[r, g]], rng.choice(o[8:], U), v[r, g]); A[r, g] = np.where(isp[A[r, g]], rng.choice(o[8:], (16, U)), A[r, g])
                c = rng.integers(24, 57, (16, 1)); Xg[:, at] = c; Xg[:, h] = c; Xg[:, hw] = zt; Xg[:, o[:1]] = c; Xg[:, o[1:2]] = c + 60
                n[:, o[0]] = o[0]; v[r, g, us[:6]] = o[0]; y[r, g][:, us[:6]] = c; A[r, g][:15, us[:6]] = at; A[r, g][15, us[:6]] = o[1]
                Xg[:, o[4:8]] = np.stack([level(s) for s in (2052, 2051, 4080, 4079)], axis=1)
                n[:, o[2:4]] = o[[4, 6]]; n[15, o[2:4]] = o[[5, 7]]; v[r, g, us[6:8]] = o[2:4]; y[r, g][:, us[6:8]] = 0
                w[r, g] = 3072; w[r, g, 14] = 16; w[r, g, 15] = 1
                ss = rng.permutation(S)[:48].reshape(6, 8); z[r, g][:, ss] = zt[:, :, None]; j[r, g][ss] = us[:6][:, None]
    return pack(X, nb, v, A, y, j, z, w)
def setup_inputs_crowd(rng):
    X, nb, v, A, y, j, z, w = parts(rng); h = U // 2
    for q in range(N):
        home = (q - 1) % N; miss = int(rng.integers(0, 8))
        for g in range(8):
            Xg, n, m = X[q, g], nb[q, g], g & 3; pl = rng.permutation(P)
            if m == 2: i = int(np.argmin(pl)); pl[i] = pl[0]; pl[0] = 0
            o, e, b = pl[0], pl[1], pl[2]
            ev = pl[16:16 + h].copy() if m == 2 else np.full(h, e)
            if m & 1: ev[rng.integers(0, h)] = pl[3]
            od = np.full(h, o)
            if (g + q) & 1: od[rng.integers(0, h)] = pl[4]
            v[q, g, 0::2] = ev; v[q, g, 1::2] = od; n[:, ev] = ev[None, :]
            if m != 3: n[:, o] = b; n[:, pl[4]] = pl[5]
            Xg[:, b] = 10; Xg[:, o] = 250; Xg[:, pl[6]] = 240; Xg[:, e] = 200
            if m == 2: Xg[:, b] = 250; Xg[:, pl[8]] = 10; n[:, b] = pl[8]
            A[q, g, :, 0::2] = ev; A[q, g, :, 1::2] = (o, o, o, pl[6])[m]
            if m == 1: A[q, g, :, 1 + 2 * int(rng.integers(0, h))] = pl[6]
            t = 2 * rng.integers(0, h, S)
            if m == 0: t[:] = t[0]
            if m == 1: t[:] = t[0]; t[rng.integers(0, S)] = (t[0] + 2) % U
            if (q & 1) and g == miss:
                us = 2 * int(rng.integers(0, h)); Xg[:, pl[7]] = Xg[:, v[q, g, us]]; A[q, g, :, us] = pl[7]
                t = np.where(t == us, (us + 2) % U, t); t[rng.integers(0, S)] = us
            j[home, g] = t
    return pack(X, nb, v, A, y, j, z, w)
def setup_inputs_ties(rng):
    X, nb, v, A, y, j, z, w = parts(rng); c = 17 * rng.integers(0, 16, (N, 8, 16, 12)); c[:, 1::2, :, :6] = (c[:, 1::2, :, :6] >> 2) - ((c[:, 1::2, :, :6] >> 2) % 17)
    def some(n): return np.take_along_axis(c, rng.integers(0, 12, (N, 8, 1, n)), 3)
    X, y, z = some(P), some(U), some(S); nb[:, ::2, 8:] = nb[:, ::2, :8]; nb[:, 3, 1::2] = nb[:, 3, 0::2]
    v[:, 2] = rng.integers(0, 40, (N, U)); v[:, 5] = P - 1 - rng.integers(0, 40, (N, U)); A[:, 2, ::2] = v[:, 2, None, :]
    return pack(X, nb, v, A, y, j, z, w)
def check_inputs(d):
    bad = []
    for k, hi in (("x", 255), ("nb", P - 1), ("v0", P - 1), ("a0", P - 1), ("y0", 255), ("j0", U - 1), ("z0", 255), ("w", 4095)):
        a = np.asarray(d[k]).astype(np.float64)
        if not (np.min(a) >= 0 and np.max(a) <= hi): bad.append("range of " + k)
        elif not np.all(a == np.floor(a)): bad.append("whole numbers of " + k)
    return bad
def pick(X, k):
    return np.take_along_axis(X, k[:, :, None, :], 3)
def far(X, K, y):
    return np.stack([np.sum(np.abs(pick(X, K[:, :, l]) - y), axis=2) for l in range(16)], axis=2)
def reference(x, nb, v0, a0, y0, j0, z0, w):
    def vec(a): return a.astype(np.float32).astype(np.int64).reshape(N, 8, 16, -1)
    X, y, z = vec(x), vec(y0), vec(z0); nbr, A, W = (a.astype(np.int64).reshape(N, 8, 16, -1) for a in (nb, a0, w))
    v, j = v0.astype(np.int64), j0.astype(np.int64); lv = np.arange(1, 17)[None, None, :, None]
    tr = np.tile(np.arange(P), (N, 8, 1)); finds = np.zeros(N, np.int64)
    for t in range(1, RO + 1):
        n = pick(nbr, v); k = np.argmin(far(X, n, y), axis=2)
        v2 = np.take_along_axis(n, k[:, :, None, :], 2)[:, :, 0]; xn = pick(X, v2)
        new = far(X, A, xn) > TH * lv + 16 * (finds & 15)[:, None, None, None]
        top = 15 - np.argmax(new[:, :, ::-1], axis=2); some = np.any(new, axis=2)
        old = np.take_along_axis(A, top[:, :, None, :], 2)[:, :, 0]; xw = (xn + y) >> 1
        for r in range(N):
            for g in range(8):
                o = old[r, g][some[r, g]]; tr[r, g, o] = o
                q, i = np.unique(v[r, g], return_index=True); tr[r, g, q] = v2[r, g, i]
                q, i = np.unique(v2[r, g], return_index=True); X[r, g][:, q] = xw[r, g][:, i]
        A = np.where(new, v2[:, :, None, :], A); y = np.abs(y - xn); v = v2
        zz, jj = np.roll(z, t, axis=0), np.roll(j, t, axis=0)
        u = np.sum(W * zz, axis=2) & 4095; B = pick(A, jj)
        h = (((B * u[:, :, None, :]) >> 5) + B) & (P - 1)
        hit = far(X, h, zz) <= PH * lv
        l = np.where(np.any(hit, axis=2), np.argmax(hit, axis=2), 15)
        p = np.take_along_axis(B, l[:, :, None, :], 2)[:, :, 0]
        for c in range(3): p = np.take_along_axis(tr, p, 2)
        xp = pick(X, p); found = p == np.take_along_axis(v, jj, 2)
        zz = np.where(found[:, :, None, :], (zz + xp) >> 1, np.abs(zz - xp)); jj = np.where(found, u & (U - 1), jj)
        finds = np.sum(found, axis=(1, 2)); z, j = np.roll(zz, -t, axis=0), np.roll(jj, -t, axis=0)
    return {"yv": v.astype(np.float32), "ya": A.reshape(N, 128, U).astype(np.float32), "yy": y.reshape(N, 128, U).astype(np.float32).astype(BF),
            "yj": j.astype(np.float32), "yz": z.reshape(N, 128, S).astype(np.float32).astype(BF), "yt": tr.astype(np.float32)}

@@ -1,0 +1,657 @@
+from concourse.mybir import AluOpType, AxisListType, ActivationFunctionType
+
+A_ = AluOpType
+F_ = ActivationFunctionType
+WN = 4352
+MAGIC = 12582912.0
+RO = 4
+
+CFG = {
+    "stage": 512,
+    "gN": ["SV", "SS", "SS", "SS"], "gR": ["SS"] * 4, "gH": ["SVSV"] * 4,
+    "pN": "cccc", "pR": "cccc", "pH": "cccc",
+    "hN": 1, "hR": 1, "hH": 2,
+    "small": "S", "evac": "VS",
+}
+
+S = {}
+
+
+def _sb(names, shape, dty):
+    for n in names.split():
+        S[n] = ("sbuf", shape, dty)
+
+
+_sb("X TR", [128, WN], "bfloat16")
+_sb("NB", [128, 4096], "int32")
+_sb("GN MN GR MR GH MH EB", [128, 4096], "bfloat16")
+_sb("TD G16 G16l", [128, 2048], "bfloat16")
+_sb("A0 A1 NBf PM SEL SEH RS T2 Bf Pf COL COLG DUMR", [128, 256], "float32")
+_sb("Ai Si Hi VJi", [128, 256], "int32")
+_sb("NBu Au Ru Hu", [128, 256], "uint16")
+_sb("Y0 Y1 NE XN VS0 VS1 BS NW XW CS KC ONE NH PS XP VJ AD AB HS AM LO RWU RWS", [128, 256], "bfloat16")
+_sb("KR0 KR1 KH0 KH1 KDR KDH", [128, 256], "bfloat16")
+_sb("ZO0 ZO1 ZO2 ZO3 ZO4 ZI1 ZI2 ZI3 ZI4", [128, 272], "bfloat16")
+_sb("E1 E8 GB GBl", [128, 144], "bfloat16")
+_sb("I nI hI I4 nI4 BO nBO BR BH GR16 GS16", [128, 128], "bfloat16")
+_sb("If Jf I2f ONf", [128, 128], "float32")
+_sb("CL", [128, 512], "bfloat16")
+_sb("GS", [128, 64], "bfloat16")
+_sb("C", [128, 64], "float32")
+_sb("Ci", [128, 16], "int32")
+_sb("Wf", [128, 256], "float32")
+_sb("Wi", [128, 256], "int32")
+_sb("Wb", [128, 64], "bfloat16")
+_sb("Wu", [128, 256], "uint16")
+_sb("OUT", [128, 512], "float32")
+for _b in range(8):
+    S["P%d" % _b] = ("psum", [128, 512], "float32")
+SCRATCH = S
+NDMA = 18
+SEMAPHORES = ["V", "S", "P", "G"] + ["d%d" % k for k in range(NDMA)] + ["arr%d" % k for k in range(1, 5)] + ["sent%d" % k for k in range(4)]
+
+PL = {"CY": 1.0, "PCY": 0.5, "GA": 1.56, "SC": 3.8, "LAT": 120.0, "OVH": 40.0, "MM": 5.0, "SLACK": 60.0, "BW": 250.0, "SEED": 1, "NOISE": 300.0}
+
+
+def build(g, T, dest):
+    CY, PCY, GA, SC, OVH = PL["CY"], PL["PCY"], PL["GA"], PL["SC"], PL["OVH"]
+    ops = []
+    acc = {}
+    ndma = [0]
+    Q = {"V": g.vector, "S": g.scalar, "P": g.tensor, "G": g, "Y": g.sync}
+    al = slice(None)
+
+    def top(name, rows, a=None, b=None, s=None):
+        r = range(S[name][1][1])[a:b:s]
+        return (T[name][0:rows, a:b:s], name, r[0], r[-1] + 1, len(r), S[name][2] in ("bfloat16", "uint16"), s or 1)
+
+    def c(name, a=None, b=None, s=None):
+        return top(name, 128, a, b, s)
+
+    def sub(x, a, b, s=None, rows=128):
+        return top(x[1], rows, x[2] + a, x[2] + b, s)
+
+    def add(alts, rd, wr, **kw):
+        k = len(ops)
+        raw, oth = set(), set()
+
+        def meets(a, e):
+            return e[0] < a[3] and a[2] < e[1] and (a[6] != e[4] or (a[2] - e[0]) % a[6] == 0)
+        for a in rd:
+            raw.update(e[3] for e in acc.setdefault(a[1], []) if e[2] and meets(a, e))
+        for a in wr:
+            oth.update(e[3] for e in acc.setdefault(a[1], []) if meets(a, e))
+        for a in wr:
+            if a[3] - a[2] == a[4]:
+                acc[a[1]] = [e for e in acc[a[1]] if not (a[2] <= e[0] and e[1] <= a[3])]
+        for a in rd:
+            acc[a[1]].append((a[2], a[3], False, k, a[6]))
+        for a in wr:
+            acc[a[1]].append((a[2], a[3], True, k, a[6]))
+        banks = set(a[1] for a in list(rd) + list(wr) if S[a[1]][0] == "psum")
+        op = dict(alts=alts, raw=raw, oth=oth - raw, banks=banks, lat=0.0, sem=None, opens=None, closes=None, starts=None, out=wr[0][1] if wr else "")
+        op.update(kw)
+        ops.append(op)
+        return k
+
+    def isp(a):
+        return S[a[1]][0] == "psum"
+
+    def vc(n):
+        return max(64.0, n) * CY + OVH
+
+    def sv(x):
+        return x[0] if isinstance(x, tuple) else x
+
+    def cols(*xs):
+        return [x for x in xs if isinstance(x, tuple)]
+
+    def ts(out, in0, s1, op0, s2=None, op1=None):
+        r = 0.5 if out[5] and in0[5] else 1.0
+        if op1 is None:
+            f = lambda: g.vector.tensor_scalar(out[0], in0[0], sv(s1), None, op0)
+        else:
+            f = lambda: g.vector.tensor_scalar(out[0], in0[0], sv(s1), sv(s2), op0, op1)
+        return add({"V": ([f], vc(out[4] * r))}, [in0] + cols(s1, s2), [out])
+
+    def tt(out, a, b, op):
+        r = 1.0 if isp(a) or isp(b) else 2.0
+        return add({"V": ([lambda: g.vector.tensor_tensor(out[0], a[0], b[0], op)], vc(out[4] * r))}, [a, b], [out])
+
+    def cp(out, a, eng="V"):
+        alts = {}
+        if "V" in eng:
+            alts["V"] = ([lambda: g.vector.tensor_copy(out[0], a[0])], vc(out[4] * (0.5 if out[5] and a[5] else 1.0)))
+        if "S" in eng:
+            alts["S"] = ([lambda: g.scalar.activation(out[0], a[0], F_.Copy)], vc(out[4]))
+        return add(alts, [a], [out])
+
+    def ms(out, v):
+        return add({"V": ([lambda: g.vector.memset(out[0], v)], vc(out[4] * (0.5 if out[5] else 1.0)))}, [], [out])
+
+    def act(out, a, fn, bias=0.0, scale=1.0):
+        return add({"S": ([lambda: g.scalar.activation(out[0], a[0], fn, bias=sv(bias), scale=scale)], vc(out[4]))}, [a] + cols(bias), [out])
+
+    def scan(out, d0, d1, op0, op1):
+        return add({"V": ([lambda: g.vector.tensor_tensor_scan(out[0], d0[0], d1[0], 0.0, op0, op1)], vc(out[4]))}, [d0, d1], [out])
+
+    def gat(out, win, off, eng=None):
+        eng = eng or CFG["small"]
+        n = off[4] * 16
+        alts = {}
+        if "V" in eng:
+            alts["V"] = ([lambda: g.vector.tensor_copy(out[0], win[0].indirect(off[0]))], 60 + n * GA * CY)
+        if "S" in eng:
+            alts["S"] = ([lambda: g.scalar.activation(out[0], win[0].indirect(off[0]), F_.Copy)], 78 + n * GA * CY)
+        return add(alts, [win, off], [out])
+
+    def sca(win, off, src):
+        return add({"V": ([lambda: g.vector.tensor_copy(win[0].indirect(off[0]), src[0])], 60 + src[4] * SC * CY)}, [off, src], [win])
+
+    def mm(terms, first=True, last=True, each=False):
+        fs, cost, rd, wr = [], 0.0, [], []
+        for k, (o, l, r) in enumerate(terms):
+            st = each or (first and k == 0)
+            sp = each or (last and k == len(terms) - 1)
+            fs.append(lambda o=o, l=l, r=r, st=st, sp=sp: g.tensor.matmul(o[0], l[0], r[0], st, sp))
+            cost += max(min(64, l[4]), r[4]) * PCY * (1 if r[5] else 4) + PL["MM"]
+            rd += [l, r]
+            wr.append(o)
+        bank = terms[0][0][1]
+        return add({"P": (fs, cost + OVH)}, rd, wr, starts=bank if first else None,
+                   opens=bank if first and not last else None, closes=bank if last and not first else None)
+
+    def gp(f, n, rd, wr):
+        return add({"G": ([f], 170 + 2 * n * CY)}, rd, wr)
+
+    def dma(q, out, in_, rd, wr, nbytes, **kw):
+        s = "d%d" % ndma[0]
+        ndma[0] += 1
+        return add({q: ([lambda: Q[q].dma_start(out, in_, **kw)], 60.0 if q != "G" else 1000.0)}, rd, wr, sem=s, lat=1800 + nbytes / PL["BW"])
+
+    def wf(k):
+        return c("Wf", 16 * k, 16 * k + 16)
+
+    def wi(k, n=1):
+        return c("Wi", 16 * k, 16 * (k + n))
+
+    def wu(k):
+        return c("Wu", 16 * k, 16 * k + 16)
+
+    def col(k):
+        return c("C", k, k + 1)
+
+    def ci(k):
+        return c("Ci", k, k + 1)
+
+    def E(name, l, rows=128):
+        return top(name, rows, 15 - l, 143 - l)
+
+    def gs(k):
+        return c("GS", 8 * k, 8 * k + 8)
+
+    def const(out, k):
+        return (out, top("CL", 1, 128 * k, 128 * k + 128), top("ONE", 1, 0, 256))
+
+    def crow(out, name):
+        return (out, top("ONE", 1, 0, 128), top(name, 1, 0, 256))
+
+    def toW(out, e, src, rows=128):
+        return [(out, E(e, i, rows), top(src, rows, i, 256, 16)) for i in range(16)]
+
+    for s in (0, 1):
+        dma("S", T.VJi[s:16:2, :], T.v0[:], [], [c("VJi", s, s + 1)], 8192)
+    dma("S", T.VJi[32:40, :], T.j0[:], [], [c("VJi", 2, 3)], 8192)
+    dma("Y", T.Ai[:], T.a0[:], [], [c("Ai")], 131072)
+    dma("Y", T.X[:, 0:4096], T.x[:], [], [c("X", 0, 4096)], 1 << 20)
+    dma("Y", T.NB[:], T.nb[:], [], [c("NB")], 3 << 20)
+    dma("S", T.ZO0[:, 0:256], T.z0[:], [], [c("ZO0", 0, 256)], 65536)
+    dma("S", T.Y0[:], T.y0[:], [], [c("Y0")], 65536)
+    dma("S", T.Ci[:, 8:9], T.w[:], [], [c("Ci", 8, 12)], 512)
+    gp(lambda: g.iota(T.Ci[:, 0:1], [[0, 1]], 0, 1), 1, [], [ci(0)])
+    gp(lambda: g.iota(T.COL[:], [[1, 256]], 0, 0, allow_small_or_imprecise_dtypes=True), 256, [], [c("COL")])
+    gp(lambda: g.iota(T.KC[:], [[0, 16], [1, 16]], 0, 0, allow_small_or_imprecise_dtypes=True), 256, [], [c("KC")])
+    gp(lambda: g.iota(T.COLG[:], [[1, 16], [0, 16]], 0, 0, allow_small_or_imprecise_dtypes=True), 256, [], [c("COLG")])
+    P_, L_, G_, T15, RV, KB, THR, M0, M1, WH, WL, FS, T8, T16, OD, G2, EV, TS16, N4 = range(19)
+    LT, HI = 24, 40
+    cp(col(P_), ci(0))
+    ts(ci(1), ci(0), 15, A_.bitwise_and)
+    ts(ci(2), ci(0), 4, A_.arith_shift_right)
+    ts(ci(3), ci(0), 1, A_.bitwise_and)
+    ts(ci(7), ci(0), 1, A_.arith_shift_right)
+    cp(col(L_), ci(1))
+    cp(col(G_), ci(2))
+    cp(col(OD), ci(3))
+    cp(col(G2), ci(7))
+    ts(col(EV), ci(3), -1.0, A_.mult, 1.0, A_.add)
+    ts(col(T15), ci(2), 16.0, A_.mult, 15.0, A_.add)
+    ts(col(T16), ci(7), 16.0, A_.mult, 15.0, A_.add)
+    ts(col(TS16), ci(7), 16.0, A_.mult, col(OD), A_.add)
+    ts(col(T8), ci(0), 16.0, A_.mult, 15.0 - 512.0, A_.add)
+    ts(col(RV), ci(1), -1.0, A_.mult, col(T15), A_.add)
+    ms(col(N4), -4096.0)
+    ms(c("ONE"), 1.0)
+    ms(c("ONf"), 1.0)
+    for k, v in enumerate((-0.25, -4096.0, -2016.0, -4194304.0)):
+        ms(top("CL", 1, 128 * k, 128 * k + 128), v)
+    ts(c("GB"), c("COL", 0, 144), col(T16), A_.is_equal)
+    ts(c("GBl"), c("COL", 0, 144), col(T16), A_.is_equal, col(OD), A_.mult)
+    ts(c("GR16"), c("COLG", 0, 128), col(G2), A_.is_equal)
+    ts(c("GS16"), c("COL", 0, 128), col(TS16), A_.is_equal)
+    for n, v in (("E1", 1.0), ("E8", 8192.0)):
+        ts(c(n), c("COL", 0, 144), col(T15), A_.is_equal, v, A_.mult)
+    for n, v in (("I", 1.0), ("nI", -1.0), ("hI", 0.5), ("I4", 4096.0), ("nI4", -4096.0), ("If", 1.0), ("I2f", 2048.0)):
+        ts(c(n), c("COL", 0, 128), col(P_), A_.is_equal, v, A_.mult)
+    ts(c("Jf"), c("COL", 0, 128), col(RV), A_.is_equal)
+    ts(c("BO"), c("COLG", 0, 128), col(G_), A_.is_equal)
+    ts(c("nBO"), c("COLG", 0, 128), col(G_), A_.is_equal, -1.0, A_.mult)
+    for k, v in enumerate((1.0, 2.0, -1.0, 16.0, 32.0, -16.0)):
+        ts(gs(k), c("COL", 0, 8), col(G_), A_.is_equal, v, A_.mult)
+    ts(col(KB), ci(1), -4096.0, A_.mult, 61440.0, A_.add)
+    ts(col(M0), ci(1), 0.0, A_.is_equal, 256.0, A_.mult)
+    ts(col(M1), ci(1), 1.0, A_.is_equal)
+    ts(c("LO"), c("COL"), col(M1), A_.mult)
+    ts(c("C", HI, HI + 17), c("COL", 0, 17), col(M0), A_.mult)
+    for k in range(17):
+        o = c("TR", 256 * k, 256 * k + 256)
+        add({"V": ([lambda o=o, k=k: g.vector.tensor_scalar(o[0], T.LO[:], T.C[:, HI + k:HI + k + 1], None, A_.add)], vc(128)),
+             "S": ([lambda o=o, k=k: g.scalar.activation(o[0], T.LO[:], F_.Identity, bias=T.C[:, HI + k:HI + k + 1])], vc(256))},
+            [c("LO"), col(HI + k)], [o])
+    ms(c("X", 4096, WN), 0.0)
+    ms(c("CS", 0, 16), 0.0)
+    ts(c("RS"), c("KC"), 0.0, A_.is_equal, 1000000.0, A_.mult)
+    r1 = lambda n: top(n, 1, 0, 256)
+    ts(r1("KR0"), r1("KC"), -80.0, A_.mult, -80.0, A_.add)
+    ts(r1("KR1"), r1("KC"), -5.0, A_.mult, -5.5, A_.add)
+    ts(r1("KH0"), r1("KC"), 96.0, A_.mult, -1536.0, A_.add)
+    ts(r1("KH1"), r1("KC"), 6.0, A_.mult, -96.5, A_.add)
+    ms(top("KH0", 1, 0, 256, 16), -65536.0)
+    ts(r1("KDH"), r1("KC"), -4096.0, A_.mult, 61440.0, A_.add)
+    ts(r1("PM"), r1("COLG"), 16.0, A_.mult, 15.0, A_.add)
+    tt(r1("SEL"), r1("PM"), r1("KC"), A_.subtract)
+    ts(r1("KDR"), r1("SEL"), 8192.0, A_.mult)
+    for n, key, pos in (("BR", "pR", lambda l: l), ("BH", "pH", lambda l: 15 - l)):
+        cp(c(n), c("nBO"))
+        for l in range(16):
+            if CFG[key][l // 4] == "d":
+                ms(c(n, pos(l), 128, 16), 0.0)
+    ts(c("C", LT, LT + 16), c("COL", 0, 16), col(L_), A_.is_gt)
+    for i in range(1, 16):
+        ts(c("TD", 128 * i, 128 * i + 128), E("E8", i), col(LT + i), A_.mult)
+    DUM, VF, BF, T1, T3, VJW, FW, J1, J2, KS, T4 = range(11)
+    ts(wf(T1), c("COL", 0, 16), 16.0, A_.mult, col(L_), A_.add)
+    ts(wf(DUM), wf(T1), 4096.0, A_.add)
+    ts(wf(KS), c("COL", 0, 16), 131072.0, A_.mult, 4096.0 + 15 * 8192.0, A_.add)
+    ts(ci(4), ci(8), 63, A_.bitwise_and)
+    cp(col(WL), ci(4))
+    tt(col(WH), ci(8), col(WL), A_.subtract)
+    ts(gs(6), gs(0), col(WH), A_.mult)
+    ts(gs(7), gs(0), col(WL), A_.mult)
+
+    pK, pD = c("P0", 0, 256), c("P0", 256, 512)
+    pH, pS = c("P1", 0, 256), c("P1", 256, 512)
+    pB, pU = c("P2", 0, 256), c("P2", 256, 512)
+    pY, pX = c("P3", 0, 256), c("P3", 256, 512)
+    pZ, pT = c("P4", 0, 256), c("P4", 256, 512)
+    pQ, pE = c("P6", 0, 256) if CFG["stage"] == 512 else c("P5", 256, 512), c("P6", 256, 512)
+    pR = pK if "d" in CFG["pN"] + CFG["pR"] + CFG["pH"] else c("P5", 0, 256)
+    pA = c(pR[1], 256, 512)
+    X = c("X", 0, 4096)
+
+    def pw(k):
+        return c("P7", 256 + 16 * k, 272 + 16 * k)
+    V0, V1, OV0, OV1, OB, JU, PU0 = range(7)
+
+    def send(t):
+        src, dst, s = "ZO%d" % t, "ZI%d" % (t + 1), "arr%d" % (t + 1)
+        add({"G": ([lambda: g.remote_dma(T[dst][:], T[src][:], T.sem[s], T.sem["sent%d" % t], dest[1], dest[0], dest[2])], 500.0)},
+            [c(src)], [c(dst)], sem=s, lat=2500.0, remote=True)
+
+    def rows(src, mask, k, p, row):
+        cp(wi(k), src)
+        ts(c("Wi", 16 * k + 16, 16 * k + 48, 2), wi(k), mask, A_.bitwise_and)
+        ts(c("Wi", 16 * k + 17, 16 * k + 48, 2), wi(k), 255, A_.bitwise_and)
+        o = 32 * (k // 4)
+        cp(c("Wb", o, o + 32), wi(k + 1, 2))
+        mm([(sub(p, 128 * h, 128 * h + 128, rows=16), c("Wb", o + 16 * h, o + 16 * h + 16), c("I")) for h in (0, 1)], each=True)
+        cp(top(row, 16), sub(p, 0, 256, rows=16), CFG["evac"])
+
+    def dedup(keyf, off):
+        cp(c("Ru"), pU)
+        for k in range(16):
+            ts(c("EB", 256 * k, 256 * k + 256 - 16 * k), c("Ru", 16 * k, 256), c("Wf", 16 * keyf + k, 16 * keyf + k + 1), A_.is_equal)
+        for k0 in (0, 5, 10):
+            mm([(c("P7", 16 * k + 16, 256), c("BO"), c("EB", 256 * k + 16, 256 * k + 256 - 16 * k)) for k in range(k0, k0 + 5)], first=k0 == 0, last=k0 == 10)
+        cp(c("CS", 16, 256), c("P7", 16, 256), CFG["evac"])
+        mm([(pw(0), c("TD", 128 * i, 128 * i + 128), c("EB", i, 4096, 256)) for i in range(1, 16)] + toW(pw(0), "E8", "CS"))
+        tt(wf(T1), pw(0), wf(DUM), A_.min)
+        tt(wf(T3), wf(T1), wf(keyf), A_.max)
+        cp(off, wf(T3))
+
+    def gather(job, lst, t):
+        en = CFG["g" + job][t - 1]
+        w = 256 // len(en)
+        for h, e in enumerate(en):
+            gat(c("G" + job, 16 * w * h, 16 * w * (h + 1)), X, c(lst, w * h, w * (h + 1)), "VS" if e == "A" else e)
+
+    stage = [0]
+
+    def dist(job, oth, pc, pd, head, f0, pos, skip=None):
+        Gn, Mn, path, nh = "G" + job, "M" + job, CFG["p" + job], CFG["h" + job]
+        wd = 256 // nh
+        k0, ends = len(ops), []
+        if "c" in path:
+            mm([(pc, c("I"), c(oth, 0, 256))])
+        k = mm(head[:1], last=False)
+        for nm in (Gn, pd[1]):
+            ops[k]["oth"].update([e[3] for e in acc[nm] if e[2] and e[3] != k and (nm == Gn and e[0] == 0 or nm != Gn and job != "R")])
+        tail = head[1:]
+        for p in range(nh):
+            u0 = wd * p
+            per = CFG["stage"] // wd
+            for l0 in range(0, 16, per):
+                ls = [l for l in range(l0, l0 + per) if l != skip]
+                gl = lambda l, a=0, n=wd: c(Gn, 16 * (u0 + a) + l, 16 * (u0 + a + n), 16)
+                ml = lambda l, a=0, n=wd: c(Mn, 16 * u0 + wd * l + a, 16 * u0 + wd * l + a + n)
+                o = lambda l, a: sub(pd, u0 + a + pos(l), u0 + a + 128, 16)
+                parts = [(l, a) for l in ls for a in range(0, wd, 128)]
+                if path[l0 // 4] == "c":
+                    for l in ls:
+                        tt(ml(l), gl(l), sub(pc, u0, u0 + wd), A_.max)
+                    mm([(o(l, a), gl(l, a, 128), gs(f0 + 2)) for l, a in parts], first=False, last=False)
+                    terms = [(o(l, a), ml(l, a, 128), gs(f0 + 1)) for l, a in parts]
+                else:
+                    if not ls:
+                        mm([(o(l0 - 1, 0), c("CS", 0, 128), gs(8))], first=False, last=True)
+                        continue
+                    stage[0] += 1
+                    sb = "P5" if CFG["stage"] == 512 or stage[0] % 2 else "P6"
+                    for j, l in enumerate(ls):
+                        so = c(sb, wd * j, wd * j + wd)
+                        mm([(so, c("I"), gl(l)), (so, c("nI"), c(oth, u0, u0 + wd))])
+                    act(c(Mn, 16 * u0 + wd * l0, 16 * u0 + wd * (l0 + len(ls))), c(sb, 0, wd * len(ls)), F_.Abs)
+                    terms = [(o(l, a), ml(l, a, 128), gs(f0)) for l, a in parts]
+                acc[pd[1]] = [e for e in acc[pd[1]] if e[1] - e[0] == 256 or e[0] >= pd[3] or e[1] <= pd[2]]
+                ends.append(mm(tail + terms, first=False, last=(p == nh - 1 and l0 + per == 16)))
+                tail = []
+        ops[ends[-1]]["oth"].update(k for k in range(k0, ends[-1]) if ops[k]["out"] == pd[1] and "P" in ops[k]["alts"])
+        acc[pd[1]].append((pd[2], pd[3], True, ends[-1], 1))
+
+    def turn(p, src, ident):
+        return [(sub(p, 128 * h, 128 * h + 128), c(src, 128 * h, 128 * h + 128), c(ident)) for h in (0, 1)]
+
+    def lists(vu, vs):
+        mm(toW(pw(1), "GB", "RWU", 16))
+        if vu is not None:
+            cp(vu, pw(1))
+        mm([(pU, top("GR16", 16), top("RWU", 16))])
+        mm([(pB, top("GS16", 16), top("RWU", 16))])
+        cp(c(vs), pB, CFG["evac"])
+
+    ts(top("Si", 16), top("VJi", 16), 255, A_.bitwise_and)
+    ts(top("Hi", 16), top("VJi", 16), 3840, A_.bitwise_and)
+    ts(top("PM", 16), top("Si", 16), top("C", 16, OD, OD + 1), A_.mult)
+    ts(top("SEL", 16), top("Hi", 16), top("C", 16, EV, EV + 1), A_.mult)
+    tt(top("RWU", 16), top("PM", 16), top("SEL", 16), A_.add)
+    lists(wu(V0), "VS0")
+    cp(wf(VF), pw(1))
+    jr = (T.RWS[32:40, :],) + c("RWS")[1:]
+    add({"V": ([lambda: g.vector.tensor_copy(jr[0], T.VJi[32:40, :])], vc(256))}, [c("VJi")], [jr])
+    ts(c("G16", 0, 144), c("COL", 0, 144), col(T8), A_.is_equal)
+    mm([(pw(2), (T.G16[32:40, 15 - i:143 - i],) + c("G16", 0, 128)[1:], (T.RWS[32:40, i:256:16],) + c("RWS", i, 256, 16)[1:]) for i in range(16)])
+    cp(c("ZO0", 256, 272), pw(2))
+    send(0)
+    cp(c("Au"), c("Ai"))
+    cp(c("A0"), c("Ai"))
+    dedup(VF, wu(OV0))
+
+    def users(t):
+        a, b = (t - 1) % 2, t % 2
+        y, yn, Ao, An, vs = "Y%d" % a, "Y%d" % b, "A%d" % a, "A%d" % b, "VS%d" % b
+        gat(c("NBu"), c("NB"), wu(V0 + a), "V")
+        gather("N", "NBu", t)
+        gather("R", "Au", t)
+        ts(c("NBf"), c("NBu"), col(KB), A_.add)
+        mm(turn(pD, "NBf", "If"), each=True)
+        head = [crow(pK, "KC")]
+        if "c" in CFG["pN"] and "d" in CFG["pN"]:
+            head += [(sub(pK, 128 * h, 128 * h + 128), c(y, 128 * h, 128 * h + 128), c("G16l", 0, 128)) for h in (0, 1)]
+        dist("N", y, pY, pK, head, 3, lambda l: l)
+        scan(c("PM"), c("RS"), pK, A_.add, A_.min)
+        tt(c("NE"), pK, c("PM"), A_.not_equal)
+        scan(c("SEL"), c("NE"), pD, A_.mult, A_.max)
+        rows(c("SEL", 15, 256, 16), 3840, 0, pB, "RWU")
+        lists(wu(V0 + b), vs)
+        cp(wf(VF), pw(1))
+        gat(c("XN"), X, wu(V0 + b))
+        dedup(VF, wu(OV0 + b))
+        mm([(pX, c("hI"), c("XN")), (pX, c("hI"), c(y)), const(pX, 0)])
+        ts(c("XW"), pX, MAGIC, A_.add, -MAGIC, A_.add)
+        sca(c("X"), wu(OV0 + b), c("XW"))
+        mm([(pX, c("I"), c(y)), (pX, c("nI"), c("XN"))])
+        act(c(yn), pX, F_.Abs)
+        dist("R", "XN", pY, pR, [crow(pR, "KR0"), crow(pR, "KR1")] + turn(pR, "XN", "BR"), 0, lambda l: l)
+        act(c("NW"), pR, F_.Sign, bias=0.0 if t == 1 else col(THR), scale=-1.0)
+        mm([(pB, c("BO"), c(vs))] + turn(pB, "NW", "nI4"))
+        act(c("T2"), pB, F_.Identity, bias=col(N4))
+        mm([(pX, c("If"), c(Ao)), const(pX, 1)] + turn(pX, "NW", "I4"))
+        tt(c(An), pX, c("T2"), A_.max)
+        if t < RO:
+            cp(c("Au"), c(An))
+        if t > 1:
+            mm([crow(pA, "KDR")] + turn(pA, Ao, "If"))
+            tt(wf(T4), c("NW", 0, 256, 16), wf(KS), A_.mult)
+            tt(sub(pA, 0, 256, 16), sub(pA, 0, 256, 16), wf(T4), A_.max)
+            scan(c("SEL"), c("NW"), pA, A_.mult, A_.max)
+            rows(c("SEL", 15, 256, 16), 7936, 0, pB, "RWU")
+            lists(None, "BS")
+            cp(wf(BF), pw(1))
+            dedup(BF, wu(OB))
+            sca(c("TR"), wu(OB), c("BS"))
+        sca(c("TR"), wu(OV0 + a), c(vs))
+
+    def seekers(t):
+        b = t % 2
+        zi, zo, An, vs = "ZI%d" % t, "ZO%d" % t, "A%d" % b, "VS%d" % b
+        z, j = c(zi, 0, 256), c(zi, 256, 272)
+        cp(wu(JU), j)
+        for h in (0, 1):
+            mm([(sub(pw(2), 8 * h, 8 * h + 8), c(zi, 128 * h, 128 * h + 128), gs(k)) for k in (6, 7)])
+        rows(pw(2), 3840, 4, pE, "RWS")
+        mm([(pT, top("GR16", 16), top("RWS", 16)), const(pT, 2)])
+        mm(toW(pw(5), "GBl", "RWS", 16))
+        tt(wf(J1), pw(5), j, A_.subtract)
+        gat(c("Bf"), c(An), wu(JU))
+        gat(c("VJ"), c(vs), wu(JU))
+        mm(toW(pw(4), "E1", "VJ"))
+        cp(wf(VJW), pw(4))
+        mm([(pQ, c("I2f"), c("Bf")), const(pQ, 3)])
+        tt(c("Pf"), c("Bf"), pT, A_.mult)
+        tt(c("Si"), c("Pf"), pQ, A_.add)
+        ts(c("Hi"), c("Si"), 5, A_.arith_shift_right, 4095, A_.bitwise_and)
+        cp(c("Hu"), c("Hi"))
+        gather("H", "Hu", t)
+        mm([crow(pE, "KDH")] + turn(pE, "Bf", "Jf"))
+        dist("H", zi, pZ, pH, [crow(pH, "KH0"), crow(pH, "KH1")] + turn(pH, zi, "BH"), 0, lambda l: 15 - l, 15)
+        act(c("NH"), pH, F_.Sign)
+        scan(c("SEH"), c("NH"), pE, A_.mult, A_.max)
+        rows(c("SEH", 15, 256, 16), 3840, 4, pQ, "RWS")
+        mm(toW(pw(3), "GB", "RWS", 16))
+        for k in range(3):
+            cp(wu(PU0), pw(3))
+            gat(c("PS"), c("TR", 0, 4096), wu(PU0))
+            mm(toW(pw(3), "E1", "PS"))
+        cp(wu(PU0), pw(3))
+        gat(c("XP"), X, wu(PU0))
+        tt(wf(FW), pw(3), wf(VJW), A_.is_equal)
+        if t < RO:
+            add({"V": ([lambda: g.vector.tensor_reduce(T.C[:, FS:FS + 1], wf(FW)[0], AxisListType.X, A_.add)], vc(16))}, [wf(FW)], [col(FS)])
+            pf = sub(pw(6), 0, 1)
+            mm([(pf, c("ONf"), col(FS))])
+            cp(ci(5), pf)
+            ts(ci(6), ci(5), 15, A_.bitwise_and)
+            ts(col(THR), ci(6), 16.0, A_.mult)
+        tt(wf(J2), wf(J1), wf(FW), A_.mult)
+        tt(c(zo, 256, 272), wf(J2), j, A_.add)
+        mm([(pS, c("BO"), c("PS")), (pS, c("nBO"), c("VJ"))])
+        act(c("AB"), pS, F_.Abs)
+        mm([(pT, c("I4"), c("AB"))])
+        mm([(pE, c("I"), z), (pE, c("nI"), c("XP"))])
+        act(c("AD"), pE, F_.Abs)
+        mm([(pS, c("hI"), z), (pS, c("nI4"), c("AB")), const(pS, 0), (pS, c("hI"), c("XP"))])
+        ts(c("HS"), pS, MAGIC, A_.add, -MAGIC, A_.add)
+        tt(pT, c("AD"), pT, A_.min)
+        tt(c(zo, 0, 256), c("HS"), pT, A_.max)
+        if t < RO:
+            send(t)
+
+    if "c" in CFG["pN"] and "d" in CFG["pN"]:
+        ts(c("G16l", 0, 128), c("nBO"), 16.0, A_.mult)
+        for l in range(16):
+            if CFG["pN"][l // 4] == "d":
+                ms(c("G16l", l, 128, 16), 0.0)
+    users(1)
+    for t in range(1, RO + 1):
+        seekers(t)
+        if t < RO:
+            users(t + 1)
+        if t == RO - 1:
+            dma("Y", T.ya[:], T.A0[:], [c("A0")], [], 131072)
+            dma("Y", T.yy[:], T.Y0[:], [c("Y0")], [], 65536)
+            o = top("P3", 8, 0, 256)
+            mm([(o, gs(0), c("VS0"))])
+            cp(top("OUT", 8, 0, 256), o, "VS")
+            dma("Y", T.yv[:], T.OUT[0:8, 0:256], [c("OUT", 0, 256)], [], 8192)
+            dma("G", T.yt[:], T.TR[0:128:16, 0:4096], [c("TR")], [c("DUMR")], 131072)
+            dma("G", T.yt[:], T.TR[1:128:16, 0:4096], [c("TR"), c("DUMR")], [], 131072, accum_op=A_.add, max_dma_last_dim=4096)
+    dma("Y", T.yz[:], T.ZO4[:, 0:256], [c("ZO4", 0, 256)], [], 65536)
+    mm([(top("P3", 8, 256 + i, 512, 16), c("I", i, 128, 16), c("ZO4", 256, 272)) for i in range(16)], each=True)
+    cp(top("OUT", 8, 256, 512), top("P3", 8, 256, 512), "V")
+    dma("S", T.yj[:], T.OUT[0:8, 256:512], [c("OUT", 256, 512)], [], 8192)
+    return ops, Q, ndma[0]
+
+
+def schedule(ops):
+    LAT, SLACK = PL["LAT"], PL["SLACK"]
+    n = len(ops)
+    succ = [[] for _ in range(n)]
+    for k, o in enumerate(ops):
+        for d in o["raw"] | o["oth"]:
+            succ[d].append(k)
+    bl = [0.0] * n
+    for k in range(n - 1, -1, -1):
+        o = ops[k]
+        bl[k] = min(a[1] for a in o["alts"].values()) + o["lat"] + max([bl[s] + LAT for s in succ[k]] + [0.0])
+    x = PL["SEED"]
+    pr = list(bl)
+    if x:
+        for k in range(n):
+            x = (x * 1103515245 + 12345) % 2147483648
+            pr[k] += PL["NOISE"] * x / 2147483648.0
+    seq = []
+    left = [len(o["raw"] | o["oth"]) for o in ops]
+    ready = [k for k in range(n) if left[k] == 0]
+    free = dict((e, 0.0) for e in "VSPGY")
+    end, eng, rt = [0.0] * n, [None] * n, [0.0] * n
+    last, lock = {}, {}
+    order = dict((e, []) for e in "VSPGY")
+    busy = dict((e, 0.0) for e in "VSPGY")
+    while ready:
+        best = None
+        for e in "PVSGY":
+            cand = []
+            for k in ready:
+                o = ops[k]
+                if e not in o["alts"] or (o["starts"] and lock.get(o["starts"])):
+                    continue
+                r = rt[k]
+                for b in o["banks"]:
+                    if b in last and eng[last[b]] != e:
+                        r = max(r, end[last[b]] + LAT)
+                cand.append((max(r, free[e]), k))
+            if not cand:
+                continue
+            t0 = min(x[0] for x in cand)
+            s, k = max((x for x in cand if x[0] <= t0 + SLACK), key=lambda x: pr[x[1]])
+            if best is None or t0 < best[0]:
+                best = (t0, s, k, e)
+        t0, s, k, e = best
+        o = ops[k]
+        o["dyn"] = set(last[b] for b in o["banks"] if b in last and eng[last[b]] != e)
+        eng[k] = e
+        free[e] = s + o["alts"][e][1]
+        busy[e] += o["alts"][e][1]
+        end[k] = free[e] + o["lat"]
+        o["t"] = s
+        for b in o["banks"]:
+            last[b] = k
+        if o["opens"]:
+            lock[o["opens"]] = True
+        if o["closes"]:
+            lock[o["closes"]] = False
+        order[e].append(k)
+        seq.append(k)
+        ready.remove(k)
+        for s2 in succ[k]:
+            wait = e != "P" or "P" not in ops[s2]["alts"]
+            rt[s2] = max(rt[s2], end[k] + LAT if wait else s)
+            left[s2] -= 1
+            if left[s2] == 0:
+                ready.append(s2)
+    assert sum(len(v) for v in order.values()) == n
+    return order, eng, max(end), busy, seq
+
+
+def rank_program(g, core, T, topo):
+    rank = T.rank_of(core)
+    if rank is None:
+        return
+    nxt = T.cores[(rank + 1) % len(T.cores)]
+    rid, pid, _ = topo.addr(nxt)
+    mask = topo.mask(core, nxt)
+    neng = len(topo.engines(core, nxt))
+    ops, Q, nd = build(g, T, (rid, pid, mask))
+    order, eng, _, _, seq = schedule(ops)
+    tick = {}
+    for e, L in order.items():
+        m = 0
+        for k in L:
+            o = ops[k]
+            if o["sem"]:
+                tick[k] = (o["sem"], neng if o.get("remote") else 16)
+            else:
+                m += 1
+                tick[k] = (e, m)
+    seen_all, clock, waits = {}, {}, {}
+    seen = dict((e, {}) for e in order)
+    for k in seq:
+        o, e = ops[k], eng[k]
+        deps = [d for d in o["raw"] | o["oth"] | o["dyn"] if not (e == "P" and eng[d] == "P")]
+        need = {}
+        for d in sorted(deps, key=lambda d: -ops[d]["t"]):
+            s, v = tick[d]
+            if seen[e].get(s, 0) < v:
+                need[s] = max(need.get(s, 0), v)
+                for s2, v2 in clock[d].items():
+                    seen[e][s2] = max(seen[e].get(s2, 0), v2)
+        waits[k] = need
+        clock[k] = {} if o.get("remote") else dict(seen[e])
+        clock[k][tick[k][0]] = tick[k][1]
+    for e, L in order.items():
+        for k in L:
+            o = ops[k]
+            for s, v in sorted(waits[k].items()):
+                Q[e].wait_ge(T.sem[s], v)
+                seen_all[s] = max(seen_all.get(s, 0), v)
+            for f in o["alts"][e][0]:
+                ins = f()
+            if not o.get("remote"):
+                ins.then_inc(T.sem[o["sem"] or e], 16 if o["sem"] else 1)
+    top = {}
+    for s, v in tick.values():
+        top[s] = max(top.get(s, 0), v)
+    for s, v in sorted(top.items()):
+        if seen_all.get(s, 0) < v:
+            g.sync.wait_ge(T.sem[s], v)
+    for t in range(RO):
+        g.sync.wait_ge(T.sem["sent%d" % t], neng)

@@ -1,17 +1,18 @@
+import math
 from concourse.mybir import AluOpType, AxisListType, ActivationFunctionType
 
 A_ = AluOpType
 F_ = ActivationFunctionType
-WN = 4352
+WN = 4368
+SPARE = 4112.0
 MAGIC = 12582912.0
 RO = 4
 
 CFG = {
-    "stage": 512,
-    "gN": ["SV", "SS", "SS", "SS"], "gR": ["SS"] * 4, "gH": ["SVSV"] * 4,
-    "pN": "cccc", "pR": "cccc", "pH": "cccc",
-    "hN": 1, "hR": 1, "hH": 2,
-    "small": "S", "evac": "VS",
+    "gN": ["SVSVSVSV"] + ["S" * 8] * 3, "gR": ["S" * 8] * 4, "gH": ["S" * 8] * 3 + ["SVSSVSSV"],
+    "hN": [(0, 128, 256)] * 4, "hR": [(0, 128, 256)] * 4, "hH": [(0, 128, 256)] * 4,
+    "cN": [(0, 0)] * 4, "cR": [(0, 0)] * 4, "cH": [(0, 0)] * 4,
+    "small": "VS", "evac": "VS",
 }
 
 S = {}
@@ -22,35 +23,43 @@ def _sb(names, shape, dty):
         S[n] = ("sbuf", shape, dty)
 
 
-_sb("X TR", [128, WN], "bfloat16")
+_sb("X", [128, WN], "bfloat16")
+_sb("TR", [128, WN], "float32")
 _sb("NB", [128, 4096], "int32")
-_sb("GN MN GR MR GH MH EB", [128, 4096], "bfloat16")
-_sb("TD G16 G16l", [128, 2048], "bfloat16")
-_sb("A0 A1 NBf PM SEL SEH RS T2 Bf Pf COL COLG DUMR", [128, 256], "float32")
-_sb("Ai Si Hi VJi", [128, 256], "int32")
-_sb("NBu Au Ru Hu", [128, 256], "uint16")
-_sb("Y0 Y1 NE XN VS0 VS1 BS NW XW CS KC ONE NH PS XP VJ AD AB HS AM LO RWU RWS", [128, 256], "bfloat16")
-_sb("KR0 KR1 KH0 KH1 KDR KDH", [128, 256], "bfloat16")
+_sb("GN MN GR MR GH MH MC EB EC", [128, 4096], "bfloat16")
+_sb("TD", [128, 2048], "bfloat16")
+_sb("AW V0 V1 PM SEL SEP SC RS MK PR Pf COL COLG KC DUMR", [128, 256], "float32")
+_sb("Ai Si Ui Hi VJi", [128, 256], "int32")
+_sb("NBu Au Hu", [128, 256], "uint16")
+_sb("A0 A1 NBc RW RP RU0 RU1 RB ZH Bc VJ PS", [128, 256], "float16")
+_sb("Y0 Y1 NE XN XW SR SH ONE XP FD HS M1 MB JR C2K KR KD", [128, 256], "bfloat16")
 _sb("ZO0 ZO1 ZO2 ZO3 ZO4 ZI1 ZI2 ZI3 ZI4", [128, 272], "bfloat16")
-_sb("E1 E8 GB GBl", [128, 144], "bfloat16")
-_sb("I nI hI I4 nI4 BO nBO BR BH GR16 GS16", [128, 128], "bfloat16")
-_sb("If Jf I2f ONf", [128, 128], "float32")
-_sb("CL", [128, 512], "bfloat16")
-_sb("GS", [128, 64], "bfloat16")
+_sb("E1 E2 nE Es EW E4 S4 G4", [128, 144], "bfloat16")
+_sb("CQ", [128, 144], "float32")
+_sb("MQ", [128, 64], "float32")
+_sb("I nI I4 nI4 I2 I32 KI nKI BO nBO BO8 WH WL TH RG", [128, 128], "bfloat16")
+_sb("fI", [128, 128], "float16")
+_sb("T16", [128, 16], "float16")
+_sb("O16", [128, 128], "float32")
+_sb("CL KK", [128, 512], "bfloat16")
+_sb("MX", [128, 1024], "bfloat16")
+_sb("GS", [128, 48], "bfloat16")
 _sb("C", [128, 64], "float32")
 _sb("Ci", [128, 16], "int32")
-_sb("Wf", [128, 256], "float32")
-_sb("Wi", [128, 256], "int32")
-_sb("Wb", [128, 64], "bfloat16")
-_sb("Wu", [128, 256], "uint16")
-_sb("OUT", [128, 512], "float32")
+_sb("Wf", [128, 128], "float32")
+_sb("Wi", [128, 32], "int32")
+_sb("Wu", [128, 128], "uint16")
+_sb("OUT", [128, 768], "float32")
 for _b in range(8):
     S["P%d" % _b] = ("psum", [128, 512], "float32")
 SCRATCH = S
 NDMA = 18
 SEMAPHORES = ["V", "S", "P", "G"] + ["d%d" % k for k in range(NDMA)] + ["arr%d" % k for k in range(1, 5)] + ["sent%d" % k for k in range(4)]
 
-PL = {"CY": 1.0, "PCY": 0.5, "GA": 1.56, "SC": 3.8, "LAT": 120.0, "OVH": 40.0, "MM": 5.0, "SLACK": 60.0, "BW": 250.0, "SEED": 1, "NOISE": 300.0}
+SETS = [dict(CY=.85, PCY=.43, GA=1.56, SC=3.8, LAT=100., OVH=10., MM=3., BW=250., SEND=2000., W=0.5),
+        dict(CY=1.0, PCY=.55, GA=1.3, SC=2.8, LAT=150., OVH=25., MM=8., BW=350., SEND=1500., W=0.4)]
+PL = {"SEED": 1, "NOISE": 0.0, "PASSES": 2, "STEPS": 40000, "TEMP": 80.0, "MEAN": 0.3,
+      "LEAD": {"g": -5000.0, "m": -5000.0, "y": 20000.0, "r": -3000.0}}
 
 
 def build(g, T, dest):
@@ -58,12 +67,13 @@ def build(g, T, dest):
     ops = []
     acc = {}
     ndma = [0]
+    tail = {}
+    tag = [""]
     Q = {"V": g.vector, "S": g.scalar, "P": g.tensor, "G": g, "Y": g.sync}
-    al = slice(None)
 
     def top(name, rows, a=None, b=None, s=None):
         r = range(S[name][1][1])[a:b:s]
-        return (T[name][0:rows, a:b:s], name, r[0], r[-1] + 1, len(r), S[name][2] in ("bfloat16", "uint16"), s or 1)
+        return (T[name][0:rows, a:b:s], name, r[0], r[-1] + 1, len(r), S[name][2] in ("bfloat16", "uint16", "float16"), s or 1)
 
     def c(name, a=None, b=None, s=None):
         return top(name, 128, a, b, s)
@@ -76,20 +86,19 @@ def build(g, T, dest):
         raw, oth = set(), set()
 
         def meets(a, e):
-            return e[0] < a[3] and a[2] < e[1] and (a[6] != e[4] or (a[2] - e[0]) % a[6] == 0)
+            return e[0] < a[3] and a[2] < e[1] and (a[2] - e[0]) % math.gcd(a[6], e[4]) == 0
         for a in rd:
             raw.update(e[3] for e in acc.setdefault(a[1], []) if e[2] and meets(a, e))
         for a in wr:
             oth.update(e[3] for e in acc.setdefault(a[1], []) if meets(a, e))
         for a in wr:
-            if a[3] - a[2] == a[4]:
-                acc[a[1]] = [e for e in acc[a[1]] if not (a[2] <= e[0] and e[1] <= a[3])]
-        for a in rd:
-            acc[a[1]].append((a[2], a[3], False, k, a[6]))
-        for a in wr:
-            acc[a[1]].append((a[2], a[3], True, k, a[6]))
+            acc[a[1]] = [e for e in acc[a[1]] if not (a[2] <= e[0] and e[1] <= a[3] and e[4] % a[6] == 0 and (e[0] - a[2]) % a[6] == 0)]
+        for a in set(x[1:] for x in rd):
+            acc[a[0]].append((a[1], a[2], False, k, a[5]))
+        for a in set(x[1:] for x in wr):
+            acc[a[0]].append((a[1], a[2], True, k, a[5]))
         banks = set(a[1] for a in list(rd) + list(wr) if S[a[1]][0] == "psum")
-        op = dict(alts=alts, raw=raw, oth=oth - raw, banks=banks, lat=0.0, sem=None, opens=None, closes=None, starts=None, out=wr[0][1] if wr else "")
+        op = dict(alts=alts, raw=raw, oth=oth - raw, soft=set(), banks=banks, lat=0.0, sem=None, out=wr[0][1] if wr else "", tag=tag[0])
         op.update(kw)
         ops.append(op)
         return k
@@ -118,13 +127,15 @@ def build(g, T, dest):
         r = 1.0 if isp(a) or isp(b) else 2.0
         return add({"V": ([lambda: g.vector.tensor_tensor(out[0], a[0], b[0], op)], vc(out[4] * r))}, [a, b], [out])
 
-    def cp(out, a, eng="V"):
+    def cp(out, a, eng="V", bias=None):
         alts = {}
         if "V" in eng:
-            alts["V"] = ([lambda: g.vector.tensor_copy(out[0], a[0])], vc(out[4] * (0.5 if out[5] and a[5] else 1.0)))
+            f = (lambda: g.vector.tensor_copy(out[0], a[0])) if bias is None else (lambda: g.vector.tensor_scalar(out[0], a[0], bias[0], None, A_.add))
+            alts["V"] = ([f], vc(out[4] * (0.5 if out[5] and a[5] else 1.0)))
         if "S" in eng:
-            alts["S"] = ([lambda: g.scalar.activation(out[0], a[0], F_.Copy)], vc(out[4]))
-        return add(alts, [a], [out])
+            f = (lambda: g.scalar.activation(out[0], a[0], F_.Copy)) if bias is None else (lambda: g.scalar.activation(out[0], a[0], F_.Identity, bias=bias[0]))
+            alts["S"] = ([f], vc(out[4]))
+        return add(alts, [a] + cols(bias), [out])
 
     def ms(out, v):
         return add({"V": ([lambda: g.vector.memset(out[0], v)], vc(out[4] * (0.5 if out[5] else 1.0)))}, [], [out])
@@ -140,16 +151,16 @@ def build(g, T, dest):
         n = off[4] * 16
         alts = {}
         if "V" in eng:
-            alts["V"] = ([lambda: g.vector.tensor_copy(out[0], win[0].indirect(off[0]))], 60 + n * GA * CY)
+            alts["V"] = ([lambda: g.vector.tensor_copy(out[0], win[0].indirect(off[0]))], 50 + n * GA * CY)
         if "S" in eng:
-            alts["S"] = ([lambda: g.scalar.activation(out[0], win[0].indirect(off[0]), F_.Copy)], 78 + n * GA * CY)
+            alts["S"] = ([lambda: g.scalar.activation(out[0], win[0].indirect(off[0]), F_.Copy)], 65 + n * GA * CY)
         return add(alts, [win, off], [out])
 
     def sca(win, off, src):
-        return add({"V": ([lambda: g.vector.tensor_copy(win[0].indirect(off[0]), src[0])], 60 + src[4] * SC * CY)}, [off, src], [win])
+        return add({"V": ([lambda: g.vector.tensor_copy(win[0].indirect(off[0]), src[0])], 50 + src[4] * SC * CY)}, [off, src], [win])
 
-    def mm(terms, first=True, last=True, each=False):
-        fs, cost, rd, wr = [], 0.0, [], []
+    def mm(terms, first=True, last=True, each=False, after=()):
+        fs, cost, rd, wr = [], 0.0, list(after), []
         for k, (o, l, r) in enumerate(terms):
             st = each or (first and k == 0)
             sp = each or (last and k == len(terms) - 1)
@@ -158,22 +169,39 @@ def build(g, T, dest):
             rd += [l, r]
             wr.append(o)
         bank = terms[0][0][1]
-        return add({"P": (fs, cost + OVH)}, rd, wr, starts=bank if first else None,
-                   opens=bank if first and not last else None, closes=bank if last and not first else None)
+        k = add({"P": (fs, cost)}, rd, wr)
+        st = tail.setdefault(bank, {"end": [], "since": [], "outs": set()})
+        ops[k]["soft"].update(st["end"])
+        if first and last:
+            st["since"].append(k)
+        else:
+            ops[k]["soft"].update(st["since"])
+            st["end"], st["since"] = [k], []
+            st["outs"] = set(o[1:] for o in wr) | (set() if first else st["outs"])
+            if last:
+                for a in st["outs"]:
+                    acc[bank].append((a[1], a[2], True, k, a[5]))
+        return k
 
     def gp(f, n, rd, wr):
         return add({"G": ([f], 170 + 2 * n * CY)}, rd, wr)
 
-    def dma(q, out, in_, rd, wr, nbytes, **kw):
+    busy = [2000.0]
+
+    def dma(q, out, in_, rd, wr, nbytes, load=False, **kw):
         s = "d%d" % ndma[0]
         ndma[0] += 1
-        return add({q: ([lambda: Q[q].dma_start(out, in_, **kw)], 60.0 if q != "G" else 1000.0)}, rd, wr, sem=s, lat=1800 + nbytes / PL["BW"])
+        lat = 2000 + nbytes / PL["BW"]
+        if load:
+            busy[0] += nbytes / PL["BW"]
+            lat = busy[0]
+        return add({q: ([lambda: Q[q].dma_start(out, in_, **kw)], 60.0 if q != "G" else 1000.0)}, rd, wr, sem=s, lat=lat)
 
     def wf(k):
         return c("Wf", 16 * k, 16 * k + 16)
 
-    def wi(k, n=1):
-        return c("Wi", 16 * k, 16 * (k + n))
+    def wi(k):
+        return c("Wi", 16 * k, 16 * k + 16)
 
     def wu(k):
         return c("Wu", 16 * k, 16 * k + 16)
@@ -187,419 +215,525 @@ def build(g, T, dest):
     def E(name, l, rows=128):
         return top(name, rows, 15 - l, 143 - l)
 
-    def gs(k):
-        return c("GS", 8 * k, 8 * k + 8)
-
-    def const(out, k):
-        return (out, top("CL", 1, 128 * k, 128 * k + 128), top("ONE", 1, 0, 256))
-
-    def crow(out, name):
-        return (out, top("ONE", 1, 0, 128), top(name, 1, 0, 256))
+    def const(out, k, n=256):
+        return (out, top("CL", 1, 128 * k, 128 * k + 128), top("ONE", 1, 0, n))
 
     def toW(out, e, src, rows=128):
         return [(out, E(e, i, rows), top(src, rows, i, 256, 16)) for i in range(16)]
 
-    for s in (0, 1):
-        dma("S", T.VJi[s:16:2, :], T.v0[:], [], [c("VJi", s, s + 1)], 8192)
-    dma("S", T.VJi[32:40, :], T.j0[:], [], [c("VJi", 2, 3)], 8192)
-    dma("Y", T.Ai[:], T.a0[:], [], [c("Ai")], 131072)
-    dma("Y", T.X[:, 0:4096], T.x[:], [], [c("X", 0, 4096)], 1 << 20)
-    dma("Y", T.NB[:], T.nb[:], [], [c("NB")], 3 << 20)
-    dma("S", T.ZO0[:, 0:256], T.z0[:], [], [c("ZO0", 0, 256)], 65536)
-    dma("S", T.Y0[:], T.y0[:], [], [c("Y0")], 65536)
-    dma("S", T.Ci[:, 8:9], T.w[:], [], [c("Ci", 8, 12)], 512)
+    ld = [dma("Y", T.VJi[0:8, :], T.v0[:], [], [c("VJi")], 8192, True),
+          dma("Y", T.Ai[:], T.a0[:], [], [c("Ai")], 131072, True),
+          dma("Y", T.X[:, 0:4096], T.x[:], [], [c("X", 0, 4096)], 1 << 20, True),
+          dma("Y", T.Hi[0:8, :], T.j0[:], [], [c("Hi")], 8192, True),
+          dma("Y", T.Ci[:, 8:9], T.w[:], [], [c("Ci", 8, 12)], 512, True),
+          dma("Y", T.ZO0[:, 0:256], T.z0[:], [], [c("ZO0", 0, 256)], 65536, True),
+          dma("Y", T.Y0[:], T.y0[:], [], [c("Y0")], 65536, True),
+          dma("Y", T.NB[:], T.nb[:], [], [c("NB")], 2 << 20, True)]
+    for k in ld[1:]:
+        ops[k]["soft"].add(k - 1)
+    small = dict(allow_small_or_imprecise_dtypes=True)
     gp(lambda: g.iota(T.Ci[:, 0:1], [[0, 1]], 0, 1), 1, [], [ci(0)])
-    gp(lambda: g.iota(T.COL[:], [[1, 256]], 0, 0, allow_small_or_imprecise_dtypes=True), 256, [], [c("COL")])
-    gp(lambda: g.iota(T.KC[:], [[0, 16], [1, 16]], 0, 0, allow_small_or_imprecise_dtypes=True), 256, [], [c("KC")])
-    gp(lambda: g.iota(T.COLG[:], [[1, 16], [0, 16]], 0, 0, allow_small_or_imprecise_dtypes=True), 256, [], [c("COLG")])
-    P_, L_, G_, T15, RV, KB, THR, M0, M1, WH, WL, FS, T8, T16, OD, G2, EV, TS16, N4 = range(19)
-    LT, HI = 24, 40
+    gp(lambda: g.iota(T.COL[:], [[1, 256]], 0, 0, **small), 256, [], [c("COL")])
+    gp(lambda: g.iota(T.COLG[:], [[1, 16], [0, 16]], 0, 0, **small), 256, [], [c("COLG")])
+    gp(lambda: g.iota(T.KC[:], [[0, 16], [1, 16]], 0, 0, **small), 256, [], [c("KC")])
+    gp(lambda: g.iota(T.KK[0:1, 0:256], [[0, 16], [1, 16]], 0, 0, **small), 256, [], [c("KK", 0, 256)])
+    gp(lambda: g.iota(T.KK[0:1, 256:512], [[0, 16], [-8192, 16]], 131072, 0, **small), 256, [], [c("KK", 256, 512)])
+    gp(lambda: g.iota(T.TR[:], [[1, WN]], -2048, 0, **small), WN, [], [c("TR")])
+    P_, L_, G_, T15, Q4, L0, W8, WH_, WL_, FS, FR, THR, QC, THH, CH, P2K, K0, K1, K2, K3, K4, K5 = range(22)
+    LT = 24
+    BIG = 2097152.0
+    ms(c("CQ"), -1.0)
+    gp(lambda: g.iota(T.CQ[:, 3:131:4], [[1, 8], [0, 4]], 0, 0, **small), 32, [], [c("CQ")])
+    gp(lambda: g.iota(T.SC[:, 0:64], [[0, 16], [1, 4]], 0, 0, **small), 64, [], [c("SC", 0, 64)])
     cp(col(P_), ci(0))
     ts(ci(1), ci(0), 15, A_.bitwise_and)
     ts(ci(2), ci(0), 4, A_.arith_shift_right)
-    ts(ci(3), ci(0), 1, A_.bitwise_and)
-    ts(ci(7), ci(0), 1, A_.arith_shift_right)
+    ts(ci(3), ci(1), 2, A_.arith_shift_right)
     cp(col(L_), ci(1))
     cp(col(G_), ci(2))
-    cp(col(OD), ci(3))
-    cp(col(G2), ci(7))
-    ts(col(EV), ci(3), -1.0, A_.mult, 1.0, A_.add)
+    cp(col(Q4), ci(3))
+    ts(col(QC), ci(3), -BIG, A_.mult, 3 * BIG, A_.add)
+    ts(c("SC", 64, 128), c("SC", 0, 64), col(Q4), A_.is_equal, 9 * BIG, A_.mult)
+    ts(c("MQ"), c("SC", 64, 128), -BIG, A_.add)
     ts(col(T15), ci(2), 16.0, A_.mult, 15.0, A_.add)
-    ts(col(T16), ci(7), 16.0, A_.mult, 15.0, A_.add)
-    ts(col(TS16), ci(7), 16.0, A_.mult, col(OD), A_.add)
-    ts(col(T8), ci(0), 16.0, A_.mult, 15.0 - 512.0, A_.add)
-    ts(col(RV), ci(1), -1.0, A_.mult, col(T15), A_.add)
-    ms(col(N4), -4096.0)
+    ts(col(L0), ci(1), 0.0, A_.is_equal)
+    ts(col(FR), ci(1), 15.0, A_.is_equal, 65536.0, A_.mult)
+    ts(col(FS), ci(1), 102.0, A_.mult, 102.5, A_.add)
+    tt(col(THH), col(FR), col(FS), A_.add)
+    ts(col(CH), ci(1), 4096.0, A_.mult, 4096.0, A_.add)
+    for k, (m, v) in enumerate(((75.0, -80.0), (74.5, -80.0), (-524288.0, 524288.0), (-16384.0, 0.0), (262144.0, 0.0), (2048.0, 0.0))):
+        ts(col(K0 + k), ci(0), m, A_.mult, v, A_.add)
+    c2 = lambda k: top("C", 2, k, k + 1)
+    ts(top("KR", 2), top("KC", 2), c2(K0), A_.mult, c2(K1), A_.add)
+    ts(top("SEP", 2), top("COLG", 2), c2(K2), A_.mult)
+    ts(top("AW", 2), top("KC", 2), c2(K3), A_.mult, c2(K4), A_.add)
+    ts(top("AW", 2, 0, 256, 16), top("AW", 2, 0, 256, 16), c2(K5), A_.add)
+    tt(top("KD", 2), top("SEP", 2), top("AW", 2), A_.add)
+    ms(col(P2K), 2048.0)
     ms(c("ONE"), 1.0)
-    ms(c("ONf"), 1.0)
-    for k, v in enumerate((-0.25, -4096.0, -2016.0, -4194304.0)):
+    ms(c("O16"), 16.0)
+    ms(c("C2K"), 2048.0)
+    for k, v in enumerate((2048.0, -4128768.0, -120.0, -4096.0)):
         ms(top("CL", 1, 128 * k, 128 * k + 128), v)
-    ts(c("GB"), c("COL", 0, 144), col(T16), A_.is_equal)
-    ts(c("GBl"), c("COL", 0, 144), col(T16), A_.is_equal, col(OD), A_.mult)
-    ts(c("GR16"), c("COLG", 0, 128), col(G2), A_.is_equal)
-    ts(c("GS16"), c("COL", 0, 128), col(TS16), A_.is_equal)
-    for n, v in (("E1", 1.0), ("E8", 8192.0)):
+    ts(top("G4", 8), top("CQ", 8), top("C", 8, P_, P_ + 1), A_.is_equal)
+    ts(top("RG", 8), top("COLG", 8, 0, 128), top("C", 8, P_, P_ + 1), A_.is_equal)
+    for n, v in (("E4", 1.0), ("S4", col(L0))):
+        ts(c(n), c("CQ"), col(G_), A_.is_equal, v, A_.mult)
+    for n, v in (("E1", 1.0), ("E2", 2.0), ("nE", -1.0), ("Es", col(L0))):
         ts(c(n), c("COL", 0, 144), col(T15), A_.is_equal, v, A_.mult)
-    for n, v in (("I", 1.0), ("nI", -1.0), ("hI", 0.5), ("I4", 4096.0), ("nI4", -4096.0), ("If", 1.0), ("I2f", 2048.0)):
+    for n, v in (("I", 1.0), ("nI", -1.0), ("I4", 4096.0), ("nI4", -4096.0), ("I2", 2048.0), ("I32", 32.0), ("KI", 1024.0), ("nKI", -1024.0), ("fI", 2047.0 / 4096.0)):
         ts(c(n), c("COL", 0, 128), col(P_), A_.is_equal, v, A_.mult)
-    ts(c("Jf"), c("COL", 0, 128), col(RV), A_.is_equal)
-    ts(c("BO"), c("COLG", 0, 128), col(G_), A_.is_equal)
-    ts(c("nBO"), c("COLG", 0, 128), col(G_), A_.is_equal, -1.0, A_.mult)
-    for k, v in enumerate((1.0, 2.0, -1.0, 16.0, 32.0, -16.0)):
-        ts(gs(k), c("COL", 0, 8), col(G_), A_.is_equal, v, A_.mult)
-    ts(col(KB), ci(1), -4096.0, A_.mult, 61440.0, A_.add)
-    ts(col(M0), ci(1), 0.0, A_.is_equal, 256.0, A_.mult)
-    ts(col(M1), ci(1), 1.0, A_.is_equal)
-    ts(c("LO"), c("COL"), col(M1), A_.mult)
-    ts(c("C", HI, HI + 17), c("COL", 0, 17), col(M0), A_.mult)
-    for k in range(17):
-        o = c("TR", 256 * k, 256 * k + 256)
-        add({"V": ([lambda o=o, k=k: g.vector.tensor_scalar(o[0], T.LO[:], T.C[:, HI + k:HI + k + 1], None, A_.add)], vc(128)),
-             "S": ([lambda o=o, k=k: g.scalar.activation(o[0], T.LO[:], F_.Identity, bias=T.C[:, HI + k:HI + k + 1])], vc(256))},
-            [c("LO"), col(HI + k)], [o])
+    for n, v in (("BO", 1.0), ("BO8", 8192.0)):
+        ts(c(n), c("COLG", 0, 128), col(G_), A_.is_equal, v, A_.mult)
+    for k, v in enumerate((32.0, -16.0, 16.0, 2.0, -1.0, 1.0)):
+        ts(c("GS", 8 * k, 8 * k + 8), c("COL", 0, 8), col(G_), A_.is_equal, v, A_.mult)
     ms(c("X", 4096, WN), 0.0)
-    ms(c("CS", 0, 16), 0.0)
     ts(c("RS"), c("KC"), 0.0, A_.is_equal, 1000000.0, A_.mult)
-    r1 = lambda n: top(n, 1, 0, 256)
-    ts(r1("KR0"), r1("KC"), -80.0, A_.mult, -80.0, A_.add)
-    ts(r1("KR1"), r1("KC"), -5.0, A_.mult, -5.5, A_.add)
-    ts(r1("KH0"), r1("KC"), 96.0, A_.mult, -1536.0, A_.add)
-    ts(r1("KH1"), r1("KC"), 6.0, A_.mult, -96.5, A_.add)
-    ms(top("KH0", 1, 0, 256, 16), -65536.0)
-    ts(r1("KDH"), r1("KC"), -4096.0, A_.mult, 61440.0, A_.add)
-    ts(r1("PM"), r1("COLG"), 16.0, A_.mult, 15.0, A_.add)
-    tt(r1("SEL"), r1("PM"), r1("KC"), A_.subtract)
-    ts(r1("KDR"), r1("SEL"), 8192.0, A_.mult)
-    for n, key, pos in (("BR", "pR", lambda l: l), ("BH", "pH", lambda l: 15 - l)):
-        cp(c(n), c("nBO"))
-        for l in range(16):
-            if CFG[key][l // 4] == "d":
-                ms(c(n, pos(l), 128, 16), 0.0)
+    ts(c("PM"), c("KC"), col(L_), A_.is_equal)
+    ts(c("MB"), c("PM"), -30720.0, A_.mult, 32768.0, A_.add)
+    ts(c("SEL"), c("COL"), SPARE, A_.add)
+    tt(c("MK"), c("SEL"), c("PM"), A_.mult)
+    ts(c("PR", 0, 128), c("KC", 0, 128), col(L_), A_.is_gt, 4096.0, A_.mult)
+    tt(c("Pf", 0, 128), c("PR", 0, 128), c("BO"), A_.mult)
+    tt(c("TH"), c("Pf", 0, 128), c("nI4"), A_.add)
     ts(c("C", LT, LT + 16), c("COL", 0, 16), col(L_), A_.is_gt)
     for i in range(1, 16):
-        ts(c("TD", 128 * i, 128 * i + 128), E("E8", i), col(LT + i), A_.mult)
-    DUM, VF, BF, T1, T3, VJW, FW, J1, J2, KS, T4 = range(11)
-    ts(wf(T1), c("COL", 0, 16), 16.0, A_.mult, col(L_), A_.add)
-    ts(wf(DUM), wf(T1), 4096.0, A_.add)
-    ts(wf(KS), c("COL", 0, 16), 131072.0, A_.mult, 4096.0 + 15 * 8192.0, A_.add)
+        ts(c("TD", 128 * i, 128 * i + 128), c("BO8"), col(LT + i), A_.mult)
     ts(ci(4), ci(8), 63, A_.bitwise_and)
-    cp(col(WL), ci(4))
-    tt(col(WH), ci(8), col(WL), A_.subtract)
-    ts(gs(6), gs(0), col(WH), A_.mult)
-    ts(gs(7), gs(0), col(WL), A_.mult)
+    ts(ci(5), ci(8), 255, A_.bitwise_and)
+    cp(col(WL_), ci(4))
+    cp(col(W8), ci(5))
+    tt(col(WH_), ci(8), col(WL_), A_.subtract)
+    ts(c("WH"), c("BO"), col(WH_), A_.mult)
+    ts(c("WL"), c("BO"), col(WL_), A_.mult)
+    ts(c("EW"), c("E4"), col(W8), A_.mult)
 
-    pK, pD = c("P0", 0, 256), c("P0", 256, 512)
-    pH, pS = c("P1", 0, 256), c("P1", 256, 512)
-    pB, pU = c("P2", 0, 256), c("P2", 256, 512)
-    pY, pX = c("P3", 0, 256), c("P3", 256, 512)
-    pZ, pT = c("P4", 0, 256), c("P4", 256, 512)
-    pQ, pE = c("P6", 0, 256) if CFG["stage"] == 512 else c("P5", 256, 512), c("P6", 256, 512)
-    pR = pK if "d" in CFG["pN"] + CFG["pR"] + CFG["pH"] else c("P5", 0, 256)
-    pA = c(pR[1], 256, 512)
+    lo = lambda b: c("P%d" % b, 0, 256)
+    hi = lambda b: c("P%d" % b, 256, 512)
     X = c("X", 0, 4096)
-
-    def pw(k):
-        return c("P7", 256 + 16 * k, 272 + 16 * k)
-    V0, V1, OV0, OV1, OB, JU, PU0 = range(7)
+    pu = lambda k: c("P4", 256 + 64 * k, 320 + 64 * k)
+    pw = lambda k: c("P7", 256 + 64 * k, 320 + 64 * k)
+    V0, V1, OV0, OV1, OB, JU, PU = range(7)
+    T1, T2, T3, J1, J2 = range(5)
+    EV = CFG["evac"]
 
     def send(t):
         src, dst, s = "ZO%d" % t, "ZI%d" % (t + 1), "arr%d" % (t + 1)
         add({"G": ([lambda: g.remote_dma(T[dst][:], T[src][:], T.sem[s], T.sem["sent%d" % t], dest[1], dest[0], dest[2])], 500.0)},
-            [c(src)], [c(dst)], sem=s, lat=2500.0, remote=True)
+            [c(src)], [c(dst)], sem=s, lat=PL["SEND"] if t else busy[0], remote=True)
 
-    def rows(src, mask, k, p, row):
-        cp(wi(k), src)
-        ts(c("Wi", 16 * k + 16, 16 * k + 48, 2), wi(k), mask, A_.bitwise_and)
-        ts(c("Wi", 16 * k + 17, 16 * k + 48, 2), wi(k), 255, A_.bitwise_and)
-        o = 32 * (k // 4)
-        cp(c("Wb", o, o + 32), wi(k + 1, 2))
-        mm([(sub(p, 128 * h, 128 * h + 128, rows=16), c("Wb", o + 16 * h, o + 16 * h + 16), c("I")) for h in (0, 1)], each=True)
-        cp(top(row, 16), sub(p, 0, 256, rows=16), CFG["evac"])
-
-    def dedup(keyf, off):
-        cp(c("Ru"), pU)
+    def dedup(ru, key, eb, off):
+        p = lo(4)
         for k in range(16):
-            ts(c("EB", 256 * k, 256 * k + 256 - 16 * k), c("Ru", 16 * k, 256), c("Wf", 16 * keyf + k, 16 * keyf + k + 1), A_.is_equal)
-        for k0 in (0, 5, 10):
-            mm([(c("P7", 16 * k + 16, 256), c("BO"), c("EB", 256 * k + 16, 256 * k + 256 - 16 * k)) for k in range(k0, k0 + 5)], first=k0 == 0, last=k0 == 10)
-        cp(c("CS", 16, 256), c("P7", 16, 256), CFG["evac"])
-        mm([(pw(0), c("TD", 128 * i, 128 * i + 128), c("EB", i, 4096, 256)) for i in range(1, 16)] + toW(pw(0), "E8", "CS"))
-        tt(wf(T1), pw(0), wf(DUM), A_.min)
-        tt(wf(T3), wf(T1), wf(keyf), A_.max)
-        cp(off, wf(T3))
+            ts(c(eb, 256 * k, 256 * k + 256 - 16 * k), c(ru, 16 * k, 256), col(QC), A_.subtract,
+               c("SC", 64 * key + 4 * k + 3, 64 * key + 4 * k + 4), A_.is_equal)
+        blk = lambda k: (sub(p, 16 * k + 16, 256), c("BO8"), c(eb, 256 * k + 16, 256 * k + 256 - 16 * k))
+        mm([(p, c("I"), c("MB")), (p, c("I"), c(ru))] + [blk(k) for k in range(4)], last=False)
+        mm([blk(k) for k in range(4, 9)], first=False, last=False)
+        mm([blk(k) for k in range(9, 15)], first=False, last=False)
+        mm([(sub(p, i, 256, 16), c("TD", 128 * i, 128 * i + 128), c(eb, i, 4096, 256)) for i in range(1, 16)], first=False)
+        scan(c("PR"), c("MK"), p, A_.max, A_.min)
+        cp(off, c("PR", 15, 256, 16))
 
     def gather(job, lst, t):
         en = CFG["g" + job][t - 1]
         w = 256 // len(en)
         for h, e in enumerate(en):
-            gat(c("G" + job, 16 * w * h, 16 * w * (h + 1)), X, c(lst, w * h, w * (h + 1)), "VS" if e == "A" else e)
+            ops[gat(c("G" + job, 16 * w * h, 16 * w * (h + 1)), X, c(lst, w * h, w * (h + 1)))]["pref"] = e
 
-    stage = [0]
+    def dist(job, oth, pd, head, t):
+        Gn, Mn, cuts = "G" + job, "M" + job, CFG["h" + job][t - 1]
+        pc = "P0" if job == "H" else "P1"
+        f0 = 0 if job == "N" else 24
+        mm([(c(pc, r, 512, 2), c("I"), c(oth, 0, 256)) for r in (0, 1)], each=True)
+        first = True
+        for u0, u1, nc in zip(cuts, cuts[1:], CFG["c" + job][t - 1]):
+            wd = u1 - u0
+            lv = lambda n, l, a=u0, b=u1: c(n, 16 * a + l, 16 * b, 16)
 
-    def dist(job, oth, pc, pd, head, f0, pos, skip=None):
-        Gn, Mn, path, nh = "G" + job, "M" + job, CFG["p" + job], CFG["h" + job]
-        wd = 256 // nh
-        k0, ends = len(ops), []
-        if "c" in path:
-            mm([(pc, c("I"), c(oth, 0, 256))])
-        k = mm(head[:1], last=False)
-        for nm in (Gn, pd[1]):
-            ops[k]["oth"].update([e[3] for e in acc[nm] if e[2] and e[3] != k and (nm == Gn and e[0] == 0 or nm != Gn and job != "R")])
-        tail = head[1:]
-        for p in range(nh):
-            u0 = wd * p
-            per = CFG["stage"] // wd
-            for l0 in range(0, 16, per):
-                ls = [l for l in range(l0, l0 + per) if l != skip]
-                gl = lambda l, a=0, n=wd: c(Gn, 16 * (u0 + a) + l, 16 * (u0 + a + n), 16)
-                ml = lambda l, a=0, n=wd: c(Mn, 16 * u0 + wd * l + a, 16 * u0 + wd * l + a + n)
-                o = lambda l, a: sub(pd, u0 + a + pos(l), u0 + a + 128, 16)
-                parts = [(l, a) for l in ls for a in range(0, wd, 128)]
-                if path[l0 // 4] == "c":
-                    for l in ls:
-                        tt(ml(l), gl(l), sub(pc, u0, u0 + wd), A_.max)
-                    mm([(o(l, a), gl(l, a, 128), gs(f0 + 2)) for l, a in parts], first=False, last=False)
-                    terms = [(o(l, a), ml(l, a, 128), gs(f0 + 1)) for l, a in parts]
+            def terms(n, ls, f):
+                if job != "H":
+                    return [(sub(pd, a + l, a + 128, 16), lv(n, l, a, a + 128), c("GS", f0 + 8 * f, f0 + 8 * f + 8)) for l in ls for a in range(u0, u1, 128)]
+                return [(sub(pd, u0, u1), E(("E2", "nE", "E1")[f], l), lv(n, l)) for l in ls if l < 15]
+            if nc < 8 and (job != "N" or nc):
+                m = less(16.0 if job == "N" else 1.0, nc)
+                head = head + ([(sub(pd, u0, u1), m, c(oth, u0, u1))] if job == "H" else [(sub(pd, a, a + 128), c(oth, a, a + 128), m) for a in range(u0, u1, 128)])
+            for l in range(nc, 8, 2):
+                mm(head + terms(Gn, [x + o for x in range(l, min(l + 2, 8)) for o in (0, 8)], 1), first=first, last=False, after=[c(pc)])
+                head, first = [], False
+            steps = []
+            per = 256 // wd
+            for l in range(0, nc, per):
+                steps.append((l / nc, "c", [x + o for x in range(l, min(l + per, nc)) for o in (0, 8)]))
+            for l in range(nc, 8):
+                steps.append(((l - nc + 0.5) / (8 - nc), "a", [l, l + 8]))
+            steps.sort()
+            for i, (_, path, ls) in enumerate(steps):
+                l = ls[0]
+                if path == "c":
+                    for q, x in enumerate(ls):
+                        so = c("P5", wd * q, wd * q + wd)
+                        mm([(so, c("nI"), c(oth, u0, u1)), (so, c("I"), lv(Gn, x))])
+                    md = c("MC", 16 * u0 + 2 * wd * l, 16 * u0 + 2 * wd * l + wd * len(ls))
+                    act(md, c("P5", 0, wd * len(ls)), F_.Abs)
+                    if job == "H":
+                        tm = [(sub(pd, u0, u1), E("E1", x), sub(md, wd * q, wd * q + wd)) for q, x in enumerate(ls)]
+                    else:
+                        tm = [(sub(pd, a + x, a + 128, 16), sub(md, wd * q + a - u0, wd * q + a - u0 + 128), c("GS", f0 + 16, f0 + 24)) for q, x in enumerate(ls) for a in range(u0, u1, 128)]
                 else:
-                    if not ls:
-                        mm([(o(l0 - 1, 0), c("CS", 0, 128), gs(8))], first=False, last=True)
-                        continue
-                    stage[0] += 1
-                    sb = "P5" if CFG["stage"] == 512 or stage[0] % 2 else "P6"
-                    for j, l in enumerate(ls):
-                        so = c(sb, wd * j, wd * j + wd)
-                        mm([(so, c("I"), gl(l)), (so, c("nI"), c(oth, u0, u0 + wd))])
-                    act(c(Mn, 16 * u0 + wd * l0, 16 * u0 + wd * (l0 + len(ls))), c(sb, 0, wd * len(ls)), F_.Abs)
-                    terms = [(o(l, a), ml(l, a, 128), gs(f0)) for l, a in parts]
-                acc[pd[1]] = [e for e in acc[pd[1]] if e[1] - e[0] == 256 or e[0] >= pd[3] or e[1] <= pd[2]]
-                ends.append(mm(tail + terms, first=False, last=(p == nh - 1 and l0 + per == 16)))
-                tail = []
-        ops[ends[-1]]["oth"].update(k for k in range(k0, ends[-1]) if ops[k]["out"] == pd[1] and "P" in ops[k]["alts"])
-        acc[pd[1]].append((pd[2], pd[3], True, ends[-1], 1))
+                    if l == 7 and job == "H":
+                        tt(lv(Mn, l), lv(Gn, l), c(pc, 2 * u0, 2 * u1, 2), A_.max)
+                    else:
+                        tt(c(Mn, 16 * u0 + l, 16 * u1, 8), c(Gn, 16 * u0 + l, 16 * u1, 8), c(pc, 2 * u0, 2 * u1), A_.max)
+                    tm = terms(Mn, ls, 0)
+                mm(head + tm, first=first, last=u1 == 256 and i == len(steps) - 1)
+                head, first = [], False
+
+    made = {}
+
+    def less(f, nc):
+        if (f, nc) not in made:
+            k = len(made)
+            made[f, nc] = c("MX", 128 * k, 128 * k + 128)
+            keep, tag[0] = tag[0], ""
+            ts(made[f, nc], c("BO"), -f, A_.mult)
+            for l in range(nc):
+                ms(sub(made[f, nc], l, 128, 8), 0.0)
+            tag[0] = keep
+        return made[f, nc]
 
     def turn(p, src, ident):
         return [(sub(p, 128 * h, 128 * h + 128), c(src, 128 * h, 128 * h + 128), c(ident)) for h in (0, 1)]
 
-    def lists(vu, vs):
-        mm(toW(pw(1), "GB", "RWU", 16))
-        if vu is not None:
-            cp(vu, pw(1))
-        mm([(pU, top("GR16", 16), top("RWU", 16))])
-        mm([(pB, top("GS16", 16), top("RWU", 16))])
-        cp(c(vs), pB, CFG["evac"])
+    def pick(p, e, src, k, rows=128):
+        mm([(p, top(e, rows, 3 - i, 131 - i), top(src, rows, i, 256, 4)) for i in range(4)])
+        scan(c("SC", 64 * k, 64 * k + 64), c("MQ"), p, A_.add, A_.min)
+        return c("SC", 64 * k + 3, 64 * k + 64, 4)
 
-    ts(top("Si", 16), top("VJi", 16), 255, A_.bitwise_and)
-    ts(top("Hi", 16), top("VJi", 16), 3840, A_.bitwise_and)
-    ts(top("PM", 16), top("Si", 16), top("C", 16, OD, OD + 1), A_.mult)
-    ts(top("SEL", 16), top("Hi", 16), top("C", 16, EV, EV + 1), A_.mult)
-    tt(top("RWU", 16), top("PM", 16), top("SEL", 16), A_.add)
-    lists(wu(V0), "VS0")
-    cp(wf(VF), pw(1))
-    jr = (T.RWS[32:40, :],) + c("RWS")[1:]
-    add({"V": ([lambda: g.vector.tensor_copy(jr[0], T.VJi[32:40, :])], vc(256))}, [c("VJi")], [jr])
-    ts(c("G16", 0, 144), c("COL", 0, 144), col(T8), A_.is_equal)
-    mm([(pw(2), (T.G16[32:40, 15 - i:143 - i],) + c("G16", 0, 128)[1:], (T.RWS[32:40, i:256:16],) + c("RWS", i, 256, 16)[1:]) for i in range(16)])
-    cp(c("ZO0", 256, 272), pw(2))
-    send(0)
+    def rows(b, rw):
+        mm([(top("P%d" % b, 8, 128 * h, 128 * h + 128), c("T16", 8 * h, 8 * h + 8), c("I")) for h in (0, 1)], each=True)
+        cp(top(rw, 8), top("P%d" % b, 8, 0, 256), EV)
+
+    def lists(vu, b):
+        ts(vu, pick(pu(0), "G4", "RW", 0, 8), col(QC), A_.add, 2048.0, A_.add)
+        mm([(hi(2), top("RG", 8), top("RW", 8))])
+        cp(c("RU%d" % b), hi(2), EV)
+
+    ts(top("RW", 8), top("VJi", 8), -2048.0, A_.add)
+    lists(wu(V0), 0)
+    ts(c("A0"), c("Ai"), -2048.0, A_.add)
     cp(c("Au"), c("Ai"))
-    cp(c("A0"), c("Ai"))
-    dedup(VF, wu(OV0))
+    cp(top("JR", 8), top("Hi", 8))
+    cp(c("ZO0", 256, 272), pick(pw(0), "G4", "JR", 2, 8), "V", col(QC))
+    send(0)
+    dedup("RU0", 0, "EB", wu(OV0))
 
     def users(t):
         a, b = (t - 1) % 2, t % 2
-        y, yn, Ao, An, vs = "Y%d" % a, "Y%d" % b, "A%d" % a, "A%d" % b, "VS%d" % b
+        y, yn, Ao, An, ru = "Y%d" % a, "Y%d" % b, "A%d" % a, "A%d" % b, "RU%d" % b
+        tag[0] = "g%d" % t
+        gather("R", "Au", t)
+        tag[0] = "n%d" % t
         gat(c("NBu"), c("NB"), wu(V0 + a), "V")
         gather("N", "NBu", t)
-        gather("R", "Au", t)
-        ts(c("NBf"), c("NBu"), col(KB), A_.add)
-        mm(turn(pD, "NBf", "If"), each=True)
-        head = [crow(pK, "KC")]
-        if "c" in CFG["pN"] and "d" in CFG["pN"]:
-            head += [(sub(pK, 128 * h, 128 * h + 128), c(y, 128 * h, 128 * h + 128), c("G16l", 0, 128)) for h in (0, 1)]
-        dist("N", y, pY, pK, head, 3, lambda l: l)
-        scan(c("PM"), c("RS"), pK, A_.add, A_.min)
-        tt(c("NE"), pK, c("PM"), A_.not_equal)
-        scan(c("SEL"), c("NE"), pD, A_.mult, A_.max)
-        rows(c("SEL", 15, 256, 16), 3840, 0, pB, "RWU")
-        lists(wu(V0 + b), vs)
-        cp(wf(VF), pw(1))
+        ts(c("NBc"), c("NBu"), -2048.0, A_.add)
+        dist("N", y, lo(2), [(c("P2"), top("ONE", 1, 0, 128), top("KK", 1))] + turn(hi(2), "NBc", "I"), t)
+        scan(c("PM"), c("RS"), lo(2), A_.add, A_.min)
+        tt(c("NE"), lo(2), c("PM"), A_.not_equal)
+        scan(c("SEL"), c("NE"), hi(2), A_.mult, A_.max)
+        ts(wf(T1), c("SEL", 15, 256, 16), MAGIC * 8192, A_.add, -MAGIC * 8192, A_.add)
+        tt(c("T16"), c("SEL", 15, 256, 16), wf(T1), A_.subtract)
+        rows(2, "RW")
+        lists(wu(V0 + b), b)
+        cp(c("V%d" % b), hi(2), EV)
         gat(c("XN"), X, wu(V0 + b))
-        dedup(VF, wu(OV0 + b))
-        mm([(pX, c("hI"), c("XN")), (pX, c("hI"), c(y)), const(pX, 0)])
-        ts(c("XW"), pX, MAGIC, A_.add, -MAGIC, A_.add)
+        tag[0] = "d%d" % t
+        dedup(ru, 0, "EB", wu(OV0 + b))
+        mm([(lo(2), c("fI"), c("XN")), (lo(2), c("fI"), c(y))])
+        ts(c("XW"), lo(2), MAGIC, A_.add, -MAGIC, A_.add)
+        tag[0] = "y%d" % t
+        mm([(hi(2), c("I"), c(y)), (hi(2), c("nI"), c("XN"))])
+        act(c(yn), hi(2), F_.Abs)
+        tag[0] = "m%d" % t
+        dist("R", "XN", lo(3), [(lo(3), top("ONE", 2, 0, 128), top("KR", 2))], t)
+        mm([const(lo(5), 3), const(hi(5), 3), (lo(5), c("I"), c(Ao)), (hi(5), top("RG", 8), top("RW", 8))], last=False)
+
+    def renew(t):
+        a, b = (t - 1) % 2, t % 2
+        Ao, An, ru = "A%d" % a, "A%d" % b, "RU%d" % b
+        tag[0] = "d%d" % t
         sca(c("X"), wu(OV0 + b), c("XW"))
-        mm([(pX, c("I"), c(y)), (pX, c("nI"), c("XN"))])
-        act(c(yn), pX, F_.Abs)
-        dist("R", "XN", pY, pR, [crow(pR, "KR0"), crow(pR, "KR1")] + turn(pR, "XN", "BR"), 0, lambda l: l)
-        act(c("NW"), pR, F_.Sign, bias=0.0 if t == 1 else col(THR), scale=-1.0)
-        mm([(pB, c("BO"), c(vs))] + turn(pB, "NW", "nI4"))
-        act(c("T2"), pB, F_.Identity, bias=col(N4))
-        mm([(pX, c("If"), c(Ao)), const(pX, 1)] + turn(pX, "NW", "I4"))
-        tt(c(An), pX, c("T2"), A_.max)
+        tag[0] = "r%d" % t
+        act(c("SR"), lo(3), F_.Sign, bias=0.0 if t == 1 else col(THR), scale=-1.0)
+        mm(turn(hi(5), "SR", "nI4") + turn(lo(5), "SR", "I4"), first=False)
+        cp(c("Pf"), hi(5), EV)
+        tt(c("AW"), c("Pf"), lo(5), A_.max)
         if t < RO:
-            cp(c("Au"), c(An))
+            cp(c(An), c("AW"), EV)
+            ts(c("Au"), c(An), 2048.0, A_.add)
+        tag[0] = "p%d" % t
         if t > 1:
-            mm([crow(pA, "KDR")] + turn(pA, Ao, "If"))
-            tt(wf(T4), c("NW", 0, 256, 16), wf(KS), A_.mult)
-            tt(sub(pA, 0, 256, 16), sub(pA, 0, 256, 16), wf(T4), A_.max)
-            scan(c("SEL"), c("NW"), pA, A_.mult, A_.max)
-            rows(c("SEL", 15, 256, 16), 7936, 0, pB, "RWU")
-            lists(None, "BS")
-            cp(wf(BF), pw(1))
-            dedup(BF, wu(OB))
-            sca(c("TR"), wu(OB), c("BS"))
-        sca(c("TR"), wu(OV0 + a), c(vs))
+            mm([(hi(3), top("ONE", 2, 0, 128), top("KD", 2))] + turn(hi(3), Ao, "I") + [(sub(hi(3), 0, 256, 16), c("I2"), c("SR", 0, 256, 16))])
+            scan(c("SEP"), c("SR"), hi(3), A_.mult, A_.max)
+            ts(wf(T2), c("SEP", 15, 256, 16), MAGIC * 16384, A_.add, -MAGIC * 16384, A_.add)
+            tt(wf(T3), c("SEP", 15, 256, 16), wf(T2), A_.subtract)
+            ts(c("T16"), wf(T3), 2048.0, A_.min)
+            rows(5, "RP")
+            pick(pu(1), "G4", "RP", 1, 8)
+            mm([(hi(5), top("RG", 8), top("RP", 8))])
+            cp(c("RB"), hi(5), EV)
+            dedup("RB", 1, "EC", wu(OB))
+            sca(c("TR"), wu(OB), c("RB"))
+        sca(c("TR"), wu(OV0 + a), c(ru))
 
     def seekers(t):
         b = t % 2
-        zi, zo, An, vs = "ZI%d" % t, "ZO%d" % t, "A%d" % b, "VS%d" % b
+        zi, zo = "ZI%d" % t, "ZO%d" % t
         z, j = c(zi, 0, 256), c(zi, 256, 272)
+        tag[0] = "h%d" % t
         cp(wu(JU), j)
-        for h in (0, 1):
-            mm([(sub(pw(2), 8 * h, 8 * h + 8), c(zi, 128 * h, 128 * h + 128), gs(k)) for k in (6, 7)])
-        rows(pw(2), 3840, 4, pE, "RWS")
-        mm([(pT, top("GR16", 16), top("RWS", 16)), const(pT, 2)])
-        mm(toW(pw(5), "GBl", "RWS", 16))
-        tt(wf(J1), pw(5), j, A_.subtract)
-        gat(c("Bf"), c(An), wu(JU))
-        gat(c("VJ"), c(vs), wu(JU))
-        mm(toW(pw(4), "E1", "VJ"))
-        cp(wf(VJW), pw(4))
-        mm([(pQ, c("I2f"), c("Bf")), const(pQ, 3)])
-        tt(c("Pf"), c("Bf"), pT, A_.mult)
-        tt(c("Si"), c("Pf"), pQ, A_.add)
+        mm([(hi(6), c("WH"), z), (hi(6), c("WL"), z)])
+        cp(c("Si"), hi(6))
+        ts(c("Ui"), c("Si"), 4095, A_.bitwise_and)
+        tag[0] = "j%d" % t
+        cp(wi(0), pick(pw(0), "EW", zi, 2))
+        ts(wi(1), wi(0), 255, A_.bitwise_and)
+        tt(wf(J1), wi(1), j, A_.subtract)
+        tag[0] = "h%d" % t
+        gat(c("Bc"), c("AW"), wu(JU))
+        gat(c("VJ"), c("V%d" % b), wu(JU))
+        mm([const(lo(7), 0), (lo(7), c("I"), c("Bc"))])
+        mm([const(lo(6), 1), (lo(6), c("I32"), c("Bc"))])
+        mm([(hi(6), c("I"), c("VJ"))])
+        tt(c("DUMR"), c("Ui"), lo(7), A_.mult)
+        tt(c("Si"), c("DUMR"), lo(6), A_.add)
         ts(c("Hi"), c("Si"), 5, A_.arith_shift_right, 4095, A_.bitwise_and)
         cp(c("Hu"), c("Hi"))
+        tag[0] = "H%d" % t
         gather("H", "Hu", t)
-        mm([crow(pE, "KDH")] + turn(pE, "Bf", "Jf"))
-        dist("H", zi, pZ, pH, [crow(pH, "KH0"), crow(pH, "KH1")] + turn(pH, zi, "BH"), 0, lambda l: 15 - l, 15)
-        act(c("NH"), pH, F_.Sign)
-        scan(c("SEH"), c("NH"), pE, A_.mult, A_.max)
-        rows(c("SEH", 15, 256, 16), 3840, 4, pQ, "RWS")
-        mm(toW(pw(3), "GB", "RWS", 16))
+        dist("H", zi, lo(6), [], t)
+        tag[0] = "c%d" % t
+        act(c("SH"), lo(6), F_.Sign, bias=col(THH), scale=-1.0)
+        mm([(lo(7), c("I"), c("Bc")), (lo(7), c("TH"), c("SH"))])
+        ts(c("ZH"), lo(7), col(CH), A_.add, 2048.0, A_.min)
+        ts(wu(PU), pick(pw(1), "E4", "ZH", 3), col(QC), A_.add, -28672.0, A_.add)
         for k in range(3):
-            cp(wu(PU0), pw(3))
-            gat(c("PS"), c("TR", 0, 4096), wu(PU0))
-            mm(toW(pw(3), "E1", "PS"))
-        cp(wu(PU0), pw(3))
-        gat(c("XP"), X, wu(PU0))
-        tt(wf(FW), pw(3), wf(VJW), A_.is_equal)
+            gat(c("PS"), c("TR", 0, 4096), wu(PU))
+            ts(wu(PU), pick(pw(1), "S4", "PS", 3), col(QC), A_.add, 2048.0, A_.add)
+        gat(c("XP"), X, wu(PU))
+        tt(c("FD"), c("PS"), hi(6), A_.is_equal)
+        mm([(lo(6), c("I"), z), (hi(6), c("nI"), z), (lo(6), c("nKI"), c("FD")), (hi(6), c("nKI"), c("FD"))], last=False)
+        fw = sub(pw(2), 0, 16)
+        mm(toW(fw, "Es", "FD"))
+        mm([(lo(7), c("fI"), z), (lo(7), c("KI"), c("FD")), (lo(7), c("fI"), c("XP"))])
+        mm([(lo(6), c("nI"), c("XP")), (hi(6), c("I"), c("XP"))], first=False)
         if t < RO:
-            add({"V": ([lambda: g.vector.tensor_reduce(T.C[:, FS:FS + 1], wf(FW)[0], AxisListType.X, A_.add)], vc(16))}, [wf(FW)], [col(FS)])
-            pf = sub(pw(6), 0, 1)
-            mm([(pf, c("ONf"), col(FS))])
-            cp(ci(5), pf)
-            ts(ci(6), ci(5), 15, A_.bitwise_and)
-            ts(col(THR), ci(6), 16.0, A_.mult)
-        tt(wf(J2), wf(J1), wf(FW), A_.mult)
+            add({"V": ([lambda: g.vector.tensor_reduce(T.C[:, FS:FS + 1], fw[0], AxisListType.X, A_.add)], vc(16))}, [fw], [col(FS)])
+            pf = sub(pw(3), 0, 1)
+            mm([const(pf, 2, 1), (pf, c("O16"), col(FS))])
+            ts(col(FR), pf, MAGIC * 256, A_.add, -MAGIC * 256, A_.add)
+            ts(col(THR), pf, col(FR), A_.subtract, 120.0, A_.add)
+        tt(wf(J2), wf(J1), fw, A_.mult)
         tt(c(zo, 256, 272), wf(J2), j, A_.add)
-        mm([(pS, c("BO"), c("PS")), (pS, c("nBO"), c("VJ"))])
-        act(c("AB"), pS, F_.Abs)
-        mm([(pT, c("I4"), c("AB"))])
-        mm([(pE, c("I"), z), (pE, c("nI"), c("XP"))])
-        act(c("AD"), pE, F_.Abs)
-        mm([(pS, c("hI"), z), (pS, c("nI4"), c("AB")), const(pS, 0), (pS, c("hI"), c("XP"))])
-        ts(c("HS"), pS, MAGIC, A_.add, -MAGIC, A_.add)
-        tt(pT, c("AD"), pT, A_.min)
-        tt(c(zo, 0, 256), c("HS"), pT, A_.max)
+        ts(c("HS"), lo(7), MAGIC - 1024.0, A_.add, -MAGIC, A_.add)
+        tt(c("M1"), c("HS"), lo(6), A_.max)
+        tt(c(zo, 0, 256), c("M1"), hi(6), A_.max)
         if t < RO:
             send(t)
 
-    if "c" in CFG["pN"] and "d" in CFG["pN"]:
-        ts(c("G16l", 0, 128), c("nBO"), 16.0, A_.mult)
-        for l in range(16):
-            if CFG["pN"][l // 4] == "d":
-                ms(c("G16l", l, 128, 16), 0.0)
     users(1)
+    renew(1)
     for t in range(1, RO + 1):
-        seekers(t)
         if t < RO:
             users(t + 1)
+        seekers(t)
+        if t < RO:
+            renew(t + 1)
+        tag[0] = ""
         if t == RO - 1:
-            dma("Y", T.ya[:], T.A0[:], [c("A0")], [], 131072)
+            cp(c("OUT", 512, 768), c("AW"), "VS", col(P2K))
+            dma("Y", T.ya[:], T.OUT[:, 512:768], [c("OUT", 512, 768)], [], 131072)
             dma("Y", T.yy[:], T.Y0[:], [c("Y0")], [], 65536)
-            o = top("P3", 8, 0, 256)
-            mm([(o, gs(0), c("VS0"))])
-            cp(top("OUT", 8, 0, 256), o, "VS")
+            cp(top("OUT", 8, 0, 256), top("RW", 8), "VS", top("C", 8, P2K, P2K + 1))
             dma("Y", T.yv[:], T.OUT[0:8, 0:256], [c("OUT", 0, 256)], [], 8192)
-            dma("G", T.yt[:], T.TR[0:128:16, 0:4096], [c("TR")], [c("DUMR")], 131072)
-            dma("G", T.yt[:], T.TR[1:128:16, 0:4096], [c("TR"), c("DUMR")], [], 131072, accum_op=A_.add, max_dma_last_dim=4096)
+            dma("G", T.yt[:], T.TR[0:128:16, 0:4096], [c("TR")], [c("JR")], 131072)
+            dma("G", T.yt[:], T.C2K[:], [c("C2K"), c("JR")], [], 131072, accum_op=A_.add)
     dma("Y", T.yz[:], T.ZO4[:, 0:256], [c("ZO4", 0, 256)], [], 65536)
     mm([(top("P3", 8, 256 + i, 512, 16), c("I", i, 128, 16), c("ZO4", 256, 272)) for i in range(16)], each=True)
-    cp(top("OUT", 8, 256, 512), top("P3", 8, 256, 512), "V")
-    dma("S", T.yj[:], T.OUT[0:8, 256:512], [c("OUT", 256, 512)], [], 8192)
+    cp(top("OUT", 8, 256, 512), top("P3", 8, 256, 512), "VS")
+    dma("Y", T.yj[:], T.OUT[0:8, 256:512], [c("OUT", 256, 512)], [], 8192)
     return ops, Q, ndma[0]
 
 
-def schedule(ops):
-    LAT, SLACK = PL["LAT"], PL["SLACK"]
-    n = len(ops)
+def plan(ops):
+    n, LAT = len(ops), PL["LAT"]
+    pred = [sorted(o["raw"] | o["oth"] | o["soft"]) for o in ops]
     succ = [[] for _ in range(n)]
-    for k, o in enumerate(ops):
-        for d in o["raw"] | o["oth"]:
+    for k in range(n):
+        for d in pred[k]:
             succ[d].append(k)
-    bl = [0.0] * n
+
+    def place(urge, back, eng):
+        eng, at = list(eng), [0.0] * n
+        dur = lambda k: ops[k]["alts"][eng[k]][1]
+        before, after = (succ, pred) if back else (pred, succ)
+        left = [len(x) for x in before]
+        ready = [k for k in range(n) if not left[k]]
+        use = {}
+        while ready:
+            k = max(ready, key=lambda k: urge[k])
+            ready.remove(k)
+            o, best = ops[k], None
+            for e in [o.get("pref") or ("S" if "S" in o["alts"] else list(o["alts"])[0])]:
+                d, t = o["alts"][e][1], 0.0
+                for x in before[k]:
+                    p, s = (k, x) if back else (x, k)
+                    free = eng[x] == e == "P"
+                    t = max(t, at[x] + dur(x) + (0.0 if free or p in ops[s]["soft"] else LAT + ops[p]["lat"]))
+                if back and not before[k]:
+                    t = o["lat"]
+                spans = sorted([u[:2] for u in use.get(e, [])] + [(u[0] - LAT, u[1] + LAT) for b in o["banks"] for u in use.get(b, []) if u[2] != e])
+                for a, b in spans:
+                    if b > t:
+                        if a >= t + d:
+                            break
+                        t = b
+                if best is None or t + d < best[0]:
+                    best = (t + d, t, e)
+            at[k], eng[k] = best[1], best[2]
+            for r in [eng[k]] + list(o["banks"]):
+                use.setdefault(r, []).append((at[k], best[0], eng[k]))
+            for x in after[k]:
+                left[x] -= 1
+                if not left[x]:
+                    ready.append(x)
+        return at, eng, [at[k] + dur(k) + (0.0 if back else ops[k]["lat"]) for k in range(n)]
+
+    urge, x = [0.0] * n, PL["SEED"]
     for k in range(n - 1, -1, -1):
-        o = ops[k]
-        bl[k] = min(a[1] for a in o["alts"].values()) + o["lat"] + max([bl[s] + LAT for s in succ[k]] + [0.0])
-    x = PL["SEED"]
-    pr = list(bl)
-    if x:
+        urge[k] = min(a[1] for a in ops[k]["alts"].values()) + ops[k]["lat"] + max([urge[s] + LAT for s in succ[k]] + [0.0])
+    for k in range(n):
+        urge[k] += PL["LEAD"].get(ops[k]["tag"], PL["LEAD"].get(ops[k]["tag"][:1], 0.0))
+    best = None
+    for _ in range(PL["PASSES"]):
         for k in range(n):
             x = (x * 1103515245 + 12345) % 2147483648
-            pr[k] += PL["NOISE"] * x / 2147483648.0
-    seq = []
-    left = [len(o["raw"] | o["oth"]) for o in ops]
-    ready = [k for k in range(n) if left[k] == 0]
-    free = dict((e, 0.0) for e in "VSPGY")
-    end, eng, rt = [0.0] * n, [None] * n, [0.0] * n
-    last, lock = {}, {}
-    order = dict((e, []) for e in "VSPGY")
-    busy = dict((e, 0.0) for e in "VSPGY")
-    while ready:
-        best = None
-        for e in "PVSGY":
-            cand = []
-            for k in ready:
-                o = ops[k]
-                if e not in o["alts"] or (o["starts"] and lock.get(o["starts"])):
-                    continue
-                r = rt[k]
-                for b in o["banks"]:
-                    if b in last and eng[last[b]] != e:
-                        r = max(r, end[last[b]] + LAT)
-                cand.append((max(r, free[e]), k))
-            if not cand:
+            urge[k] += PL["NOISE"] * x / 2147483648.0
+        at, eng, end = place(urge, False, [None] * n)
+        if best is None or max(end) < best[0]:
+            best = (max(end), at, eng)
+        urge = place(end, True, eng)[2]
+    return best
+
+
+def polish(sets, seq, eng):
+    ops = sets[0][0]
+    n, eng = len(ops), list(eng)
+    pred = [o["raw"] | o["oth"] | o["soft"] for o in ops]
+    hard = [[d for d in o["raw"] | o["oth"] if not (eng[k] == "P" and eng[d] == "P")] for k, o in enumerate(ops)]
+    succ = [set() for _ in range(n)]
+    for k in range(n):
+        for d in pred[k]:
+            succ[d].add(k)
+    banks = [sorted(o["banks"]) for o in ops]
+    durs = [[o["alts"][eng[k]][1] for k, o in enumerate(m[0])] for m in sets]
+    lats = [[o["lat"] for o in m[0]] for m in sets]
+    x = [PL["SEED"]]
+
+    def rnd(m):
+        x[0] = (x[0] * 1103515245 + 12345) % 2147483648
+        return (x[0] >> 8) % m
+
+    def run(seq, a, old):
+        prev0, last0 = {}, {}
+        for k in seq[:a]:
+            prev0[eng[k]] = k
+            for b in banks[k]:
+                last0[b] = k
+        res, tot = [], 0.0
+        for i, m in enumerate(sets):
+            dur, lat, LAT = durs[i], lats[i], m[1]
+            end, why = (list(old[i][0]), list(old[i][1])) if old else ([0.0] * n, [None] * n)
+            prev, last = dict(prev0), dict(last0)
+            for k in seq[a:]:
+                e = eng[k]
+                w = prev.get(e)
+                t = 0.0 if w is None else end[w] - lat[w] - LAT
+                for d in hard[k]:
+                    if end[d] > t:
+                        t, w = end[d], d
+                for b in banks[k]:
+                    d = last.get(b)
+                    if d is not None and end[d] > t and eng[d] != e:
+                        t, w = end[d], d
+                    last[b] = k
+                prev[e], end[k], why[k] = k, t + dur[k] + lat[k] + LAT, w
+            res.append((end, why))
+            tot += (max(end) + PL["MEAN"] * sum(end) / n) * m[2]
+        return tot, res
+
+    cur, r = run(seq, 0, None)
+    best = (cur, seq, list(eng))
+    for it in range(PL["STEPS"]):
+        end, why = r[rnd(len(r))]
+        k = end.index(max(end)) if rnd(5) < 3 else rnd(n)
+        pairs = []
+        while why[k] is not None:
+            if why[k] not in pred[k]:
+                pairs.append((why[k], k))
+            k = why[k]
+        if not pairs:
+            continue
+        j, k = pairs[rnd(len(pairs))]
+        a, b, how, more, flip = seq.index(j), seq.index(k), rnd(20), (0, 0, 0, 3, 10, 30)[rnd(6)], None
+        if how < 3:
+            flip = (j, k)[rnd(2)]
+            if len(ops[flip]["alts"]) < 2:
                 continue
-            t0 = min(x[0] for x in cand)
-            s, k = max((x for x in cand if x[0] <= t0 + SLACK), key=lambda x: pr[x[1]])
-            if best is None or t0 < best[0]:
-                best = (t0, s, k, e)
-        t0, s, k, e = best
+            new = seq
+        else:
+            up = how < 12
+            a, b = (max(0, a - more), b) if up else (a, min(n - 1, b + more))
+            mv = set([k if up else j])
+            for y in (reversed(seq[a:b]) if up else seq[a + 1:b + 1]):
+                if not mv.isdisjoint(succ[y] if up else pred[y]):
+                    mv.add(y)
+            if j in mv and k in mv:
+                continue
+            mid = seq[a:b + 1]
+            new = seq[:a] + [y for y in mid if (y in mv) == up] + [y for y in mid if (y in mv) != up] + seq[b + 1:]
+        for turn in (0, 1):
+            if flip is not None:
+                eng[flip] = "S" if eng[flip] == "V" else "V"
+                for i, m in enumerate(sets):
+                    durs[i][flip] = m[0][flip]["alts"][eng[flip]][1]
+            if turn == 0:
+                v, r2 = run(new, a, r)
+                if v <= cur - PL["TEMP"] * (1 - it / PL["STEPS"]) * math.log((rnd(1000) + 1) / 1000.0):
+                    seq, cur, r = new, v, r2
+                    if v < best[0]:
+                        best = (v, seq, list(eng))
+                    break
+    return best
+
+
+PLAN = []
+
+
+def schedule(ops, sets=None):
+    if not PLAN:
+        span, at, eng = plan(ops)
+        PLAN.append(polish(sets, sorted(range(len(ops)), key=lambda k: (at[k], k)), eng))
+    span, seq, eng = PLAN[0]
+    order, last = dict((e, []) for e in "VSPGY"), {}
+    for i, k in enumerate(seq):
         o = ops[k]
-        o["dyn"] = set(last[b] for b in o["banks"] if b in last and eng[last[b]] != e)
-        eng[k] = e
-        free[e] = s + o["alts"][e][1]
-        busy[e] += o["alts"][e][1]
-        end[k] = free[e] + o["lat"]
-        o["t"] = s
+        o["t"] = i
+        o["dyn"] = set(last[b] for b in o["banks"] if b in last and eng[last[b]] != eng[k])
         for b in o["banks"]:
             last[b] = k
-        if o["opens"]:
-            lock[o["opens"]] = True
-        if o["closes"]:
-            lock[o["closes"]] = False
-        order[e].append(k)
-        seq.append(k)
-        ready.remove(k)
-        for s2 in succ[k]:
-            wait = e != "P" or "P" not in ops[s2]["alts"]
-            rt[s2] = max(rt[s2], end[k] + LAT if wait else s)
-            left[s2] -= 1
-            if left[s2] == 0:
-                ready.append(s2)
-    assert sum(len(v) for v in order.values()) == n
-    return order, eng, max(end), busy, seq
+        order[eng[k]].append(k)
+    return order, eng, seq
 
 
 def rank_program(g, core, T, topo):
@@ -610,8 +744,13 @@ def rank_program(g, core, T, topo):
     rid, pid, _ = topo.addr(nxt)
     mask = topo.mask(core, nxt)
     neng = len(topo.engines(core, nxt))
+    sets = []
+    for m in ([] if PLAN else SETS):
+        PL.update(m)
+        sets.append((build(g, T, (rid, pid, mask))[0], PL["LAT"], PL["W"]))
+    PL.update(SETS[0])
     ops, Q, nd = build(g, T, (rid, pid, mask))
-    order, eng, _, _, seq = schedule(ops)
+    order, eng, seq = schedule(ops, sets)
     tick = {}
     for e, L in order.items():
         m = 0

@@ -12,6 +12,7 @@ CFG = {
     "gN": ["SVSVSVSV"] + ["S" * 8] * 3, "gR": ["S" * 8] * 4, "gH": ["S" * 8] * 3 + ["SVSSVSSV"],
     "hN": [(0, 128, 256)] * 4, "hR": [(0, 128, 256)] * 4, "hH": [(0, 128, 256)] * 4,
     "cN": [(0, 0)] * 4, "cR": [(0, 0)] * 4, "cH": [(0, 0)] * 4,
+    "lag": [(8, 0)] * 3, "pool": 2, "early": 1,
     "small": "VS", "evac": "VS",
 }
 
@@ -37,7 +38,7 @@ _sb("ZO0 ZO1 ZO2 ZO3 ZO4 ZI1 ZI2 ZI3 ZI4", [128, 272], "bfloat16")
 _sb("E1 E2 nE Es EW E4 S4 G4", [128, 144], "bfloat16")
 _sb("CQ", [128, 144], "float32")
 _sb("MQ", [128, 64], "float32")
-_sb("I nI I4 nI4 I2 I32 KI nKI BO nBO BO8 WH WL TH RG", [128, 128], "bfloat16")
+_sb("I nI I4 nI4 I2 I32 KI nKI BO nBO BO8 WH WL TH RG K8", [128, 128], "bfloat16")
 _sb("fI", [128, 128], "float16")
 _sb("T16", [128, 16], "float16")
 _sb("O16", [128, 128], "float32")
@@ -56,10 +57,9 @@ SCRATCH = S
 NDMA = 18
 SEMAPHORES = ["V", "S", "P", "G"] + ["d%d" % k for k in range(NDMA)] + ["arr%d" % k for k in range(1, 5)] + ["sent%d" % k for k in range(4)]
 
-SETS = [dict(CY=.85, PCY=.43, GA=1.56, SC=3.8, LAT=100., OVH=10., MM=3., BW=250., SEND=2000., W=0.5),
-        dict(CY=1.0, PCY=.55, GA=1.3, SC=2.8, LAT=150., OVH=25., MM=8., BW=350., SEND=1500., W=0.4)]
-PL = {"SEED": 1, "NOISE": 0.0, "PASSES": 2, "STEPS": 40000, "TEMP": 80.0, "MEAN": 0.3,
-      "LEAD": {"g": -5000.0, "m": -5000.0, "y": 20000.0, "r": -3000.0}}
+SETS = [dict(CY=.85, PCY=.45, GA=1.4, SC=3.0, LAT=240., OVH=10., MM=3., BW=400., SEND=3000., W=1.0)]
+PL = {"SEED": 4, "NOISE": 0.0, "PASSES": 2, "STEPS": 70000, "TEMP": 150.0, "MEAN": 0.3,
+      "LEAD": {"y": 20000.0, "n": 8000.0, "d": 12000.0}}
 
 
 def build(g, T, dest):
@@ -67,8 +67,8 @@ def build(g, T, dest):
     ops = []
     acc = {}
     ndma = [0]
-    tail = {}
-    tag = [""]
+    tail, mark = {}, {}
+    tag = ["0"]
     Q = {"V": g.vector, "S": g.scalar, "P": g.tensor, "G": g, "Y": g.sync}
 
     def top(name, rows, a=None, b=None, s=None):
@@ -137,6 +137,15 @@ def build(g, T, dest):
             alts["S"] = ([f], vc(out[4]))
         return add(alts, [a] + cols(bias), [out])
 
+    def mul(out, a, v):
+        return add({"V": ([lambda: g.vector.tensor_scalar(out[0], a[0], sv(v), None, A_.mult)], vc(out[4] * 0.5)),
+                    "S": ([lambda: g.scalar.activation(out[0], a[0], F_.Copy, scale=sv(v))], vc(out[4]))}, [a] + cols(v), [out], pref="SV"[len(ops) % 2])
+
+    def gcp(out, a):
+        if not CFG["pool"]:
+            return cp(out, a, CFG["evac"])
+        return gp(lambda: g.affine_select(out[0], a[0], [[0, out[4]]], A_.is_equal, 0.0, 0, 0), out[4], [a], [out])
+
     def ms(out, v):
         return add({"V": ([lambda: g.vector.memset(out[0], v)], vc(out[4] * (0.5 if out[5] else 1.0)))}, [], [out])
 
@@ -169,7 +178,7 @@ def build(g, T, dest):
             rd += [l, r]
             wr.append(o)
         bank = terms[0][0][1]
-        k = add({"P": (fs, cost)}, rd, wr)
+        k = add({"P": (fs, cost)}, rd, wr, banks=set(o[1] for o in wr))
         st = tail.setdefault(bank, {"end": [], "since": [], "outs": set()})
         ops[k]["soft"].update(st["end"])
         if first and last:
@@ -227,8 +236,8 @@ def build(g, T, dest):
           dma("Y", T.Hi[0:8, :], T.j0[:], [], [c("Hi")], 8192, True),
           dma("Y", T.Ci[:, 8:9], T.w[:], [], [c("Ci", 8, 12)], 512, True),
           dma("Y", T.ZO0[:, 0:256], T.z0[:], [], [c("ZO0", 0, 256)], 65536, True),
-          dma("Y", T.Y0[:], T.y0[:], [], [c("Y0")], 65536, True),
-          dma("Y", T.NB[:], T.nb[:], [], [c("NB")], 2 << 20, True)]
+          dma("Y", T.NB[:], T.nb[:], [], [c("NB")], 2 << 20, True),
+          dma("Y", T.Y0[:], T.y0[:], [], [c("Y0")], 65536, True)]
     for k in ld[1:]:
         ops[k]["soft"].add(k - 1)
     small = dict(allow_small_or_imprecise_dtypes=True)
@@ -238,6 +247,7 @@ def build(g, T, dest):
     gp(lambda: g.iota(T.KC[:], [[0, 16], [1, 16]], 0, 0, **small), 256, [], [c("KC")])
     gp(lambda: g.iota(T.KK[0:1, 0:256], [[0, 16], [1, 16]], 0, 0, **small), 256, [], [c("KK", 0, 256)])
     gp(lambda: g.iota(T.KK[0:1, 256:512], [[0, 16], [-8192, 16]], 131072, 0, **small), 256, [], [c("KK", 256, 512)])
+    gp(lambda: g.iota(T.K8[:], [[0, 16], [1, 8]], 0, 0, **small), 128, [], [c("K8")])
     gp(lambda: g.iota(T.TR[:], [[1, WN]], -2048, 0, **small), WN, [], [c("TR")])
     P_, L_, G_, T15, Q4, L0, W8, WH_, WL_, FS, FR, THR, QC, THH, CH, P2K, K0, K1, K2, K3, K4, K5 = range(22)
     LT = 24
@@ -277,16 +287,16 @@ def build(g, T, dest):
         ms(top("CL", 1, 128 * k, 128 * k + 128), v)
     ts(top("G4", 8), top("CQ", 8), top("C", 8, P_, P_ + 1), A_.is_equal)
     ts(top("RG", 8), top("COLG", 8, 0, 128), top("C", 8, P_, P_ + 1), A_.is_equal)
-    for n, v in (("E4", 1.0), ("S4", col(L0))):
-        ts(c(n), c("CQ"), col(G_), A_.is_equal, v, A_.mult)
-    for n, v in (("E1", 1.0), ("E2", 2.0), ("nE", -1.0), ("Es", col(L0))):
-        ts(c(n), c("COL", 0, 144), col(T15), A_.is_equal, v, A_.mult)
-    for n, v in (("I", 1.0), ("nI", -1.0), ("I4", 4096.0), ("nI4", -4096.0), ("I2", 2048.0), ("I32", 32.0), ("KI", 1024.0), ("nKI", -1024.0), ("fI", 2047.0 / 4096.0)):
-        ts(c(n), c("COL", 0, 128), col(P_), A_.is_equal, v, A_.mult)
-    for n, v in (("BO", 1.0), ("BO8", 8192.0)):
-        ts(c(n), c("COLG", 0, 128), col(G_), A_.is_equal, v, A_.mult)
-    for k, v in enumerate((32.0, -16.0, 16.0, 2.0, -1.0, 1.0)):
-        ts(c("GS", 8 * k, 8 * k + 8), c("COL", 0, 8), col(G_), A_.is_equal, v, A_.mult)
+    ts(c("E4"), c("CQ"), col(G_), A_.is_equal)
+    ts(c("E1"), c("COL", 0, 144), col(T15), A_.is_equal)
+    ts(c("I"), c("COL", 0, 128), col(P_), A_.is_equal)
+    ts(c("BO"), c("COLG", 0, 128), col(G_), A_.is_equal)
+    ts(c("GS", 40, 48), c("COL", 0, 8), col(G_), A_.is_equal)
+    for n, m, v in (("S4", "E4", col(L0)), ("E2", "E1", 2.0), ("nE", "E1", -1.0), ("Es", "E1", col(L0)), ("nI", "I", -1.0), ("I4", "I", 4096.0), ("nI4", "I", -4096.0),
+                    ("I2", "I", 2048.0), ("I32", "I", 32.0), ("KI", "I", 1024.0), ("nKI", "I", -1024.0), ("fI", "I", 2047.0 / 4096.0), ("BO8", "BO", 8192.0)):
+        mul(c(n), c(m), v)
+    for k, v in enumerate((32.0, -16.0, 16.0, 2.0, -1.0)):
+        mul(c("GS", 8 * k, 8 * k + 8), c("GS", 40, 48), v)
     ms(c("X", 4096, WN), 0.0)
     ts(c("RS"), c("KC"), 0.0, A_.is_equal, 1000000.0, A_.mult)
     ts(c("PM"), c("KC"), col(L_), A_.is_equal)
@@ -298,15 +308,15 @@ def build(g, T, dest):
     tt(c("TH"), c("Pf", 0, 128), c("nI4"), A_.add)
     ts(c("C", LT, LT + 16), c("COL", 0, 16), col(L_), A_.is_gt)
     for i in range(1, 16):
-        ts(c("TD", 128 * i, 128 * i + 128), c("BO8"), col(LT + i), A_.mult)
+        mul(c("TD", 128 * i, 128 * i + 128), c("BO8"), col(LT + i))
     ts(ci(4), ci(8), 63, A_.bitwise_and)
     ts(ci(5), ci(8), 255, A_.bitwise_and)
     cp(col(WL_), ci(4))
     cp(col(W8), ci(5))
     tt(col(WH_), ci(8), col(WL_), A_.subtract)
-    ts(c("WH"), c("BO"), col(WH_), A_.mult)
-    ts(c("WL"), c("BO"), col(WL_), A_.mult)
-    ts(c("EW"), c("E4"), col(W8), A_.mult)
+    mul(c("WH"), c("BO"), col(WH_))
+    mul(c("WL"), c("BO"), col(WL_))
+    mul(c("EW"), c("E4"), col(W8))
 
     lo = lambda b: c("P%d" % b, 0, 256)
     hi = lambda b: c("P%d" % b, 256, 512)
@@ -324,9 +334,14 @@ def build(g, T, dest):
 
     def dedup(ru, key, eb, off):
         p = lo(4)
-        for k in range(16):
-            ts(c(eb, 256 * k, 256 * k + 256 - 16 * k), c(ru, 16 * k, 256), col(QC), A_.subtract,
-               c("SC", 64 * key + 4 * k + 3, 64 * key + 4 * k + 4), A_.is_equal)
+        for k0, k1 in ((0, 2), (2, 4), (4, 6), (6, 9), (9, 12), (12, 16)):
+            fs, wr, cost = [], [], 0.0
+            for k in range(k0, k1):
+                o = c(eb, 256 * k, 256 * k + 256 - 16 * k)
+                fs.append(lambda o=o, k=k: g.vector.tensor_scalar(o[0], T[ru][:, 16 * k:256], T.C[:, QC:QC + 1], T.SC[:, 64 * key + 4 * k + 3:64 * key + 4 * k + 4], A_.subtract, A_.is_equal))
+                wr.append(o)
+                cost += vc(o[4] * 0.5)
+            add({"V": (fs, cost)}, [c(ru), col(QC), c("SC", 64 * key, 64 * key + 64)], wr)
         blk = lambda k: (sub(p, 16 * k + 16, 256), c("BO8"), c(eb, 256 * k + 16, 256 * k + 256 - 16 * k))
         mm([(p, c("I"), c("MB")), (p, c("I"), c(ru))] + [blk(k) for k in range(4)], last=False)
         mm([blk(k) for k in range(4, 9)], first=False, last=False)
@@ -339,11 +354,15 @@ def build(g, T, dest):
         en = CFG["g" + job][t - 1]
         w = 256 // len(en)
         for h, e in enumerate(en):
-            ops[gat(c("G" + job, 16 * w * h, 16 * w * (h + 1)), X, c(lst, w * h, w * (h + 1)))]["pref"] = e
+            k = gat(c("G" + job, 16 * w * h, 16 * w * (h + 1)), X, c(lst, w * h, w * (h + 1)))
+            ops[k]["pref"] = e
+            mark[job, t, h] = k
+            if job == "H" and t < RO and h == CFG["lag"][t - 1][1]:
+                ops[k]["soft"].update(mark["N", t + 1, x] for x in range(CFG["lag"][t - 1][0]))
 
     def dist(job, oth, pd, head, t):
         Gn, Mn, cuts = "G" + job, "M" + job, CFG["h" + job][t - 1]
-        pc = "P0" if job == "H" else "P1"
+        pc, ps = "P0" if job == "H" else "P1", "P0" if job == "N" else "P5"
         f0 = 0 if job == "N" else 24
         mm([(c(pc, r, 512, 2), c("I"), c(oth, 0, 256)) for r in (0, 1)], each=True)
         first = True
@@ -356,7 +375,7 @@ def build(g, T, dest):
                     return [(sub(pd, a + l, a + 128, 16), lv(n, l, a, a + 128), c("GS", f0 + 8 * f, f0 + 8 * f + 8)) for l in ls for a in range(u0, u1, 128)]
                 return [(sub(pd, u0, u1), E(("E2", "nE", "E1")[f], l), lv(n, l)) for l in ls if l < 15]
             if nc < 8 and (job != "N" or nc):
-                m = less(16.0 if job == "N" else 1.0, nc)
+                m = made[16.0 if job == "N" else 1.0, nc]
                 head = head + ([(sub(pd, u0, u1), m, c(oth, u0, u1))] if job == "H" else [(sub(pd, a, a + 128), c(oth, a, a + 128), m) for a in range(u0, u1, 128)])
             for l in range(nc, 8, 2):
                 mm(head + terms(Gn, [x + o for x in range(l, min(l + 2, 8)) for o in (0, 8)], 1), first=first, last=False, after=[c(pc)])
@@ -372,10 +391,10 @@ def build(g, T, dest):
                 l = ls[0]
                 if path == "c":
                     for q, x in enumerate(ls):
-                        so = c("P5", wd * q, wd * q + wd)
+                        so = c(ps, wd * q, wd * q + wd)
                         mm([(so, c("nI"), c(oth, u0, u1)), (so, c("I"), lv(Gn, x))])
                     md = c("MC", 16 * u0 + 2 * wd * l, 16 * u0 + 2 * wd * l + wd * len(ls))
-                    act(md, c("P5", 0, wd * len(ls)), F_.Abs)
+                    act(md, c(ps, 0, wd * len(ls)), F_.Abs)
                     if job == "H":
                         tm = [(sub(pd, u0, u1), E("E1", x), sub(md, wd * q, wd * q + wd)) for q, x in enumerate(ls)]
                     else:
@@ -390,17 +409,10 @@ def build(g, T, dest):
                 head, first = [], False
 
     made = {}
-
-    def less(f, nc):
-        if (f, nc) not in made:
-            k = len(made)
-            made[f, nc] = c("MX", 128 * k, 128 * k + 128)
-            keep, tag[0] = tag[0], ""
-            ts(made[f, nc], c("BO"), -f, A_.mult)
-            for l in range(nc):
-                ms(sub(made[f, nc], l, 128, 8), 0.0)
-            tag[0] = keep
-        return made[f, nc]
+    for f, nc in sorted(set((16.0 if job == "N" else 1.0, nc) for job in "NRH" for x in CFG["c" + job] for nc in x if nc < 8 and (job != "N" or nc))):
+        made[f, nc] = c("MX", 128 * len(made), 128 * len(made) + 128)
+        ts(c("Pf", 0, 128), c("K8"), float(nc), A_.is_ge, -f, A_.mult)
+        tt(made[f, nc], c("Pf", 0, 128), c("BO"), A_.mult)
 
     def turn(p, src, ident):
         return [(sub(p, 128 * h, 128 * h + 128), c(src, 128 * h, 128 * h + 128), c(ident)) for h in (0, 1)]
@@ -434,7 +446,9 @@ def build(g, T, dest):
         tag[0] = "g%d" % t
         gather("R", "Au", t)
         tag[0] = "n%d" % t
-        gat(c("NBu"), c("NB"), wu(V0 + a), "V")
+        k = gat(c("NBu"), c("NB"), wu(V0 + a), "V")
+        if t == 1:
+            mark["first"] = k
         gather("N", "NBu", t)
         ts(c("NBc"), c("NBu"), -2048.0, A_.add)
         dist("N", y, lo(2), [(c("P2"), top("ONE", 1, 0, 128), top("KK", 1))] + turn(hi(2), "NBc", "I"), t)
@@ -445,7 +459,7 @@ def build(g, T, dest):
         tt(c("T16"), c("SEL", 15, 256, 16), wf(T1), A_.subtract)
         rows(2, "RW")
         lists(wu(V0 + b), b)
-        cp(c("V%d" % b), hi(2), EV)
+        gcp(c("V%d" % b), c(ru))
         gat(c("XN"), X, wu(V0 + b))
         tag[0] = "d%d" % t
         dedup(ru, 0, "EB", wu(OV0 + b))
@@ -469,7 +483,7 @@ def build(g, T, dest):
         cp(c("Pf"), hi(5), EV)
         tt(c("AW"), c("Pf"), lo(5), A_.max)
         if t < RO:
-            cp(c(An), c("AW"), EV)
+            (gcp if CFG["pool"] > 1 else lambda o, a: cp(o, a, EV))(c(An), c("AW"))
             ts(c("Au"), c(An), 2048.0, A_.add)
         tag[0] = "p%d" % t
         if t > 1:
@@ -562,6 +576,7 @@ def build(g, T, dest):
     mm([(top("P3", 8, 256 + i, 512, 16), c("I", i, 128, 16), c("ZO4", 256, 272)) for i in range(16)], each=True)
     cp(top("OUT", 8, 256, 512), top("P3", 8, 256, 512), "VS")
     dma("Y", T.yj[:], T.OUT[0:8, 256:512], [c("OUT", 256, 512)], [], 8192)
+    ops[mark["first"]]["soft"].update(k for k, o in enumerate(ops) if o["tag"] == "0" and "V" in o["alts"] and CFG["early"])
     return ops, Q, ndma[0]
 
 
@@ -644,30 +659,34 @@ def polish(sets, seq, eng):
         x[0] = (x[0] * 1103515245 + 12345) % 2147483648
         return (x[0] >> 8) % m
 
+    gaps = [[x + m[1] for x in lat] + [0.0] for lat, m in zip(lats, sets)]
+
     def run(seq, a, old):
-        prev0, last0 = {}, {}
+        last = dict((r, n) for r in list("VSPGY") + ["P%d" % b for b in range(8)])
         for k in seq[:a]:
-            prev0[eng[k]] = k
+            last[eng[k]] = k
             for b in banks[k]:
-                last0[b] = k
+                last[b] = k
+        rest = []
+        for k in seq[a:]:
+            e, need = eng[k], hard[k]
+            for b in banks[k]:
+                d = last[b]
+                if d < n and eng[d] != e:
+                    need = need + [d]
+                last[b] = k
+            rest.append((k, last[e], need))
+            last[e] = k
         res, tot = [], 0.0
         for i, m in enumerate(sets):
-            dur, lat, LAT = durs[i], lats[i], m[1]
-            end, why = (list(old[i][0]), list(old[i][1])) if old else ([0.0] * n, [None] * n)
-            prev, last = dict(prev0), dict(last0)
-            for k in seq[a:]:
-                e = eng[k]
-                w = prev.get(e)
-                t = 0.0 if w is None else end[w] - lat[w] - LAT
-                for d in hard[k]:
+            dur, gap = durs[i], gaps[i]
+            end, why = (old[i][0][:], old[i][1][:]) if old else ([0.0] * (n + 1), [n] * n)
+            for k, w, need in rest:
+                t = end[w] - gap[w]
+                for d in need:
                     if end[d] > t:
                         t, w = end[d], d
-                for b in banks[k]:
-                    d = last.get(b)
-                    if d is not None and end[d] > t and eng[d] != e:
-                        t, w = end[d], d
-                    last[b] = k
-                prev[e], end[k], why[k] = k, t + dur[k] + lat[k] + LAT, w
+                end[k], why[k] = t + dur[k] + gap[k], w
             res.append((end, why))
             tot += (max(end) + PL["MEAN"] * sum(end) / n) * m[2]
         return tot, res
@@ -678,7 +697,7 @@ def polish(sets, seq, eng):
         end, why = r[rnd(len(r))]
         k = end.index(max(end)) if rnd(5) < 3 else rnd(n)
         pairs = []
-        while why[k] is not None:
+        while why[k] < n:
             if why[k] not in pred[k]:
                 pairs.append((why[k], k))
             k = why[k]

@@ -10,9 +10,9 @@ RO = 4
 
 CFG = {
     "gN": ["SVSVSVSV"] + ["S" * 8] * 3, "gR": ["S" * 8] * 4, "gH": ["S" * 8] * 3 + ["SVSSVSSV"],
-    "hN": [(0, 128, 256)] * 4, "hR": [(0, 128, 256)] * 4, "hH": [(0, 128, 256)] * 4,
-    "cN": [(0, 0)] * 4, "cR": [(0, 0)] * 4, "cH": [(0, 0)] * 4,
-    "lag": [(8, 0)] * 3, "pool": 2, "early": 1,
+    "hN": [(0, 128, 256)] * 4, "hR": [(0, 128, 256)] * 4, "hH": [(0, 128, 192, 256)] * 4,
+    "cN": [(0, 0)] * 4, "cR": [(0, 0)] * 4, "cH": [(0, 0, 0)] * 4,
+    "lag": [(0, 0), (4, 0), (4, 0)], "pool": 2, "early": 1, "onS": "ngpy", "two": 0, "ahead": 1, "hop": ["vvv"] * 4,
     "small": "VS", "evac": "VS",
 }
 
@@ -24,25 +24,26 @@ def _sb(names, shape, dty):
         S[n] = ("sbuf", shape, dty)
 
 
-_sb("X", [128, WN], "bfloat16")
+_sb("X0 X1", [128, WN], "bfloat16")
 _sb("TR", [128, WN], "float32")
 _sb("NB", [128, 4096], "int32")
 _sb("GN MN GR MR GH MH MC EB EC", [128, 4096], "bfloat16")
 _sb("TD", [128, 2048], "bfloat16")
-_sb("AW V0 V1 PM SEL SEP SC RS MK PR Pf COL COLG KC DUMR", [128, 256], "float32")
+_sb("AW V0 V1 PM SEL SEP SC RS MK MV PR PQ Pf COL COLG KC DUMR", [128, 256], "float32")
 _sb("Ai Si Ui Hi VJi", [128, 256], "int32")
 _sb("NBu Au Hu", [128, 256], "uint16")
-_sb("A0 A1 NBc RW RP RU0 RU1 RB ZH Bc VJ PS", [128, 256], "float16")
-_sb("Y0 Y1 NE XN XW SR SH ONE XP FD HS M1 MB JR C2K KR KD", [128, 256], "bfloat16")
+_sb("A0 A1 NBc RW RP RU0 RU1 RB ZH Bc Bo VJ PS", [128, 256], "float16")
+_sb("Y0 Y1 NE XN XW0 XW1 SR ONE XP FD HS M1 MB JR C2K KR SL", [128, 256], "bfloat16")
 _sb("ZO0 ZO1 ZO2 ZO3 ZO4 ZI1 ZI2 ZI3 ZI4", [128, 272], "bfloat16")
 _sb("E1 E2 nE Es EW E4 S4 G4", [128, 144], "bfloat16")
 _sb("CQ", [128, 144], "float32")
 _sb("MQ", [128, 64], "float32")
-_sb("I nI I4 nI4 I2 I32 KI nKI BO nBO BO8 WH WL TH RG K8", [128, 128], "bfloat16")
+_sb("I nI I4 nI4 I2 I32 KI nKI BO BO8 WH WL TH TP RG K8 IF nIF", [128, 128], "bfloat16")
 _sb("fI", [128, 128], "float16")
-_sb("T16", [128, 16], "float16")
+_sb("T16", [128, 32], "float16")
 _sb("O16", [128, 128], "float32")
-_sb("CL KK", [128, 512], "bfloat16")
+_sb("KK SH", [128, 512], "bfloat16")
+_sb("CL", [128, 640], "bfloat16")
 _sb("MX", [128, 1024], "bfloat16")
 _sb("GS", [128, 48], "bfloat16")
 _sb("C", [128, 64], "float32")
@@ -57,9 +58,11 @@ SCRATCH = S
 NDMA = 18
 SEMAPHORES = ["V", "S", "P", "G"] + ["d%d" % k for k in range(NDMA)] + ["arr%d" % k for k in range(1, 5)] + ["sent%d" % k for k in range(4)]
 
-SETS = [dict(CY=.85, PCY=.45, GA=1.4, SC=3.0, LAT=240., OVH=10., MM=3., BW=400., SEND=3000., W=1.0)]
-PL = {"SEED": 4, "NOISE": 0.0, "PASSES": 2, "STEPS": 70000, "TEMP": 150.0, "MEAN": 0.3,
-      "LEAD": {"y": 20000.0, "n": 8000.0, "d": 12000.0}}
+SETS = [dict(CY=.85, PCY=.45, GA=1.4, SC=3.0, LAT=250., OWN=150., OVH=10., MM=3., BW=400., SEND=3000., FIRST=7000., GD=1000., W=1.0),
+        dict(CY=.85, PCY=.44, GA=1.22, SC=2.5, LAT=230., OWN=165., OVH=8., MM=2., BW=400., SEND=2500., FIRST=11000., GD=2500., W=0.6),
+        dict(CY=1.08, PCY=.55, GA=1.7, SC=4.2, LAT=260., OWN=170., OVH=10., MM=3., BW=300., SEND=3000., FIRST=15000., GD=2500., W=0.33)]
+PL = {"SEED": 4, "NOISE": 500.0, "PASSES": 10, "STEPS": 70000, "TEMP": 150.0, "MORE": 36000, "COOL": 60.0, "AGAIN": 9, "MEAN": 0.3,
+      "LEAD": {"y": 20000.0, "n": 8000.0, "d": 12000.0, "h1": 20000.0, "a1": 20000.0, "H1": 15000.0, "n2": 0.0, "m1": 15000.0, "r1": 15000.0, "c1": 10000.0}}
 
 
 def build(g, T, dest):
@@ -204,7 +207,7 @@ def build(g, T, dest):
         if load:
             busy[0] += nbytes / PL["BW"]
             lat = busy[0]
-        return add({q: ([lambda: Q[q].dma_start(out, in_, **kw)], 60.0 if q != "G" else 1000.0)}, rd, wr, sem=s, lat=lat)
+        return add({q: ([lambda: Q[q].dma_start(out, in_, **kw)], 60.0 if q != "G" else PL["GD"])}, rd, wr, sem=s, lat=lat)
 
     def wf(k):
         return c("Wf", 16 * k, 16 * k + 16)
@@ -231,13 +234,15 @@ def build(g, T, dest):
         return [(out, E(e, i, rows), top(src, rows, i, 256, 16)) for i in range(16)]
 
     ld = [dma("Y", T.VJi[0:8, :], T.v0[:], [], [c("VJi")], 8192, True),
-          dma("Y", T.Ai[:], T.a0[:], [], [c("Ai")], 131072, True),
-          dma("Y", T.X[:, 0:4096], T.x[:], [], [c("X", 0, 4096)], 1 << 20, True),
           dma("Y", T.Hi[0:8, :], T.j0[:], [], [c("Hi")], 8192, True),
           dma("Y", T.Ci[:, 8:9], T.w[:], [], [c("Ci", 8, 12)], 512, True),
           dma("Y", T.ZO0[:, 0:256], T.z0[:], [], [c("ZO0", 0, 256)], 65536, True),
           dma("Y", T.NB[:], T.nb[:], [], [c("NB")], 2 << 20, True),
-          dma("Y", T.Y0[:], T.y0[:], [], [c("Y0")], 65536, True)]
+          dma("Y", T.X0[:, 0:4096], T.x[:], [], [c("X0", 0, 4096)], 1 << 20, True),
+          dma("Y", T.Y0[:], T.y0[:], [], [c("Y0")], 65536, True),
+          dma("Y", T.Ai[:], T.a0[:], [], [c("Ai")], 131072, True)]
+    if CFG["two"]:
+        ld.append(dma("Y", T.X1[:, 0:4096], T.x[:], [], [c("X1", 0, 4096)], 1 << 20, True))
     for k in ld[1:]:
         ops[k]["soft"].add(k - 1)
     small = dict(allow_small_or_imprecise_dtypes=True)
@@ -249,7 +254,7 @@ def build(g, T, dest):
     gp(lambda: g.iota(T.KK[0:1, 256:512], [[0, 16], [-8192, 16]], 131072, 0, **small), 256, [], [c("KK", 256, 512)])
     gp(lambda: g.iota(T.K8[:], [[0, 16], [1, 8]], 0, 0, **small), 128, [], [c("K8")])
     gp(lambda: g.iota(T.TR[:], [[1, WN]], -2048, 0, **small), WN, [], [c("TR")])
-    P_, L_, G_, T15, Q4, L0, W8, WH_, WL_, FS, FR, THR, QC, THH, CH, P2K, K0, K1, K2, K3, K4, K5 = range(22)
+    P_, L_, G_, T15, Q4, L0, W8, WH_, WL_, FS, FR, THR, QC, THH, CH, P2K, K0, K1, CP, QB, N30, P3K, QV, CH1 = range(24)
     LT = 24
     BIG = 2097152.0
     ms(c("CQ"), -1.0)
@@ -271,19 +276,20 @@ def build(g, T, dest):
     ts(col(FS), ci(1), 102.0, A_.mult, 102.5, A_.add)
     tt(col(THH), col(FR), col(FS), A_.add)
     ts(col(CH), ci(1), 4096.0, A_.mult, 4096.0, A_.add)
-    for k, (m, v) in enumerate(((75.0, -80.0), (74.5, -80.0), (-524288.0, 524288.0), (-16384.0, 0.0), (262144.0, 0.0), (2048.0, 0.0))):
+    for k, (m, v) in enumerate(((75.0, -80.0), (74.5, -80.0))):
         ts(col(K0 + k), ci(0), m, A_.mult, v, A_.add)
     c2 = lambda k: top("C", 2, k, k + 1)
     ts(top("KR", 2), top("KC", 2), c2(K0), A_.mult, c2(K1), A_.add)
-    ts(top("SEP", 2), top("COLG", 2), c2(K2), A_.mult)
-    ts(top("AW", 2), top("KC", 2), c2(K3), A_.mult, c2(K4), A_.add)
-    ts(top("AW", 2, 0, 256, 16), top("AW", 2, 0, 256, 16), c2(K5), A_.add)
-    tt(top("KD", 2), top("SEP", 2), top("AW", 2), A_.add)
+    ts(col(CP), ci(1), -4096.0, A_.mult, 65536.0, A_.add)
+    ts(col(QB), col(QC), -30720.0, A_.add)
+    ms(col(N30), -30720.0)
+    ms(col(P3K), 3000.0)
     ms(col(P2K), 2048.0)
     ms(c("ONE"), 1.0)
     ms(c("O16"), 16.0)
     ms(c("C2K"), 2048.0)
-    for k, v in enumerate((2048.0, -4128768.0, -120.0, -4096.0)):
+    ts(col(CH1), ci(1), 8192.0, A_.mult)
+    for k, v in enumerate((2048.0, -4128768.0, -120.0, -4096.0, 131072.0)):
         ms(top("CL", 1, 128 * k, 128 * k + 128), v)
     ts(top("G4", 8), top("CQ", 8), top("C", 8, P_, P_ + 1), A_.is_equal)
     ts(top("RG", 8), top("COLG", 8, 0, 128), top("C", 8, P_, P_ + 1), A_.is_equal)
@@ -293,19 +299,24 @@ def build(g, T, dest):
     ts(c("BO"), c("COLG", 0, 128), col(G_), A_.is_equal)
     ts(c("GS", 40, 48), c("COL", 0, 8), col(G_), A_.is_equal)
     for n, m, v in (("S4", "E4", col(L0)), ("E2", "E1", 2.0), ("nE", "E1", -1.0), ("Es", "E1", col(L0)), ("nI", "I", -1.0), ("I4", "I", 4096.0), ("nI4", "I", -4096.0),
-                    ("I2", "I", 2048.0), ("I32", "I", 32.0), ("KI", "I", 1024.0), ("nKI", "I", -1024.0), ("fI", "I", 2047.0 / 4096.0), ("BO8", "BO", 8192.0)):
+                    ("I32", "I", 32.0), ("KI", "I", 1024.0), ("nKI", "I", -1024.0), ("fI", "I", 2047.0 / 4096.0), ("BO8", "BO", 8192.0),
+                    ("IF", "I", 131072.0), ("nIF", "I", -131072.0)):
         mul(c(n), c(m), v)
     for k, v in enumerate((32.0, -16.0, 16.0, 2.0, -1.0)):
         mul(c("GS", 8 * k, 8 * k + 8), c("GS", 40, 48), v)
-    ms(c("X", 4096, WN), 0.0)
+    for n in ("X0", "X1"):
+        ms(c(n, 4096, WN), 0.0)
     ts(c("RS"), c("KC"), 0.0, A_.is_equal, 1000000.0, A_.mult)
     ts(c("PM"), c("KC"), col(L_), A_.is_equal)
     ts(c("MB"), c("PM"), -30720.0, A_.mult, 32768.0, A_.add)
+    ts(c("MV"), c("PM"), 262144.0, A_.mult, -8192.0, A_.add)
+    ts(col(QV), ci(1), -8192.0, A_.mult, 15 * 8192.0 + 2048.0, A_.add)
     ts(c("SEL"), c("COL"), SPARE, A_.add)
     tt(c("MK"), c("SEL"), c("PM"), A_.mult)
-    ts(c("PR", 0, 128), c("KC", 0, 128), col(L_), A_.is_gt, 4096.0, A_.mult)
-    tt(c("Pf", 0, 128), c("PR", 0, 128), c("BO"), A_.mult)
-    tt(c("TH"), c("Pf", 0, 128), c("nI4"), A_.add)
+    for n, op in (("TH", A_.is_gt), ("TP", A_.is_lt)):
+        ts(c("NE", 0, 128), c("KC", 0, 128), col(L_), op, 4096.0, A_.mult)
+        tt(c("NE", 128, 256), c("NE", 0, 128), c("BO"), A_.mult)
+        tt(c(n), c("NE", 128, 256), c("nI4"), A_.add)
     ts(c("C", LT, LT + 16), c("COL", 0, 16), col(L_), A_.is_gt)
     for i in range(1, 16):
         mul(c("TD", 128 * i, 128 * i + 128), c("BO8"), col(LT + i))
@@ -320,51 +331,53 @@ def build(g, T, dest):
 
     lo = lambda b: c("P%d" % b, 0, 256)
     hi = lambda b: c("P%d" % b, 256, 512)
-    X = c("X", 0, 4096)
+    X = lambda t: c("X%d" % (t % 2 * CFG["two"]), 0, 4096)
     pu = lambda k: c("P4", 256 + 64 * k, 320 + 64 * k)
     pw = lambda k: c("P7", 256 + 64 * k, 320 + 64 * k)
-    V0, V1, OV0, OV1, OB, JU, PU = range(7)
+    V0, V1, OB, JU, PU, OV = range(6)
+    ov = lambda t: wu(OV + t % 3)
     T1, T2, T3, J1, J2 = range(5)
     EV = CFG["evac"]
 
     def send(t):
         src, dst, s = "ZO%d" % t, "ZI%d" % (t + 1), "arr%d" % (t + 1)
         add({"G": ([lambda: g.remote_dma(T[dst][:], T[src][:], T.sem[s], T.sem["sent%d" % t], dest[1], dest[0], dest[2])], 500.0)},
-            [c(src)], [c(dst)], sem=s, lat=PL["SEND"] if t else busy[0], remote=True)
+            [c(src)], [c(dst)], sem=s, lat=PL["SEND"] if t else PL["FIRST"], remote=True)
 
-    def dedup(ru, key, eb, off):
-        p = lo(4)
+    def dedup(ru, key, eb, off, p, pr):
         for k0, k1 in ((0, 2), (2, 4), (4, 6), (6, 9), (9, 12), (12, 16)):
             fs, wr, cost = [], [], 0.0
             for k in range(k0, k1):
                 o = c(eb, 256 * k, 256 * k + 256 - 16 * k)
-                fs.append(lambda o=o, k=k: g.vector.tensor_scalar(o[0], T[ru][:, 16 * k:256], T.C[:, QC:QC + 1], T.SC[:, 64 * key + 4 * k + 3:64 * key + 4 * k + 4], A_.subtract, A_.is_equal))
+                fs.append(lambda o=o, k=k: g.vector.tensor_scalar(o[0], T[ru][:, 16 * k:256], col(QB if key else QC)[0], T.SC[:, 64 * key + 4 * k + 3:64 * key + 4 * k + 4], A_.subtract, A_.is_equal))
                 wr.append(o)
                 cost += vc(o[4] * 0.5)
-            add({"V": (fs, cost)}, [c(ru), col(QC), c("SC", 64 * key, 64 * key + 64)], wr)
+            add({"V": (fs, cost)}, [c(ru), col(QB if key else QC), c("SC", 64 * key, 64 * key + 64)], wr)
         blk = lambda k: (sub(p, 16 * k + 16, 256), c("BO8"), c(eb, 256 * k + 16, 256 * k + 256 - 16 * k))
         mm([(p, c("I"), c("MB")), (p, c("I"), c(ru))] + [blk(k) for k in range(4)], last=False)
         mm([blk(k) for k in range(4, 9)], first=False, last=False)
         mm([blk(k) for k in range(9, 15)], first=False, last=False)
         mm([(sub(p, i, 256, 16), c("TD", 128 * i, 128 * i + 128), c(eb, i, 4096, 256)) for i in range(1, 16)], first=False)
-        scan(c("PR"), c("MK"), p, A_.max, A_.min)
-        cp(off, c("PR", 15, 256, 16))
+        scan(c(pr), c("MK"), p, A_.max, A_.min)
+        cp(off, c(pr, 15, 256, 16))
 
     def gather(job, lst, t):
         en = CFG["g" + job][t - 1]
         w = 256 // len(en)
         for h, e in enumerate(en):
-            k = gat(c("G" + job, 16 * w * h, 16 * w * (h + 1)), X, c(lst, w * h, w * (h + 1)))
+            k = gat(c("G" + job, 16 * w * h, 16 * w * (h + 1)), X(t if job == "H" else t - 1), c(lst, w * h, w * (h + 1)))
             ops[k]["pref"] = e
             mark[job, t, h] = k
             if job == "H" and t < RO and h == CFG["lag"][t - 1][1]:
                 ops[k]["soft"].update(mark["N", t + 1, x] for x in range(CFG["lag"][t - 1][0]))
 
-    def dist(job, oth, pd, head, t):
+    def dist(job, oth, pd, head, t, close=True):
         Gn, Mn, cuts = "G" + job, "M" + job, CFG["h" + job][t - 1]
         pc, ps = "P0" if job == "H" else "P1", "P0" if job == "N" else "P5"
         f0 = 0 if job == "N" else 24
-        mm([(c(pc, r, 512, 2), c("I"), c(oth, 0, 256)) for r in (0, 1)], each=True)
+        whole = min(CFG["c" + job][t - 1]) == 8
+        if not whole:
+            mm([(c(pc, r, 512, 2), c("I"), c(oth, 0, 256)) for r in (0, 1)], each=True)
         first = True
         for u0, u1, nc in zip(cuts, cuts[1:], CFG["c" + job][t - 1]):
             wd = u1 - u0
@@ -390,6 +403,10 @@ def build(g, T, dest):
             for i, (_, path, ls) in enumerate(steps):
                 l = ls[0]
                 if path == "c":
+                    if whole:
+                        ps = ("P0", "P1")[i % 2]
+                    elif t == 1:
+                        ps = "P5" if ps == "P0" else "P0"
                     for q, x in enumerate(ls):
                         so = c(ps, wd * q, wd * q + wd)
                         mm([(so, c("nI"), c(oth, u0, u1)), (so, c("I"), lv(Gn, x))])
@@ -405,7 +422,7 @@ def build(g, T, dest):
                     else:
                         tt(c(Mn, 16 * u0 + l, 16 * u1, 8), c(Gn, 16 * u0 + l, 16 * u1, 8), c(pc, 2 * u0, 2 * u1), A_.max)
                     tm = terms(Mn, ls, 0)
-                mm(head + tm, first=first, last=u1 == 256 and i == len(steps) - 1)
+                mm(head + tm, first=first, last=close and u1 == 256 and i == len(steps) - 1)
                 head, first = [], False
 
     made = {}
@@ -422,8 +439,8 @@ def build(g, T, dest):
         scan(c("SC", 64 * k, 64 * k + 64), c("MQ"), p, A_.add, A_.min)
         return c("SC", 64 * k + 3, 64 * k + 64, 4)
 
-    def rows(b, rw):
-        mm([(top("P%d" % b, 8, 128 * h, 128 * h + 128), c("T16", 8 * h, 8 * h + 8), c("I")) for h in (0, 1)], each=True)
+    def rows(b, rw, o):
+        mm([(top("P%d" % b, 8, 128 * h, 128 * h + 128), c("T16", o + 8 * h, o + 8 * h + 8), c("I")) for h in (0, 1)], each=True)
         cp(top(rw, 8), top("P%d" % b, 8, 0, 256), EV)
 
     def lists(vu, b):
@@ -433,12 +450,10 @@ def build(g, T, dest):
 
     ts(top("RW", 8), top("VJi", 8), -2048.0, A_.add)
     lists(wu(V0), 0)
-    ts(c("A0"), c("Ai"), -2048.0, A_.add)
-    cp(c("Au"), c("Ai"))
     cp(top("JR", 8), top("Hi", 8))
     cp(c("ZO0", 256, 272), pick(pw(0), "G4", "JR", 2, 8), "V", col(QC))
     send(0)
-    dedup("RU0", 0, "EB", wu(OV0))
+    dedup("RU0", 0, "EB", ov(0), lo(4), "PR")
 
     def users(t):
         a, b = (t - 1) % 2, t % 2
@@ -446,9 +461,7 @@ def build(g, T, dest):
         tag[0] = "g%d" % t
         gather("R", "Au", t)
         tag[0] = "n%d" % t
-        k = gat(c("NBu"), c("NB"), wu(V0 + a), "V")
-        if t == 1:
-            mark["first"] = k
+        gat(c("NBu"), c("NB"), wu(V0 + a), "V")
         gather("N", "NBu", t)
         ts(c("NBc"), c("NBu"), -2048.0, A_.add)
         dist("N", y, lo(2), [(c("P2"), top("ONE", 1, 0, 128), top("KK", 1))] + turn(hi(2), "NBc", "I"), t)
@@ -456,15 +469,19 @@ def build(g, T, dest):
         tt(c("NE"), lo(2), c("PM"), A_.not_equal)
         scan(c("SEL"), c("NE"), hi(2), A_.mult, A_.max)
         ts(wf(T1), c("SEL", 15, 256, 16), MAGIC * 8192, A_.add, -MAGIC * 8192, A_.add)
-        tt(c("T16"), c("SEL", 15, 256, 16), wf(T1), A_.subtract)
-        rows(2, "RW")
+        tt(c("T16", 0, 16), c("SEL", 15, 256, 16), wf(T1), A_.subtract)
+        rows(2, "RW", 0)
         lists(wu(V0 + b), b)
         gcp(c("V%d" % b), c(ru))
-        gat(c("XN"), X, wu(V0 + b))
+        gat(c("XN"), X(t - 1), wu(V0 + b))
         tag[0] = "d%d" % t
-        dedup(ru, 0, "EB", wu(OV0 + b))
+        dedup(ru, 0, "EB", ov(t), lo(4), "PR")
         mm([(lo(2), c("fI"), c("XN")), (lo(2), c("fI"), c(y))])
-        ts(c("XW"), lo(2), MAGIC, A_.add, -MAGIC, A_.add)
+        ts(c("XW%d" % b), lo(2), MAGIC, A_.add, -MAGIC, A_.add)
+        if t == 1 and not CFG["two"]:
+            sca(c("X0"), ov(t), c("XW%d" % b))
+        for s in range(max(1, t - 1), t + 1) if CFG["two"] else ():
+            sca(c("X%d" % b), ov(s), c("XW%d" % (s % 2)))
         tag[0] = "y%d" % t
         mm([(hi(2), c("I"), c(y)), (hi(2), c("nI"), c("XN"))])
         act(c(yn), hi(2), F_.Abs)
@@ -476,7 +493,8 @@ def build(g, T, dest):
         a, b = (t - 1) % 2, t % 2
         Ao, An, ru = "A%d" % a, "A%d" % b, "RU%d" % b
         tag[0] = "d%d" % t
-        sca(c("X"), wu(OV0 + b), c("XW"))
+        if t > 1 and not CFG["two"]:
+            sca(c("X0"), ov(t), c("XW%d" % b))
         tag[0] = "r%d" % t
         act(c("SR"), lo(3), F_.Sign, bias=0.0 if t == 1 else col(THR), scale=-1.0)
         mm(turn(hi(5), "SR", "nI4") + turn(lo(5), "SR", "I4"), first=False)
@@ -487,63 +505,103 @@ def build(g, T, dest):
             ts(c("Au"), c(An), 2048.0, A_.add)
         tag[0] = "p%d" % t
         if t > 1:
-            mm([(hi(3), top("ONE", 2, 0, 128), top("KD", 2))] + turn(hi(3), Ao, "I") + [(sub(hi(3), 0, 256, 16), c("I2"), c("SR", 0, 256, 16))])
-            scan(c("SEP"), c("SR"), hi(3), A_.mult, A_.max)
-            ts(wf(T2), c("SEP", 15, 256, 16), MAGIC * 16384, A_.add, -MAGIC * 16384, A_.add)
-            tt(wf(T3), c("SEP", 15, 256, 16), wf(T2), A_.subtract)
-            ts(c("T16"), wf(T3), 2048.0, A_.min)
-            rows(5, "RP")
-            pick(pu(1), "G4", "RP", 1, 8)
-            mm([(hi(5), top("RG", 8), top("RP", 8))])
-            cp(c("RB"), hi(5), EV)
-            dedup("RB", 1, "EC", wu(OB))
+            mm([(hi(3), c("I"), c(Ao))], last=False)
+            act(c("SL"), hi(5), F_.Sign, bias=col(P3K))
+            mm([(hi(3), c("TP"), c("SL"))], first=False)
+            ts(c("RP"), hi(3), col(CP), A_.add, 2048.0, A_.min)
+            mm([(hi(5), c("BO"), c("RP"))])
+            cp(c("RB"), hi(5), EV, col(N30))
+            pick(c("P3", 256, 320), "E4", "RP", 1)
+            dedup("RB", 1, "EC", wu(OB), lo(5), "PQ")
             sca(c("TR"), wu(OB), c("RB"))
-        sca(c("TR"), wu(OV0 + a), c(ru))
+        sca(c("TR"), ov(t - 1), c(ru))
 
-    def seekers(t):
-        b = t % 2
-        zi, zo = "ZI%d" % t, "ZO%d" % t
+    def hashed(src, pb, pq):
+        mm([const(pb, 0)], last=False)
+        mm([(pb, c("I"), c(src))], first=False)
+        mm([const(pq, 1), (pq, c("I32"), c(src))])
+        tt(c("DUMR"), c("Ui"), pb, A_.mult)
+        tt(c("Si"), c("DUMR"), pq, A_.add)
+        ts(c("Hi"), c("Si"), 5, A_.arith_shift_right, 4095, A_.bitwise_and)
+
+    def hashes(t, bc):
+        zi = "ZI%d" % t
         z, j = c(zi, 0, 256), c(zi, 256, 272)
         tag[0] = "h%d" % t
         cp(wu(JU), j)
         mm([(hi(6), c("WH"), z), (hi(6), c("WL"), z)])
         cp(c("Si"), hi(6))
         ts(c("Ui"), c("Si"), 4095, A_.bitwise_and)
+        gat(c(bc), c("AW"), wu(JU))
+        hashed(bc, lo(7), lo(6))
+        cp(c("Hu"), c("Hi"))
         tag[0] = "j%d" % t
         cp(wi(0), pick(pw(0), "EW", zi, 2))
         ts(wi(1), wi(0), 255, A_.bitwise_and)
         tt(wf(J1), wi(1), j, A_.subtract)
-        tag[0] = "h%d" % t
-        gat(c("Bc"), c("AW"), wu(JU))
-        gat(c("VJ"), c("V%d" % b), wu(JU))
-        mm([const(lo(7), 0), (lo(7), c("I"), c("Bc"))])
-        mm([const(lo(6), 1), (lo(6), c("I32"), c("Bc"))])
-        mm([(hi(6), c("I"), c("VJ"))])
-        tt(c("DUMR"), c("Ui"), lo(7), A_.mult)
-        tt(c("Si"), c("DUMR"), lo(6), A_.add)
-        ts(c("Hi"), c("Si"), 5, A_.arith_shift_right, 4095, A_.bitwise_and)
-        cp(c("Hu"), c("Hi"))
+
+    def probe(t, close):
         tag[0] = "H%d" % t
         gather("H", "Hu", t)
-        dist("H", zi, lo(6), [], t)
-        tag[0] = "c%d" % t
-        act(c("SH"), lo(6), F_.Sign, bias=col(THH), scale=-1.0)
-        mm([(lo(7), c("I"), c("Bc")), (lo(7), c("TH"), c("SH"))])
-        ts(c("ZH"), lo(7), col(CH), A_.add, 2048.0, A_.min)
+        dist("H", "ZI%d" % t, lo(6), [], t, close)
+
+    def ahead():
+        z = c("ZI1", 0, 256)
+        tag[0] = "a1"
+        gat(c("VJ"), c("V1"), wu(JU))
+        hashed("VJ", lo(7), hi(7))
+        cp(c("PQ"), c("Hi"))
+        scan(c("DUMR"), c("MV"), c("PQ"), A_.add, A_.min)
+        ts(wu(PU), c("DUMR", 15, 256, 16), col(QV), A_.add, -2048.0, A_.add)
+        gat(c("XP"), X(1), wu(PU))
+        mm([(lo(7), c("I"), z), (lo(7), c("nI"), c("XP"))])
+        act(c("M1"), lo(7), F_.Abs)
+        probe(1, False)
+        mm([(hi(6), c("BO"), c("M1"))], first=False, last=False)
+
+    def seekers(t):
+        b = t % 2
+        zi, zo = "ZI%d" % t, "ZO%d" % t
+        z, j = c(zi, 0, 256), c(zi, 256, 272)
+        if t > 1 or not CFG["ahead"]:
+            hashes(t, "Bc")
+            gat(c("VJ"), c("V%d" % b), wu(JU))
+            mm([(hi(6), c("I"), c("VJ"))])
+            probe(t, True)
+            tag[0] = "c%d" % t
+            mm([(lo(7), c("I"), c("Bc"))], last=False)
+            act(c("SH", 0, 256), lo(6), F_.Sign, bias=col(THH), scale=-1.0)
+            mm([(lo(7), c("TH"), c("SH", 0, 256))], first=False)
+            ts(c("ZH"), lo(7), col(CH), A_.add, 2048.0, A_.min)
+        else:
+            tag[0] = "c%d" % t
+            gat(c("Bc"), c("AW"), wu(JU))
+            tt(c("FD"), c("Bc"), c("Bo"), A_.is_equal)
+            mm([(lo(6), c("nIF"), c("FD")), (hi(6), c("IF"), c("FD")), const(lo(6), 4)], first=False)
+            mm([(lo(7), c("I"), c("Bc"))], last=False)
+            act(c("SH"), c("P6"), F_.Sign, bias=col(THH), scale=-1.0)
+            mm([(lo(7), c("TH"), c("SH", 0, 256)), (lo(7), c("TH"), c("SH", 256, 512))], first=False)
+            ts(c("ZH"), lo(7), col(CH1), A_.add, 2048.0, A_.min)
+            mm([(hi(6), c("I"), c("VJ"))])
         ts(wu(PU), pick(pw(1), "E4", "ZH", 3), col(QC), A_.add, -28672.0, A_.add)
         for k in range(3):
             gat(c("PS"), c("TR", 0, 4096), wu(PU))
-            ts(wu(PU), pick(pw(1), "S4", "PS", 3), col(QC), A_.add, 2048.0, A_.add)
-        gat(c("XP"), X, wu(PU))
+            if CFG["hop"][t - 1][k] == "p":
+                ts(wu(PU), pick(pw(1), "S4", "PS", 3), col(QC), A_.add, 2048.0, A_.add)
+            else:
+                scan(c("DUMR"), c("MV"), c("PS"), A_.add, A_.min)
+                ts(wu(PU), c("DUMR", 15, 256, 16), col(QV), A_.add)
+        gat(c("XP"), X(t), wu(PU))
         tt(c("FD"), c("PS"), hi(6), A_.is_equal)
         mm([(lo(6), c("I"), z), (hi(6), c("nI"), z), (lo(6), c("nKI"), c("FD")), (hi(6), c("nKI"), c("FD"))], last=False)
-        fw = sub(pw(2), 0, 16)
+        fw = c("P0", 0, 16)
         mm(toW(fw, "Es", "FD"))
-        mm([(lo(7), c("fI"), z), (lo(7), c("KI"), c("FD")), (lo(7), c("fI"), c("XP"))])
+        mm([(lo(7), c("fI"), z), (lo(7), c("KI"), c("FD"))], last=False)
+        mm([(lo(7), c("fI"), c("XP"))], first=False)
         mm([(lo(6), c("nI"), c("XP")), (hi(6), c("I"), c("XP"))], first=False)
         if t < RO:
             add({"V": ([lambda: g.vector.tensor_reduce(T.C[:, FS:FS + 1], fw[0], AxisListType.X, A_.add)], vc(16))}, [fw], [col(FS)])
-            pf = sub(pw(3), 0, 1)
+            pf = c("P0", 16, 17)
             mm([const(pf, 2, 1), (pf, c("O16"), col(FS))])
             ts(col(FR), pf, MAGIC * 256, A_.add, -MAGIC * 256, A_.add)
             ts(col(THR), pf, col(FR), A_.subtract, 120.0, A_.add)
@@ -555,7 +613,15 @@ def build(g, T, dest):
         if t < RO:
             send(t)
 
+    tag[0] = "g1"
+    ts(c("A0"), c("Ai"), -2048.0, A_.add)
+    ts(c("Au"), c("A0"), 2048.0, A_.add)
+    if CFG["ahead"]:
+        gcp(c("AW"), c("A0"))
+        hashes(1, "Bo")
     users(1)
+    if CFG["ahead"]:
+        ahead()
     renew(1)
     for t in range(1, RO + 1):
         if t < RO:
@@ -570,13 +636,17 @@ def build(g, T, dest):
             dma("Y", T.yy[:], T.Y0[:], [c("Y0")], [], 65536)
             cp(top("OUT", 8, 0, 256), top("RW", 8), "VS", top("C", 8, P2K, P2K + 1))
             dma("Y", T.yv[:], T.OUT[0:8, 0:256], [c("OUT", 0, 256)], [], 8192)
-            dma("G", T.yt[:], T.TR[0:128:16, 0:4096], [c("TR")], [c("JR")], 131072)
-            dma("G", T.yt[:], T.C2K[:], [c("C2K"), c("JR")], [], 131072, accum_op=A_.add)
+            dma("G", T.yt[:], T.C2K[:], [c("C2K")], [c("JR")], 131072)
+            dma("G", T.yt[:], T.TR[0:128:16, 0:4096], [c("TR"), c("JR")], [], 262144, accum_op=A_.add, max_dma_last_dim=8192)
     dma("Y", T.yz[:], T.ZO4[:, 0:256], [c("ZO4", 0, 256)], [], 65536)
     mm([(top("P3", 8, 256 + i, 512, 16), c("I", i, 128, 16), c("ZO4", 256, 272)) for i in range(16)], each=True)
     cp(top("OUT", 8, 256, 512), top("P3", 8, 256, 512), "VS")
     dma("Y", T.yj[:], T.OUT[0:8, 256:512], [c("OUT", 256, 512)], [], 8192)
-    ops[mark["first"]]["soft"].update(k for k, o in enumerate(ops) if o["tag"] == "0" and "V" in o["alts"] and CFG["early"])
+    for o in ops:
+        if len(o["alts"]) == 2 and o["tag"][:1] in CFG["onS"] and o["tag"][1:] != "1":
+            o["alts"].pop("V")
+    for h in range(2):
+        ops[mark["N", 1, h]]["soft"].update(k for k, o in enumerate(ops) if o["tag"] == "0" and "V" in o["alts"] and CFG["early"])
     return ops, Q, ndma[0]
 
 
@@ -604,7 +674,7 @@ def plan(ops):
                 for x in before[k]:
                     p, s = (k, x) if back else (x, k)
                     free = eng[x] == e == "P"
-                    t = max(t, at[x] + dur(x) + (0.0 if free or p in ops[s]["soft"] else LAT + ops[p]["lat"]))
+                    t = max(t, at[x] + dur(x) + (0.0 if free or p in ops[s]["soft"] else PL["OWN"] if eng[x] == e and e in "VS" else LAT + ops[p]["lat"]))
                 if back and not before[k]:
                     t = o["lat"]
                 spans = sorted([u[:2] for u in use.get(e, [])] + [(u[0] - LAT, u[1] + LAT) for b in o["banks"] for u in use.get(b, []) if u[2] != e])
@@ -641,7 +711,7 @@ def plan(ops):
     return best
 
 
-def polish(sets, seq, eng):
+def polish(sets, seq, eng, steps, temp):
     ops = sets[0][0]
     n, eng = len(ops), list(eng)
     pred = [o["raw"] | o["oth"] | o["soft"] for o in ops]
@@ -653,7 +723,7 @@ def polish(sets, seq, eng):
     banks = [sorted(o["banks"]) for o in ops]
     durs = [[o["alts"][eng[k]][1] for k, o in enumerate(m[0])] for m in sets]
     lats = [[o["lat"] for o in m[0]] for m in sets]
-    x = [PL["SEED"]]
+    x = [PL["SEED" if len(sets) == 1 else "AGAIN"]]
 
     def rnd(m):
         x[0] = (x[0] * 1103515245 + 12345) % 2147483648
@@ -662,38 +732,42 @@ def polish(sets, seq, eng):
     gaps = [[x + m[1] for x in lat] + [0.0] for lat, m in zip(lats, sets)]
 
     def run(seq, a, old):
-        last = dict((r, n) for r in list("VSPGY") + ["P%d" % b for b in range(8)])
-        for k in seq[:a]:
-            last[eng[k]] = k
+        last0 = dict((r, n) for r in list("VSPGY") + ["P%d" % b for b in range(8)])
+        for k in seq[max(0, a - 400):a]:
+            last0[eng[k]] = k
             for b in banks[k]:
-                last[b] = k
-        rest = []
-        for k in seq[a:]:
-            e, need = eng[k], hard[k]
-            for b in banks[k]:
-                d = last[b]
-                if d < n and eng[d] != e:
-                    need = need + [d]
-                last[b] = k
-            rest.append((k, last[e], need))
-            last[e] = k
+                last0[b] = k
         res, tot = [], 0.0
         for i, m in enumerate(sets):
-            dur, gap = durs[i], gaps[i]
+            dur, gap, own, last = durs[i], gaps[i], m[3], dict(last0)
             end, why = (old[i][0][:], old[i][1][:]) if old else ([0.0] * (n + 1), [n] * n)
-            for k, w, need in rest:
+            for k in seq[a:]:
+                e = eng[k]
+                w = last[e]
+                last[e] = k
                 t = end[w] - gap[w]
-                for d in need:
-                    if end[d] > t:
+                for d in hard[k]:
+                    x = end[d]
+                    if x > t:
+                        if eng[d] == e and e in "VS":
+                            x -= own
+                            if x <= t:
+                                continue
+                        t, w = x, d
+                for b in banks[k]:
+                    d = last[b]
+                    last[b] = k
+                    if end[d] > t and eng[d] != e:
                         t, w = end[d], d
-                end[k], why[k] = t + dur[k] + gap[k], w
+                end[k] = t + dur[k] + gap[k]
+                why[k] = w
             res.append((end, why))
             tot += (max(end) + PL["MEAN"] * sum(end) / n) * m[2]
         return tot, res
 
     cur, r = run(seq, 0, None)
     best = (cur, seq, list(eng))
-    for it in range(PL["STEPS"]):
+    for it in range(steps):
         end, why = r[rnd(len(r))]
         k = end.index(max(end)) if rnd(5) < 3 else rnd(n)
         pairs = []
@@ -728,7 +802,7 @@ def polish(sets, seq, eng):
                     durs[i][flip] = m[0][flip]["alts"][eng[flip]][1]
             if turn == 0:
                 v, r2 = run(new, a, r)
-                if v <= cur - PL["TEMP"] * (1 - it / PL["STEPS"]) * math.log((rnd(1000) + 1) / 1000.0):
+                if v <= cur - temp * (1 - it / steps) * math.log((rnd(1000) + 1) / 1000.0):
                     seq, cur, r = new, v, r2
                     if v < best[0]:
                         best = (v, seq, list(eng))
@@ -742,7 +816,8 @@ PLAN = []
 def schedule(ops, sets=None):
     if not PLAN:
         span, at, eng = plan(ops)
-        PLAN.append(polish(sets, sorted(range(len(ops)), key=lambda k: (at[k], k)), eng))
+        span, seq, eng = polish(sets[:1], sorted(range(len(ops)), key=lambda k: (at[k], k)), eng, PL["STEPS"], PL["TEMP"])
+        PLAN.append(polish(sets[1:], seq, eng, PL["MORE"], PL["COOL"]))
     span, seq, eng = PLAN[0]
     order, last = dict((e, []) for e in "VSPGY"), {}
     for i, k in enumerate(seq):
@@ -766,7 +841,7 @@ def rank_program(g, core, T, topo):
     sets = []
     for m in ([] if PLAN else SETS):
         PL.update(m)
-        sets.append((build(g, T, (rid, pid, mask))[0], PL["LAT"], PL["W"]))
+        sets.append((build(g, T, (rid, pid, mask))[0], PL["LAT"], PL["W"], PL["LAT"] - PL["OWN"]))
     PL.update(SETS[0])
     ops, Q, nd = build(g, T, (rid, pid, mask))
     order, eng, seq = schedule(ops, sets)

import math
from concourse.mybir import AluOpType, AxisListType, ActivationFunctionType

A_ = AluOpType
F_ = ActivationFunctionType
WN = 4368
SPARE = 4112.0
MAGIC = 12582912.0
RO = 4

CFG = {
    "gN": ["SVSVSVSV"] + ["S" * 8] * 3, "gR": ["S" * 8] * 4, "gH": ["S" * 8] * 3 + ["SVSSVSSV"],
    "hN": [(0, 128, 256)] * 4, "hR": [(0, 128, 256)] * 4, "hH": [(0, 128, 192, 256)] * 4,
    "cN": [(0, 0)] * 4, "cR": [(0, 0)] * 4, "cH": [(0, 0, 0)] * 4,
    "lag": [(0, 0), (4, 0), (4, 0)], "pool": 2, "early": 1, "onS": "ngpy", "two": 0, "ahead": 1, "hop": ["vvv"] * 4,
    "small": "VS", "evac": "VS",
}

S = {}


def _sb(names, shape, dty):
    for n in names.split():
        S[n] = ("sbuf", shape, dty)


_sb("X0 X1", [128, WN], "bfloat16")
_sb("TR", [128, WN], "float32")
_sb("NB", [128, 4096], "int32")
_sb("GN MN GR MR GH MH MC EB EC", [128, 4096], "bfloat16")
_sb("TD", [128, 2048], "bfloat16")
_sb("AW V0 V1 PM SEL SEP SC RS MK MV PR PQ Pf COL COLG KC DUMR", [128, 256], "float32")
_sb("Ai Si Ui Hi VJi", [128, 256], "int32")
_sb("NBu Au Hu", [128, 256], "uint16")
_sb("A0 A1 NBc RW RP RU0 RU1 RB ZH Bc Bo VJ PS", [128, 256], "float16")
_sb("Y0 Y1 NE XN XW0 XW1 SR ONE XP FD HS M1 MB JR C2K KR SL", [128, 256], "bfloat16")
_sb("ZO0 ZO1 ZO2 ZO3 ZO4 ZI1 ZI2 ZI3 ZI4", [128, 272], "bfloat16")
_sb("E1 E2 nE Es EW E4 S4 G4", [128, 144], "bfloat16")
_sb("CQ", [128, 144], "float32")
_sb("MQ", [128, 64], "float32")
_sb("I nI I4 nI4 I2 I32 KI nKI BO BO8 WH WL TH TP RG K8 IF nIF", [128, 128], "bfloat16")
_sb("fI", [128, 128], "float16")
_sb("T16", [128, 32], "float16")
_sb("O16", [128, 128], "float32")
_sb("KK SH", [128, 512], "bfloat16")
_sb("CL", [128, 640], "bfloat16")
_sb("MX", [128, 1024], "bfloat16")
_sb("GS", [128, 48], "bfloat16")
_sb("C", [128, 64], "float32")
_sb("Ci", [128, 16], "int32")
_sb("Wf", [128, 128], "float32")
_sb("Wi", [128, 32], "int32")
_sb("Wu", [128, 128], "uint16")
_sb("OUT", [128, 768], "float32")
for _b in range(8):
    S["P%d" % _b] = ("psum", [128, 512], "float32")
SCRATCH = S
NDMA = 18
SEMAPHORES = ["V", "S", "P", "G"] + ["d%d" % k for k in range(NDMA)] + ["arr%d" % k for k in range(1, 5)] + ["sent%d" % k for k in range(4)]

SETS = [dict(CY=.85, PCY=.45, GA=1.4, SC=3.0, LAT=250., OWN=150., OVH=10., MM=3., BW=400., SEND=3000., FIRST=7000., GD=1000., W=1.0),
        dict(CY=.85, PCY=.44, GA=1.22, SC=2.5, LAT=230., OWN=165., OVH=8., MM=2., BW=400., SEND=2500., FIRST=11000., GD=2500., W=0.6),
        dict(CY=1.08, PCY=.55, GA=1.7, SC=4.2, LAT=260., OWN=170., OVH=10., MM=3., BW=300., SEND=3000., FIRST=15000., GD=2500., W=0.33)]
PL = {"SEED": 4, "NOISE": 500.0, "PASSES": 10, "STEPS": 70000, "TEMP": 150.0, "MORE": 36000, "COOL": 60.0, "AGAIN": 9, "MEAN": 0.3,
      "LEAD": {"y": 20000.0, "n": 8000.0, "d": 12000.0, "h1": 20000.0, "a1": 20000.0, "H1": 15000.0, "n2": 0.0, "m1": 15000.0, "r1": 15000.0, "c1": 10000.0}}


def build(g, T, dest):
    CY, PCY, GA, SC, OVH = PL["CY"], PL["PCY"], PL["GA"], PL["SC"], PL["OVH"]
    ops = []
    acc = {}
    ndma = [0]
    tail, mark = {}, {}
    tag = ["0"]
    Q = {"V": g.vector, "S": g.scalar, "P": g.tensor, "G": g, "Y": g.sync}

    def top(name, rows, a=None, b=None, s=None):
        r = range(S[name][1][1])[a:b:s]
        return (T[name][0:rows, a:b:s], name, r[0], r[-1] + 1, len(r), S[name][2] in ("bfloat16", "uint16", "float16"), s or 1)

    def c(name, a=None, b=None, s=None):
        return top(name, 128, a, b, s)

    def sub(x, a, b, s=None, rows=128):
        return top(x[1], rows, x[2] + a, x[2] + b, s)

    def add(alts, rd, wr, **kw):
        k = len(ops)
        raw, oth = set(), set()

        def meets(a, e):
            return e[0] < a[3] and a[2] < e[1] and (a[2] - e[0]) % math.gcd(a[6], e[4]) == 0
        for a in rd:
            raw.update(e[3] for e in acc.setdefault(a[1], []) if e[2] and meets(a, e))
        for a in wr:
            oth.update(e[3] for e in acc.setdefault(a[1], []) if meets(a, e))
        for a in wr:
            acc[a[1]] = [e for e in acc[a[1]] if not (a[2] <= e[0] and e[1] <= a[3] and e[4] % a[6] == 0 and (e[0] - a[2]) % a[6] == 0)]
        for a in set(x[1:] for x in rd):
            acc[a[0]].append((a[1], a[2], False, k, a[5]))
        for a in set(x[1:] for x in wr):
            acc[a[0]].append((a[1], a[2], True, k, a[5]))
        banks = set(a[1] for a in list(rd) + list(wr) if S[a[1]][0] == "psum")
        op = dict(alts=alts, raw=raw, oth=oth - raw, soft=set(), banks=banks, lat=0.0, sem=None, out=wr[0][1] if wr else "", tag=tag[0])
        op.update(kw)
        ops.append(op)
        return k

    def isp(a):
        return S[a[1]][0] == "psum"

    def vc(n):
        return max(64.0, n) * CY + OVH

    def sv(x):
        return x[0] if isinstance(x, tuple) else x

    def cols(*xs):
        return [x for x in xs if isinstance(x, tuple)]

    def ts(out, in0, s1, op0, s2=None, op1=None):
        r = 0.5 if out[5] and in0[5] else 1.0
        if op1 is None:
            f = lambda: g.vector.tensor_scalar(out[0], in0[0], sv(s1), None, op0)
        else:
            f = lambda: g.vector.tensor_scalar(out[0], in0[0], sv(s1), sv(s2), op0, op1)
        return add({"V": ([f], vc(out[4] * r))}, [in0] + cols(s1, s2), [out])

    def tt(out, a, b, op):
        r = 1.0 if isp(a) or isp(b) else 2.0
        return add({"V": ([lambda: g.vector.tensor_tensor(out[0], a[0], b[0], op)], vc(out[4] * r))}, [a, b], [out])

    def cp(out, a, eng="V", bias=None):
        alts = {}
        if "V" in eng:
            f = (lambda: g.vector.tensor_copy(out[0], a[0])) if bias is None else (lambda: g.vector.tensor_scalar(out[0], a[0], bias[0], None, A_.add))
            alts["V"] = ([f], vc(out[4] * (0.5 if out[5] and a[5] else 1.0)))
        if "S" in eng:
            f = (lambda: g.scalar.activation(out[0], a[0], F_.Copy)) if bias is None else (lambda: g.scalar.activation(out[0], a[0], F_.Identity, bias=bias[0]))
            alts["S"] = ([f], vc(out[4]))
        return add(alts, [a] + cols(bias), [out])

    def mul(out, a, v):
        return add({"V": ([lambda: g.vector.tensor_scalar(out[0], a[0], sv(v), None, A_.mult)], vc(out[4] * 0.5)),
                    "S": ([lambda: g.scalar.activation(out[0], a[0], F_.Copy, scale=sv(v))], vc(out[4]))}, [a] + cols(v), [out], pref="SV"[len(ops) % 2])

    def gcp(out, a):
        if not CFG["pool"]:
            return cp(out, a, CFG["evac"])
        return gp(lambda: g.affine_select(out[0], a[0], [[0, out[4]]], A_.is_equal, 0.0, 0, 0), out[4], [a], [out])

    def ms(out, v):
        return add({"V": ([lambda: g.vector.memset(out[0], v)], vc(out[4] * (0.5 if out[5] else 1.0)))}, [], [out])

    def act(out, a, fn, bias=0.0, scale=1.0):
        return add({"S": ([lambda: g.scalar.activation(out[0], a[0], fn, bias=sv(bias), scale=scale)], vc(out[4]))}, [a] + cols(bias), [out])

    def scan(out, d0, d1, op0, op1):
        return add({"V": ([lambda: g.vector.tensor_tensor_scan(out[0], d0[0], d1[0], 0.0, op0, op1)], vc(out[4]))}, [d0, d1], [out])

    def gat(out, win, off, eng=None):
        eng = eng or CFG["small"]
        n = off[4] * 16
        alts = {}
        if "V" in eng:
            alts["V"] = ([lambda: g.vector.tensor_copy(out[0], win[0].indirect(off[0]))], 50 + n * GA * CY)
        if "S" in eng:
            alts["S"] = ([lambda: g.scalar.activation(out[0], win[0].indirect(off[0]), F_.Copy)], 65 + n * GA * CY)
        return add(alts, [win, off], [out])

    def sca(win, off, src):
        return add({"V": ([lambda: g.vector.tensor_copy(win[0].indirect(off[0]), src[0])], 50 + src[4] * SC * CY)}, [off, src], [win])

    def mm(terms, first=True, last=True, each=False, after=()):
        fs, cost, rd, wr = [], 0.0, list(after), []
        for k, (o, l, r) in enumerate(terms):
            st = each or (first and k == 0)
            sp = each or (last and k == len(terms) - 1)
            fs.append(lambda o=o, l=l, r=r, st=st, sp=sp: g.tensor.matmul(o[0], l[0], r[0], st, sp))
            cost += max(min(64, l[4]), r[4]) * PCY * (1 if r[5] else 4) + PL["MM"]
            rd += [l, r]
            wr.append(o)
        bank = terms[0][0][1]
        k = add({"P": (fs, cost)}, rd, wr, banks=set(o[1] for o in wr))
        st = tail.setdefault(bank, {"end": [], "since": [], "outs": set()})
        ops[k]["soft"].update(st["end"])
        if first and last:
            st["since"].append(k)
        else:
            ops[k]["soft"].update(st["since"])
            st["end"], st["since"] = [k], []
            st["outs"] = set(o[1:] for o in wr) | (set() if first else st["outs"])
            if last:
                for a in st["outs"]:
                    acc[bank].append((a[1], a[2], True, k, a[5]))
        return k

    def gp(f, n, rd, wr):
        return add({"G": ([f], 170 + 2 * n * CY)}, rd, wr)

    busy = [2000.0]

    def dma(q, out, in_, rd, wr, nbytes, load=False, **kw):
        s = "d%d" % ndma[0]
        ndma[0] += 1
        lat = 2000 + nbytes / PL["BW"]
        if load:
            busy[0] += nbytes / PL["BW"]
            lat = busy[0]
        return add({q: ([lambda: Q[q].dma_start(out, in_, **kw)], 60.0 if q != "G" else PL["GD"])}, rd, wr, sem=s, lat=lat)

    def wf(k):
        return c("Wf", 16 * k, 16 * k + 16)

    def wi(k):
        return c("Wi", 16 * k, 16 * k + 16)

    def wu(k):
        return c("Wu", 16 * k, 16 * k + 16)

    def col(k):
        return c("C", k, k + 1)

    def ci(k):
        return c("Ci", k, k + 1)

    def E(name, l, rows=128):
        return top(name, rows, 15 - l, 143 - l)

    def const(out, k, n=256):
        return (out, top("CL", 1, 128 * k, 128 * k + 128), top("ONE", 1, 0, n))

    def toW(out, e, src, rows=128):
        return [(out, E(e, i, rows), top(src, rows, i, 256, 16)) for i in range(16)]

    ld = [dma("Y", T.VJi[0:8, :], T.v0[:], [], [c("VJi")], 8192, True),
          dma("Y", T.Hi[0:8, :], T.j0[:], [], [c("Hi")], 8192, True),
          dma("Y", T.Ci[:, 8:9], T.w[:], [], [c("Ci", 8, 12)], 512, True),
          dma("Y", T.ZO0[:, 0:256], T.z0[:], [], [c("ZO0", 0, 256)], 65536, True),
          dma("Y", T.NB[:], T.nb[:], [], [c("NB")], 2 << 20, True),
          dma("Y", T.X0[:, 0:4096], T.x[:], [], [c("X0", 0, 4096)], 1 << 20, True),
          dma("Y", T.Y0[:], T.y0[:], [], [c("Y0")], 65536, True),
          dma("Y", T.Ai[:], T.a0[:], [], [c("Ai")], 131072, True)]
    if CFG["two"]:
        ld.append(dma("Y", T.X1[:, 0:4096], T.x[:], [], [c("X1", 0, 4096)], 1 << 20, True))
    for k in ld[1:]:
        ops[k]["soft"].add(k - 1)
    small = dict(allow_small_or_imprecise_dtypes=True)
    gp(lambda: g.iota(T.Ci[:, 0:1], [[0, 1]], 0, 1), 1, [], [ci(0)])
    gp(lambda: g.iota(T.COL[:], [[1, 256]], 0, 0, **small), 256, [], [c("COL")])
    gp(lambda: g.iota(T.COLG[:], [[1, 16], [0, 16]], 0, 0, **small), 256, [], [c("COLG")])
    gp(lambda: g.iota(T.KC[:], [[0, 16], [1, 16]], 0, 0, **small), 256, [], [c("KC")])
    gp(lambda: g.iota(T.KK[0:1, 0:256], [[0, 16], [1, 16]], 0, 0, **small), 256, [], [c("KK", 0, 256)])
    gp(lambda: g.iota(T.KK[0:1, 256:512], [[0, 16], [-8192, 16]], 131072, 0, **small), 256, [], [c("KK", 256, 512)])
    gp(lambda: g.iota(T.K8[:], [[0, 16], [1, 8]], 0, 0, **small), 128, [], [c("K8")])
    gp(lambda: g.iota(T.TR[:], [[1, WN]], -2048, 0, **small), WN, [], [c("TR")])
    P_, L_, G_, T15, Q4, L0, W8, WH_, WL_, FS, FR, THR, QC, THH, CH, P2K, K0, K1, CP, QB, N30, P3K, QV, CH1 = range(24)
    LT = 24
    BIG = 2097152.0
    ms(c("CQ"), -1.0)
    gp(lambda: g.iota(T.CQ[:, 3:131:4], [[1, 8], [0, 4]], 0, 0, **small), 32, [], [c("CQ")])
    gp(lambda: g.iota(T.SC[:, 0:64], [[0, 16], [1, 4]], 0, 0, **small), 64, [], [c("SC", 0, 64)])
    cp(col(P_), ci(0))
    ts(ci(1), ci(0), 15, A_.bitwise_and)
    ts(ci(2), ci(0), 4, A_.arith_shift_right)
    ts(ci(3), ci(1), 2, A_.arith_shift_right)
    cp(col(L_), ci(1))
    cp(col(G_), ci(2))
    cp(col(Q4), ci(3))
    ts(col(QC), ci(3), -BIG, A_.mult, 3 * BIG, A_.add)
    ts(c("SC", 64, 128), c("SC", 0, 64), col(Q4), A_.is_equal, 9 * BIG, A_.mult)
    ts(c("MQ"), c("SC", 64, 128), -BIG, A_.add)
    ts(col(T15), ci(2), 16.0, A_.mult, 15.0, A_.add)
    ts(col(L0), ci(1), 0.0, A_.is_equal)
    ts(col(FR), ci(1), 15.0, A_.is_equal, 65536.0, A_.mult)
    ts(col(FS), ci(1), 102.0, A_.mult, 102.5, A_.add)
    tt(col(THH), col(FR), col(FS), A_.add)
    ts(col(CH), ci(1), 4096.0, A_.mult, 4096.0, A_.add)
    for k, (m, v) in enumerate(((75.0, -80.0), (74.5, -80.0))):
        ts(col(K0 + k), ci(0), m, A_.mult, v, A_.add)
    c2 = lambda k: top("C", 2, k, k + 1)
    ts(top("KR", 2), top("KC", 2), c2(K0), A_.mult, c2(K1), A_.add)
    ts(col(CP), ci(1), -4096.0, A_.mult, 65536.0, A_.add)
    ts(col(QB), col(QC), -30720.0, A_.add)
    ms(col(N30), -30720.0)
    ms(col(P3K), 3000.0)
    ms(col(P2K), 2048.0)
    ms(c("ONE"), 1.0)
    ms(c("O16"), 16.0)
    ms(c("C2K"), 2048.0)
    ts(col(CH1), ci(1), 8192.0, A_.mult)
    for k, v in enumerate((2048.0, -4128768.0, -120.0, -4096.0, 131072.0)):
        ms(top("CL", 1, 128 * k, 128 * k + 128), v)
    ts(top("G4", 8), top("CQ", 8), top("C", 8, P_, P_ + 1), A_.is_equal)
    ts(top("RG", 8), top("COLG", 8, 0, 128), top("C", 8, P_, P_ + 1), A_.is_equal)
    ts(c("E4"), c("CQ"), col(G_), A_.is_equal)
    ts(c("E1"), c("COL", 0, 144), col(T15), A_.is_equal)
    ts(c("I"), c("COL", 0, 128), col(P_), A_.is_equal)
    ts(c("BO"), c("COLG", 0, 128), col(G_), A_.is_equal)
    ts(c("GS", 40, 48), c("COL", 0, 8), col(G_), A_.is_equal)
    for n, m, v in (("S4", "E4", col(L0)), ("E2", "E1", 2.0), ("nE", "E1", -1.0), ("Es", "E1", col(L0)), ("nI", "I", -1.0), ("I4", "I", 4096.0), ("nI4", "I", -4096.0),
                    ("I32", "I", 32.0), ("KI", "I", 1024.0), ("nKI", "I", -1024.0), ("fI", "I", 2047.0 / 4096.0), ("BO8", "BO", 8192.0),
                    ("IF", "I", 131072.0), ("nIF", "I", -131072.0)):
        mul(c(n), c(m), v)
    for k, v in enumerate((32.0, -16.0, 16.0, 2.0, -1.0)):
        mul(c("GS", 8 * k, 8 * k + 8), c("GS", 40, 48), v)
    for n in ("X0", "X1"):
        ms(c(n, 4096, WN), 0.0)
    ts(c("RS"), c("KC"), 0.0, A_.is_equal, 1000000.0, A_.mult)
    ts(c("PM"), c("KC"), col(L_), A_.is_equal)
    ts(c("MB"), c("PM"), -30720.0, A_.mult, 32768.0, A_.add)
    ts(c("MV"), c("PM"), 262144.0, A_.mult, -8192.0, A_.add)
    ts(col(QV), ci(1), -8192.0, A_.mult, 15 * 8192.0 + 2048.0, A_.add)
    ts(c("SEL"), c("COL"), SPARE, A_.add)
    tt(c("MK"), c("SEL"), c("PM"), A_.mult)
    for n, op in (("TH", A_.is_gt), ("TP", A_.is_lt)):
        ts(c("NE", 0, 128), c("KC", 0, 128), col(L_), op, 4096.0, A_.mult)
        tt(c("NE", 128, 256), c("NE", 0, 128), c("BO"), A_.mult)
        tt(c(n), c("NE", 128, 256), c("nI4"), A_.add)
    ts(c("C", LT, LT + 16), c("COL", 0, 16), col(L_), A_.is_gt)
    for i in range(1, 16):
        mul(c("TD", 128 * i, 128 * i + 128), c("BO8"), col(LT + i))
    ts(ci(4), ci(8), 63, A_.bitwise_and)
    ts(ci(5), ci(8), 255, A_.bitwise_and)
    cp(col(WL_), ci(4))
    cp(col(W8), ci(5))
    tt(col(WH_), ci(8), col(WL_), A_.subtract)
    mul(c("WH"), c("BO"), col(WH_))
    mul(c("WL"), c("BO"), col(WL_))
    mul(c("EW"), c("E4"), col(W8))

    lo = lambda b: c("P%d" % b, 0, 256)
    hi = lambda b: c("P%d" % b, 256, 512)
    X = lambda t: c("X%d" % (t % 2 * CFG["two"]), 0, 4096)
    pu = lambda k: c("P4", 256 + 64 * k, 320 + 64 * k)
    pw = lambda k: c("P7", 256 + 64 * k, 320 + 64 * k)
    V0, V1, OB, JU, PU, OV = range(6)
    ov = lambda t: wu(OV + t % 3)
    T1, T2, T3, J1, J2 = range(5)
    EV = CFG["evac"]

    def send(t):
        src, dst, s = "ZO%d" % t, "ZI%d" % (t + 1), "arr%d" % (t + 1)
        add({"G": ([lambda: g.remote_dma(T[dst][:], T[src][:], T.sem[s], T.sem["sent%d" % t], dest[1], dest[0], dest[2])], 500.0)},
            [c(src)], [c(dst)], sem=s, lat=PL["SEND"] if t else PL["FIRST"], remote=True)

    def dedup(ru, key, eb, off, p, pr):
        for k0, k1 in ((0, 2), (2, 4), (4, 6), (6, 9), (9, 12), (12, 16)):
            fs, wr, cost = [], [], 0.0
            for k in range(k0, k1):
                o = c(eb, 256 * k, 256 * k + 256 - 16 * k)
                fs.append(lambda o=o, k=k: g.vector.tensor_scalar(o[0], T[ru][:, 16 * k:256], col(QB if key else QC)[0], T.SC[:, 64 * key + 4 * k + 3:64 * key + 4 * k + 4], A_.subtract, A_.is_equal))
                wr.append(o)
                cost += vc(o[4] * 0.5)
            add({"V": (fs, cost)}, [c(ru), col(QB if key else QC), c("SC", 64 * key, 64 * key + 64)], wr)
        blk = lambda k: (sub(p, 16 * k + 16, 256), c("BO8"), c(eb, 256 * k + 16, 256 * k + 256 - 16 * k))
        mm([(p, c("I"), c("MB")), (p, c("I"), c(ru))] + [blk(k) for k in range(4)], last=False)
        mm([blk(k) for k in range(4, 9)], first=False, last=False)
        mm([blk(k) for k in range(9, 15)], first=False, last=False)
        mm([(sub(p, i, 256, 16), c("TD", 128 * i, 128 * i + 128), c(eb, i, 4096, 256)) for i in range(1, 16)], first=False)
        scan(c(pr), c("MK"), p, A_.max, A_.min)
        cp(off, c(pr, 15, 256, 16))

    def gather(job, lst, t):
        en = CFG["g" + job][t - 1]
        w = 256 // len(en)
        for h, e in enumerate(en):
            k = gat(c("G" + job, 16 * w * h, 16 * w * (h + 1)), X(t if job == "H" else t - 1), c(lst, w * h, w * (h + 1)))
            ops[k]["pref"] = e
            mark[job, t, h] = k
            if job == "H" and t < RO and h == CFG["lag"][t - 1][1]:
                ops[k]["soft"].update(mark["N", t + 1, x] for x in range(CFG["lag"][t - 1][0]))

    def dist(job, oth, pd, head, t, close=True):
        Gn, Mn, cuts = "G" + job, "M" + job, CFG["h" + job][t - 1]
        pc, ps = "P0" if job == "H" else "P1", "P0" if job == "N" else "P5"
        f0 = 0 if job == "N" else 24
        whole = min(CFG["c" + job][t - 1]) == 8
        if not whole:
            mm([(c(pc, r, 512, 2), c("I"), c(oth, 0, 256)) for r in (0, 1)], each=True)
        first = True
        for u0, u1, nc in zip(cuts, cuts[1:], CFG["c" + job][t - 1]):
            wd = u1 - u0
            lv = lambda n, l, a=u0, b=u1: c(n, 16 * a + l, 16 * b, 16)

            def terms(n, ls, f):
                if job != "H":
                    return [(sub(pd, a + l, a + 128, 16), lv(n, l, a, a + 128), c("GS", f0 + 8 * f, f0 + 8 * f + 8)) for l in ls for a in range(u0, u1, 128)]
                return [(sub(pd, u0, u1), E(("E2", "nE", "E1")[f], l), lv(n, l)) for l in ls if l < 15]
            if nc < 8 and (job != "N" or nc):
                m = made[16.0 if job == "N" else 1.0, nc]
                head = head + ([(sub(pd, u0, u1), m, c(oth, u0, u1))] if job == "H" else [(sub(pd, a, a + 128), c(oth, a, a + 128), m) for a in range(u0, u1, 128)])
            for l in range(nc, 8, 2):
                mm(head + terms(Gn, [x + o for x in range(l, min(l + 2, 8)) for o in (0, 8)], 1), first=first, last=False, after=[c(pc)])
                head, first = [], False
            steps = []
            per = 256 // wd
            for l in range(0, nc, per):
                steps.append((l / nc, "c", [x + o for x in range(l, min(l + per, nc)) for o in (0, 8)]))
            for l in range(nc, 8):
                steps.append(((l - nc + 0.5) / (8 - nc), "a", [l, l + 8]))
            steps.sort()
            for i, (_, path, ls) in enumerate(steps):
                l = ls[0]
                if path == "c":
                    if whole:
                        ps = ("P0", "P1")[i % 2]
                    elif t == 1:
                        ps = "P5" if ps == "P0" else "P0"
                    for q, x in enumerate(ls):
                        so = c(ps, wd * q, wd * q + wd)
                        mm([(so, c("nI"), c(oth, u0, u1)), (so, c("I"), lv(Gn, x))])
                    md = c("MC", 16 * u0 + 2 * wd * l, 16 * u0 + 2 * wd * l + wd * len(ls))
                    act(md, c(ps, 0, wd * len(ls)), F_.Abs)
                    if job == "H":
                        tm = [(sub(pd, u0, u1), E("E1", x), sub(md, wd * q, wd * q + wd)) for q, x in enumerate(ls)]
                    else:
                        tm = [(sub(pd, a + x, a + 128, 16), sub(md, wd * q + a - u0, wd * q + a - u0 + 128), c("GS", f0 + 16, f0 + 24)) for q, x in enumerate(ls) for a in range(u0, u1, 128)]
                else:
                    if l == 7 and job == "H":
                        tt(lv(Mn, l), lv(Gn, l), c(pc, 2 * u0, 2 * u1, 2), A_.max)
                    else:
                        tt(c(Mn, 16 * u0 + l, 16 * u1, 8), c(Gn, 16 * u0 + l, 16 * u1, 8), c(pc, 2 * u0, 2 * u1), A_.max)
                    tm = terms(Mn, ls, 0)
                mm(head + tm, first=first, last=close and u1 == 256 and i == len(steps) - 1)
                head, first = [], False

    made = {}
    for f, nc in sorted(set((16.0 if job == "N" else 1.0, nc) for job in "NRH" for x in CFG["c" + job] for nc in x if nc < 8 and (job != "N" or nc))):
        made[f, nc] = c("MX", 128 * len(made), 128 * len(made) + 128)
        ts(c("Pf", 0, 128), c("K8"), float(nc), A_.is_ge, -f, A_.mult)
        tt(made[f, nc], c("Pf", 0, 128), c("BO"), A_.mult)

    def turn(p, src, ident):
        return [(sub(p, 128 * h, 128 * h + 128), c(src, 128 * h, 128 * h + 128), c(ident)) for h in (0, 1)]

    def pick(p, e, src, k, rows=128):
        mm([(p, top(e, rows, 3 - i, 131 - i), top(src, rows, i, 256, 4)) for i in range(4)])
        scan(c("SC", 64 * k, 64 * k + 64), c("MQ"), p, A_.add, A_.min)
        return c("SC", 64 * k + 3, 64 * k + 64, 4)

    def rows(b, rw, o):
        mm([(top("P%d" % b, 8, 128 * h, 128 * h + 128), c("T16", o + 8 * h, o + 8 * h + 8), c("I")) for h in (0, 1)], each=True)
        cp(top(rw, 8), top("P%d" % b, 8, 0, 256), EV)

    def lists(vu, b):
        ts(vu, pick(pu(0), "G4", "RW", 0, 8), col(QC), A_.add, 2048.0, A_.add)
        mm([(hi(2), top("RG", 8), top("RW", 8))])
        cp(c("RU%d" % b), hi(2), EV)

    ts(top("RW", 8), top("VJi", 8), -2048.0, A_.add)
    lists(wu(V0), 0)
    cp(top("JR", 8), top("Hi", 8))
    cp(c("ZO0", 256, 272), pick(pw(0), "G4", "JR", 2, 8), "V", col(QC))
    send(0)
    dedup("RU0", 0, "EB", ov(0), lo(4), "PR")

    def users(t):
        a, b = (t - 1) % 2, t % 2
        y, yn, Ao, An, ru = "Y%d" % a, "Y%d" % b, "A%d" % a, "A%d" % b, "RU%d" % b
        tag[0] = "g%d" % t
        gather("R", "Au", t)
        tag[0] = "n%d" % t
        gat(c("NBu"), c("NB"), wu(V0 + a), "V")
        gather("N", "NBu", t)
        ts(c("NBc"), c("NBu"), -2048.0, A_.add)
        dist("N", y, lo(2), [(c("P2"), top("ONE", 1, 0, 128), top("KK", 1))] + turn(hi(2), "NBc", "I"), t)
        scan(c("PM"), c("RS"), lo(2), A_.add, A_.min)
        tt(c("NE"), lo(2), c("PM"), A_.not_equal)
        scan(c("SEL"), c("NE"), hi(2), A_.mult, A_.max)
        ts(wf(T1), c("SEL", 15, 256, 16), MAGIC * 8192, A_.add, -MAGIC * 8192, A_.add)
        tt(c("T16", 0, 16), c("SEL", 15, 256, 16), wf(T1), A_.subtract)
        rows(2, "RW", 0)
        lists(wu(V0 + b), b)
        gcp(c("V%d" % b), c(ru))
        gat(c("XN"), X(t - 1), wu(V0 + b))
        tag[0] = "d%d" % t
        dedup(ru, 0, "EB", ov(t), lo(4), "PR")
        mm([(lo(2), c("fI"), c("XN")), (lo(2), c("fI"), c(y))])
        ts(c("XW%d" % b), lo(2), MAGIC, A_.add, -MAGIC, A_.add)
        if t == 1 and not CFG["two"]:
            sca(c("X0"), ov(t), c("XW%d" % b))
        for s in range(max(1, t - 1), t + 1) if CFG["two"] else ():
            sca(c("X%d" % b), ov(s), c("XW%d" % (s % 2)))
        tag[0] = "y%d" % t
        mm([(hi(2), c("I"), c(y)), (hi(2), c("nI"), c("XN"))])
        act(c(yn), hi(2), F_.Abs)
        tag[0] = "m%d" % t
        dist("R", "XN", lo(3), [(lo(3), top("ONE", 2, 0, 128), top("KR", 2))], t)
        mm([const(lo(5), 3), const(hi(5), 3), (lo(5), c("I"), c(Ao)), (hi(5), top("RG", 8), top("RW", 8))], last=False)

    def renew(t):
        a, b = (t - 1) % 2, t % 2
        Ao, An, ru = "A%d" % a, "A%d" % b, "RU%d" % b
        tag[0] = "d%d" % t
        if t > 1 and not CFG["two"]:
            sca(c("X0"), ov(t), c("XW%d" % b))
        tag[0] = "r%d" % t
        act(c("SR"), lo(3), F_.Sign, bias=0.0 if t == 1 else col(THR), scale=-1.0)
        mm(turn(hi(5), "SR", "nI4") + turn(lo(5), "SR", "I4"), first=False)
        cp(c("Pf"), hi(5), EV)
        tt(c("AW"), c("Pf"), lo(5), A_.max)
        if t < RO:
            (gcp if CFG["pool"] > 1 else lambda o, a: cp(o, a, EV))(c(An), c("AW"))
            ts(c("Au"), c(An), 2048.0, A_.add)
        tag[0] = "p%d" % t
        if t > 1:
            mm([(hi(3), c("I"), c(Ao))], last=False)
            act(c("SL"), hi(5), F_.Sign, bias=col(P3K))
            mm([(hi(3), c("TP"), c("SL"))], first=False)
            ts(c("RP"), hi(3), col(CP), A_.add, 2048.0, A_.min)
            mm([(hi(5), c("BO"), c("RP"))])
            cp(c("RB"), hi(5), EV, col(N30))
            pick(c("P3", 256, 320), "E4", "RP", 1)
            dedup("RB", 1, "EC", wu(OB), lo(5), "PQ")
            sca(c("TR"), wu(OB), c("RB"))
        sca(c("TR"), ov(t - 1), c(ru))

    def hashed(src, pb, pq):
        mm([const(pb, 0)], last=False)
        mm([(pb, c("I"), c(src))], first=False)
        mm([const(pq, 1), (pq, c("I32"), c(src))])
        tt(c("DUMR"), c("Ui"), pb, A_.mult)
        tt(c("Si"), c("DUMR"), pq, A_.add)
        ts(c("Hi"), c("Si"), 5, A_.arith_shift_right, 4095, A_.bitwise_and)

    def hashes(t, bc):
        zi = "ZI%d" % t
        z, j = c(zi, 0, 256), c(zi, 256, 272)
        tag[0] = "h%d" % t
        cp(wu(JU), j)
        mm([(hi(6), c("WH"), z), (hi(6), c("WL"), z)])
        cp(c("Si"), hi(6))
        ts(c("Ui"), c("Si"), 4095, A_.bitwise_and)
        gat(c(bc), c("AW"), wu(JU))
        hashed(bc, lo(7), lo(6))
        cp(c("Hu"), c("Hi"))
        tag[0] = "j%d" % t
        cp(wi(0), pick(pw(0), "EW", zi, 2))
        ts(wi(1), wi(0), 255, A_.bitwise_and)
        tt(wf(J1), wi(1), j, A_.subtract)

    def probe(t, close):
        tag[0] = "H%d" % t
        gather("H", "Hu", t)
        dist("H", "ZI%d" % t, lo(6), [], t, close)

    def ahead():
        z = c("ZI1", 0, 256)
        tag[0] = "a1"
        gat(c("VJ"), c("V1"), wu(JU))
        hashed("VJ", lo(7), hi(7))
        cp(c("PQ"), c("Hi"))
        scan(c("DUMR"), c("MV"), c("PQ"), A_.add, A_.min)
        ts(wu(PU), c("DUMR", 15, 256, 16), col(QV), A_.add, -2048.0, A_.add)
        gat(c("XP"), X(1), wu(PU))
        mm([(lo(7), c("I"), z), (lo(7), c("nI"), c("XP"))])
        act(c("M1"), lo(7), F_.Abs)
        probe(1, False)
        mm([(hi(6), c("BO"), c("M1"))], first=False, last=False)

    def seekers(t):
        b = t % 2
        zi, zo = "ZI%d" % t, "ZO%d" % t
        z, j = c(zi, 0, 256), c(zi, 256, 272)
        if t > 1 or not CFG["ahead"]:
            hashes(t, "Bc")
            gat(c("VJ"), c("V%d" % b), wu(JU))
            mm([(hi(6), c("I"), c("VJ"))])
            probe(t, True)
            tag[0] = "c%d" % t
            mm([(lo(7), c("I"), c("Bc"))], last=False)
            act(c("SH", 0, 256), lo(6), F_.Sign, bias=col(THH), scale=-1.0)
            mm([(lo(7), c("TH"), c("SH", 0, 256))], first=False)
            ts(c("ZH"), lo(7), col(CH), A_.add, 2048.0, A_.min)
        else:
            tag[0] = "c%d" % t
            gat(c("Bc"), c("AW"), wu(JU))
            tt(c("FD"), c("Bc"), c("Bo"), A_.is_equal)
            mm([(lo(6), c("nIF"), c("FD")), (hi(6), c("IF"), c("FD")), const(lo(6), 4)], first=False)
            mm([(lo(7), c("I"), c("Bc"))], last=False)
            act(c("SH"), c("P6"), F_.Sign, bias=col(THH), scale=-1.0)
            mm([(lo(7), c("TH"), c("SH", 0, 256)), (lo(7), c("TH"), c("SH", 256, 512))], first=False)
            ts(c("ZH"), lo(7), col(CH1), A_.add, 2048.0, A_.min)
            mm([(hi(6), c("I"), c("VJ"))])
        ts(wu(PU), pick(pw(1), "E4", "ZH", 3), col(QC), A_.add, -28672.0, A_.add)
        for k in range(3):
            gat(c("PS"), c("TR", 0, 4096), wu(PU))
            if CFG["hop"][t - 1][k] == "p":
                ts(wu(PU), pick(pw(1), "S4", "PS", 3), col(QC), A_.add, 2048.0, A_.add)
            else:
                scan(c("DUMR"), c("MV"), c("PS"), A_.add, A_.min)
                ts(wu(PU), c("DUMR", 15, 256, 16), col(QV), A_.add)
        gat(c("XP"), X(t), wu(PU))
        tt(c("FD"), c("PS"), hi(6), A_.is_equal)
        mm([(lo(6), c("I"), z), (hi(6), c("nI"), z), (lo(6), c("nKI"), c("FD")), (hi(6), c("nKI"), c("FD"))], last=False)
        fw = c("P0", 0, 16)
        mm(toW(fw, "Es", "FD"))
        mm([(lo(7), c("fI"), z), (lo(7), c("KI"), c("FD"))], last=False)
        mm([(lo(7), c("fI"), c("XP"))], first=False)
        mm([(lo(6), c("nI"), c("XP")), (hi(6), c("I"), c("XP"))], first=False)
        if t < RO:
            add({"V": ([lambda: g.vector.tensor_reduce(T.C[:, FS:FS + 1], fw[0], AxisListType.X, A_.add)], vc(16))}, [fw], [col(FS)])
            pf = c("P0", 16, 17)
            mm([const(pf, 2, 1), (pf, c("O16"), col(FS))])
            ts(col(FR), pf, MAGIC * 256, A_.add, -MAGIC * 256, A_.add)
            ts(col(THR), pf, col(FR), A_.subtract, 120.0, A_.add)
        tt(wf(J2), wf(J1), fw, A_.mult)
        tt(c(zo, 256, 272), wf(J2), j, A_.add)
        ts(c("HS"), lo(7), MAGIC - 1024.0, A_.add, -MAGIC, A_.add)
        tt(c("M1"), c("HS"), lo(6), A_.max)
        tt(c(zo, 0, 256), c("M1"), hi(6), A_.max)
        if t < RO:
            send(t)

    tag[0] = "g1"
    ts(c("A0"), c("Ai"), -2048.0, A_.add)
    ts(c("Au"), c("A0"), 2048.0, A_.add)
    if CFG["ahead"]:
        gcp(c("AW"), c("A0"))
        hashes(1, "Bo")
    users(1)
    if CFG["ahead"]:
        ahead()
    renew(1)
    for t in range(1, RO + 1):
        if t < RO:
            users(t + 1)
        seekers(t)
        if t < RO:
            renew(t + 1)
        tag[0] = ""
        if t == RO - 1:
            cp(c("OUT", 512, 768), c("AW"), "VS", col(P2K))
            dma("Y", T.ya[:], T.OUT[:, 512:768], [c("OUT", 512, 768)], [], 131072)
            dma("Y", T.yy[:], T.Y0[:], [c("Y0")], [], 65536)
            cp(top("OUT", 8, 0, 256), top("RW", 8), "VS", top("C", 8, P2K, P2K + 1))
            dma("Y", T.yv[:], T.OUT[0:8, 0:256], [c("OUT", 0, 256)], [], 8192)
            dma("G", T.yt[:], T.C2K[:], [c("C2K")], [c("JR")], 131072)
            dma("G", T.yt[:], T.TR[0:128:16, 0:4096], [c("TR"), c("JR")], [], 262144, accum_op=A_.add, max_dma_last_dim=8192)
    dma("Y", T.yz[:], T.ZO4[:, 0:256], [c("ZO4", 0, 256)], [], 65536)
    mm([(top("P3", 8, 256 + i, 512, 16), c("I", i, 128, 16), c("ZO4", 256, 272)) for i in range(16)], each=True)
    cp(top("OUT", 8, 256, 512), top("P3", 8, 256, 512), "VS")
    dma("Y", T.yj[:], T.OUT[0:8, 256:512], [c("OUT", 256, 512)], [], 8192)
    for o in ops:
        if len(o["alts"]) == 2 and o["tag"][:1] in CFG["onS"] and o["tag"][1:] != "1":
            o["alts"].pop("V")
    for h in range(2):
        ops[mark["N", 1, h]]["soft"].update(k for k, o in enumerate(ops) if o["tag"] == "0" and "V" in o["alts"] and CFG["early"])
    return ops, Q, ndma[0]


def plan(ops):
    n, LAT = len(ops), PL["LAT"]
    pred = [sorted(o["raw"] | o["oth"] | o["soft"]) for o in ops]
    succ = [[] for _ in range(n)]
    for k in range(n):
        for d in pred[k]:
            succ[d].append(k)

    def place(urge, back, eng):
        eng, at = list(eng), [0.0] * n
        dur = lambda k: ops[k]["alts"][eng[k]][1]
        before, after = (succ, pred) if back else (pred, succ)
        left = [len(x) for x in before]
        ready = [k for k in range(n) if not left[k]]
        use = {}
        while ready:
            k = max(ready, key=lambda k: urge[k])
            ready.remove(k)
            o, best = ops[k], None
            for e in [o.get("pref") or ("S" if "S" in o["alts"] else list(o["alts"])[0])]:
                d, t = o["alts"][e][1], 0.0
                for x in before[k]:
                    p, s = (k, x) if back else (x, k)
                    free = eng[x] == e == "P"
                    t = max(t, at[x] + dur(x) + (0.0 if free or p in ops[s]["soft"] else PL["OWN"] if eng[x] == e and e in "VS" else LAT + ops[p]["lat"]))
                if back and not before[k]:
                    t = o["lat"]
                spans = sorted([u[:2] for u in use.get(e, [])] + [(u[0] - LAT, u[1] + LAT) for b in o["banks"] for u in use.get(b, []) if u[2] != e])
                for a, b in spans:
                    if b > t:
                        if a >= t + d:
                            break
                        t = b
                if best is None or t + d < best[0]:
                    best = (t + d, t, e)
            at[k], eng[k] = best[1], best[2]
            for r in [eng[k]] + list(o["banks"]):
                use.setdefault(r, []).append((at[k], best[0], eng[k]))
            for x in after[k]:
                left[x] -= 1
                if not left[x]:
                    ready.append(x)
        return at, eng, [at[k] + dur(k) + (0.0 if back else ops[k]["lat"]) for k in range(n)]

    urge, x = [0.0] * n, PL["SEED"]
    for k in range(n - 1, -1, -1):
        urge[k] = min(a[1] for a in ops[k]["alts"].values()) + ops[k]["lat"] + max([urge[s] + LAT for s in succ[k]] + [0.0])
    for k in range(n):
        urge[k] += PL["LEAD"].get(ops[k]["tag"], PL["LEAD"].get(ops[k]["tag"][:1], 0.0))
    best = None
    for _ in range(PL["PASSES"]):
        for k in range(n):
            x = (x * 1103515245 + 12345) % 2147483648
            urge[k] += PL["NOISE"] * x / 2147483648.0
        at, eng, end = place(urge, False, [None] * n)
        if best is None or max(end) < best[0]:
            best = (max(end), at, eng)
        urge = place(end, True, eng)[2]
    return best


def polish(sets, seq, eng, steps, temp):
    ops = sets[0][0]
    n, eng = len(ops), list(eng)
    pred = [o["raw"] | o["oth"] | o["soft"] for o in ops]
    hard = [[d for d in o["raw"] | o["oth"] if not (eng[k] == "P" and eng[d] == "P")] for k, o in enumerate(ops)]
    succ = [set() for _ in range(n)]
    for k in range(n):
        for d in pred[k]:
            succ[d].add(k)
    banks = [sorted(o["banks"]) for o in ops]
    durs = [[o["alts"][eng[k]][1] for k, o in enumerate(m[0])] for m in sets]
    lats = [[o["lat"] for o in m[0]] for m in sets]
    x = [PL["SEED" if len(sets) == 1 else "AGAIN"]]

    def rnd(m):
        x[0] = (x[0] * 1103515245 + 12345) % 2147483648
        return (x[0] >> 8) % m

    gaps = [[x + m[1] for x in lat] + [0.0] for lat, m in zip(lats, sets)]

    def run(seq, a, old):
        last0 = dict((r, n) for r in list("VSPGY") + ["P%d" % b for b in range(8)])
        for k in seq[max(0, a - 400):a]:
            last0[eng[k]] = k
            for b in banks[k]:
                last0[b] = k
        res, tot = [], 0.0
        for i, m in enumerate(sets):
            dur, gap, own, last = durs[i], gaps[i], m[3], dict(last0)
            end, why = (old[i][0][:], old[i][1][:]) if old else ([0.0] * (n + 1), [n] * n)
            for k in seq[a:]:
                e = eng[k]
                w = last[e]
                last[e] = k
                t = end[w] - gap[w]
                for d in hard[k]:
                    x = end[d]
                    if x > t:
                        if eng[d] == e and e in "VS":
                            x -= own
                            if x <= t:
                                continue
                        t, w = x, d
                for b in banks[k]:
                    d = last[b]
                    last[b] = k
                    if end[d] > t and eng[d] != e:
                        t, w = end[d], d
                end[k] = t + dur[k] + gap[k]
                why[k] = w
            res.append((end, why))
            tot += (max(end) + PL["MEAN"] * sum(end) / n) * m[2]
        return tot, res

    cur, r = run(seq, 0, None)
    best = (cur, seq, list(eng))
    for it in range(steps):
        end, why = r[rnd(len(r))]
        k = end.index(max(end)) if rnd(5) < 3 else rnd(n)
        pairs = []
        while why[k] < n:
            if why[k] not in pred[k]:
                pairs.append((why[k], k))
            k = why[k]
        if not pairs:
            continue
        j, k = pairs[rnd(len(pairs))]
        a, b, how, more, flip = seq.index(j), seq.index(k), rnd(20), (0, 0, 0, 3, 10, 30)[rnd(6)], None
        if how < 3:
            flip = (j, k)[rnd(2)]
            if len(ops[flip]["alts"]) < 2:
                continue
            new = seq
        else:
            up = how < 12
            a, b = (max(0, a - more), b) if up else (a, min(n - 1, b + more))
            mv = set([k if up else j])
            for y in (reversed(seq[a:b]) if up else seq[a + 1:b + 1]):
                if not mv.isdisjoint(succ[y] if up else pred[y]):
                    mv.add(y)
            if j in mv and k in mv:
                continue
            mid = seq[a:b + 1]
            new = seq[:a] + [y for y in mid if (y in mv) == up] + [y for y in mid if (y in mv) != up] + seq[b + 1:]
        for turn in (0, 1):
            if flip is not None:
                eng[flip] = "S" if eng[flip] == "V" else "V"
                for i, m in enumerate(sets):
                    durs[i][flip] = m[0][flip]["alts"][eng[flip]][1]
            if turn == 0:
                v, r2 = run(new, a, r)
                if v <= cur - temp * (1 - it / steps) * math.log((rnd(1000) + 1) / 1000.0):
                    seq, cur, r = new, v, r2
                    if v < best[0]:
                        best = (v, seq, list(eng))
                    break
    return best


PLAN = []


def schedule(ops, sets=None):
    if not PLAN:
        span, at, eng = plan(ops)
        span, seq, eng = polish(sets[:1], sorted(range(len(ops)), key=lambda k: (at[k], k)), eng, PL["STEPS"], PL["TEMP"])
        PLAN.append(polish(sets[1:], seq, eng, PL["MORE"], PL["COOL"]))
    span, seq, eng = PLAN[0]
    order, last = dict((e, []) for e in "VSPGY"), {}
    for i, k in enumerate(seq):
        o = ops[k]
        o["t"] = i
        o["dyn"] = set(last[b] for b in o["banks"] if b in last and eng[last[b]] != eng[k])
        for b in o["banks"]:
            last[b] = k
        order[eng[k]].append(k)
    return order, eng, seq


def rank_program(g, core, T, topo):
    rank = T.rank_of(core)
    if rank is None:
        return
    nxt = T.cores[(rank + 1) % len(T.cores)]
    rid, pid, _ = topo.addr(nxt)
    mask = topo.mask(core, nxt)
    neng = len(topo.engines(core, nxt))
    sets = []
    for m in ([] if PLAN else SETS):
        PL.update(m)
        sets.append((build(g, T, (rid, pid, mask))[0], PL["LAT"], PL["W"], PL["LAT"] - PL["OWN"]))
    PL.update(SETS[0])
    ops, Q, nd = build(g, T, (rid, pid, mask))
    order, eng, seq = schedule(ops, sets)
    tick = {}
    for e, L in order.items():
        m = 0
        for k in L:
            o = ops[k]
            if o["sem"]:
                tick[k] = (o["sem"], neng if o.get("remote") else 16)
            else:
                m += 1
                tick[k] = (e, m)
    seen_all, clock, waits = {}, {}, {}
    seen = dict((e, {}) for e in order)
    for k in seq:
        o, e = ops[k], eng[k]
        deps = [d for d in o["raw"] | o["oth"] | o["dyn"] if not (e == "P" and eng[d] == "P")]
        need = {}
        for d in sorted(deps, key=lambda d: -ops[d]["t"]):
            s, v = tick[d]
            if seen[e].get(s, 0) < v:
                need[s] = max(need.get(s, 0), v)
                for s2, v2 in clock[d].items():
                    seen[e][s2] = max(seen[e].get(s2, 0), v2)
        waits[k] = need
        clock[k] = {} if o.get("remote") else dict(seen[e])
        clock[k][tick[k][0]] = tick[k][1]
    for e, L in order.items():
        for k in L:
            o = ops[k]
            for s, v in sorted(waits[k].items()):
                Q[e].wait_ge(T.sem[s], v)
                seen_all[s] = max(seen_all.get(s, 0), v)
            for f in o["alts"][e][0]:
                ins = f()
            if not o.get("remote"):
                ins.then_inc(T.sem[o["sem"] or e], 16 if o["sem"] else 1)
    top = {}
    for s, v in tick.values():
        top[s] = max(top.get(s, 0), v)
    for s, v in sorted(top.items()):
        if seen_all.get(s, 0) < v:
            g.sync.wait_ge(T.sem[s], v)
    for t in range(RO):
        g.sync.wait_ge(T.sem["sent%d" % t], neng)
